import numpy as np
import ml_dtypes


def mxq(x, axis, fmt="e4m3"):
    dtype, down = {"e4m3": (ml_dtypes.float8_e4m3fn, 7), "e5m2": (ml_dtypes.float8_e5m2, 14)}[fmt]
    v = np.moveaxis(np.asarray(x, np.float32).astype(ml_dtypes.bfloat16).astype(np.float64), axis, -1)
    blocks = v.reshape(v.shape[:-1] + (-1, 32))
    amax = np.abs(blocks).max(-1, keepdims=True)
    byte = np.maximum(np.where(amax > 0, np.frexp(amax)[1] - 1 + 127, 0) - down, 1)
    scale = np.exp2(byte - 127.0)
    codes = (blocks / scale).astype(np.float32).astype(dtype).astype(np.float64)
    return np.moveaxis((codes * scale).reshape(v.shape), -1, axis)


WIDE = False


def mx_kscale(k):
    if not WIDE:
        return np.ones(k)
    levels = np.array([10, -10, 5, -5, 0])
    if k % 512:
        return np.exp2(np.random.permutation(np.resize(levels, k // 32))).repeat(32)
    a = np.empty((k // 512, 16))
    for p in range(k // 512):
        a[p, :8] = np.random.permutation(np.resize(levels, 8))
        for g in range(8):
            far = levels[np.abs(levels - a[p, g]) >= 10]
            a[p, g + 8] = far[np.random.randint(len(far))]
    return np.exp2(a.ravel()).repeat(32)


def f64(x):
    return np.asarray(x).astype(np.float64)


def striped(idx):
    return np.tile(np.asarray(idx).reshape(-1, 16).T, (8, 1)).astype(np.uint16)


def unstriped(offs):
    return offs[:16].T.reshape(-1).astype(np.int64)


E2M1 = np.array([0.0, 0.5, 1.0, 1.5, 2.0, 3.0, 4.0, 6.0, -0.0, -0.5, -1.0, -1.5, -2.0, -3.0, -4.0, -6.0])


def pack_weight(w, fmt):
    k, n = w.shape
    w = f64(np.asarray(w, np.float32).astype(ml_dtypes.bfloat16)).reshape(k // 32, 32, n)
    amax = np.abs(w).max(1)
    if fmt == "e4m3":
        byte = np.frexp(amax)[1] - 1 + 127 - 7
    else:
        mant, ex = np.frexp(amax / 6.0)
        byte = np.where(mant > 0.5, ex, ex - 1) + 127
    byte = np.clip(np.where(amax > 0, byte, 1), 1, 254)
    scaled = (w * np.exp2(127.0 - byte)[:, None, :]).reshape(k, n).astype(np.float32)
    by_word = np.ascontiguousarray(scaled.reshape(k // 512, 128, 4, n).transpose(0, 1, 3, 2))
    if fmt == "e4m3":
        words = by_word.astype(ml_dtypes.float8_e4m3fn).view(np.uint8)
    else:
        c = by_word.astype(ml_dtypes.float4_e2m1fn).view(np.uint8) & 0xF
        words = (c[..., 0::2] | (c[..., 1::2] << 4)).reshape(k // 512, 128, 2 * n)
    return np.ascontiguousarray(words), np.ascontiguousarray(byte.astype(np.uint8).reshape(k // 512, 16, n))


def unpack_weight(words, scales, fmt):
    g, _, n = scales.shape
    words = np.ascontiguousarray(words).reshape(g, 128, n, -1)
    if fmt == "e4m3":
        vals = words.view(ml_dtypes.float8_e4m3fn).astype(np.float64)
    else:
        nib = np.empty((g, 128, n, 4), np.uint8)
        nib[..., 0::2] = words & 0xF
        nib[..., 1::2] = words >> 4
        vals = E2M1[nib]
    vals = vals * np.repeat(np.exp2(scales.astype(np.float64) - 127.0), 8, axis=1)[..., None]
    return vals.transpose(0, 1, 3, 2).reshape(g * 512, n)


B, N, T, D, DV, NQ = 1, 1536, 4096, 512, 256, 128
PAGE = 512


def setup_inputs():
    n = np.random.standard_normal
    pages = np.random.permutation(T // PAGE)[:B * N // PAGE]
    idx = (pages[:, None] * PAGE + np.arange(PAGE)[None, :]).reshape(-1)
    s = mx_kscale(D)[:, None]
    u = np.ones(T)
    u[idx] = mx_kscale(B * N)
    r = np.random.uniform(0.5, 2.0, T)
    qp = [pack_weight(x, "e4m3") for x in n((B, D, NQ)) * s * (1.00 / np.sqrt(D))]
    k = n((D, T)) / s
    v = n((DV, T)) / (u * r)
    kp = pack_weight(k, "e4m3")
    vp = pack_weight(v.T, "e4m3")
    return {
        "q_words": np.stack([x[0] for x in qp]),
        "q_scales": np.stack([x[1] for x in qp]),
        "k_words": kp[0],
        "k_scales": kp[1],
        "v_words": vp[0],
        "v_scales": vp[1],
        "vs": np.tile(u * r, (128, 1)).astype(np.float32),
        "kb": np.tile(n(T), (128, 1)).astype(np.float32),
        "offs": striped(idx),
        "voffs": striped((pages[:, None] * DV + np.arange(DV)[None, :]).reshape(-1)),
    }


def reference(q_words, q_scales, k_words, k_scales, v_words, v_scales, vs, kb, offs, voffs):
    idx = unstriped(offs)
    k = unpack_weight(k_words, k_scales, "e4m3")
    v = unpack_weight(v_words, v_scales, "e4m3")
    v = v.reshape(T // 512, 512, DV)[unstriped(voffs)[::DV] // DV].reshape(B, N, DV)
    pick = lambda x: x[:, idx].reshape(x.shape[0], B, N).transpose(1, 0, 2)
    q = np.stack([unpack_weight(q_words[b], q_scales[b], "e4m3") for b in range(B)])
    score = q.transpose(0, 2, 1) @ pick(k)
    score = score + pick(f64(kb))[:, :1, :]
    p = score / (1.0 + np.exp(-score))
    w = p * pick(f64(vs))[:, :1, :]
    y = mxq(w, 2, "e4m3") @ v
    y = y / 16.0
    return y

@@ -1,0 +1,163 @@
+from contextlib import ExitStack
+
+import concourse.mybir as mybir
+from concourse.masks import make_identity
+
+P = 128
+PACK = 4
+PAGE = P * PACK
+PAGES = 3
+POOL_TOKENS = 4096
+POOL_PAGES = POOL_TOKENS // PAGE
+DV = 256
+NQ = 128
+LIST_ROWS = 16
+LIVE = P - 1
+K_PLANE, V_PLANE, Q_PLANE = 0, 4, 8
+
+FLOPS = 2 * NQ * PAGES * PAGE * (512 + DV)
+
+F32 = mybir.dt.float32
+BF16 = mybir.dt.bfloat16
+I32 = mybir.dt.int32
+U32 = mybir.dt.uint32
+U16 = mybir.dt.uint16
+U8 = mybir.dt.uint8
+FP8X4 = mybir.dt.float8_e4m3fn_x4
+ACT = mybir.ActivationFunctionType
+MULT = mybir.AluOpType.mult
+
+
+def tile_attend_pkv8q_silu_kb_kernel(
+    tc, q_words, q_scales, k_words, k_scales, v_words, v_scales, vs, kb, offs, voffs, out
+):
+    nc = tc.nc
+    with ExitStack() as ctx:
+        sb = ctx.enter_context(tc.tile_pool(name="sb", bufs=1))
+        ps = ctx.enter_context(tc.psum_pool(name="ps", bufs=1))
+
+        def sbuf(name, shape, dtype):
+            return sb.tile(shape, dtype, name=name, align_bytes=64)
+
+        slots = sb.tile([P, PAGES * PAGE // LIST_ROWS], U16, name="slots")
+        vcols = sb.tile([P, PAGES * DV // LIST_ROWS], U16, name="vcols")
+        kw_pool = sbuf("kw_pool", [P, POOL_TOKENS], I32)
+        ks_pool = sbuf("ks_pool", [P, POOL_TOKENS // 4], I32)
+        vw_pool = sbuf("vw_pool", [P, POOL_PAGES * DV], I32)
+        vsc_pool = sbuf("vsc_pool", [P, POOL_PAGES * DV // 4], I32)
+        kb_pool = sbuf("kb_pool", [P, POOL_TOKENS], F32)
+        vs_pool = sbuf("vs_pool", [P, POOL_TOKENS], F32)
+        qw = sbuf("qw", [P, NQ], I32)
+        qs = sbuf("qs", [P, NQ // 4], I32)
+        ident = sbuf("ident", [P, P], F32)
+        warm = sbuf("warm", [P, 1], F32)
+
+        make_identity(nc, ident[:])
+        nc.scalar.activation(warm[:], ident[:, 0:1], ACT.Silu)
+
+        nc.vector.memset(ks_pool[:], 0)
+        nc.vector.memset(qs[:], 0)
+        nc.vector.memset(vsc_pool[:], 0)
+        nc.vector.memset(kb_pool[:LIVE, :], 0.0)
+        nc.vector.memset(vs_pool[:LIVE, :16], 0.0)
+        nc.gpsimd.memset(vs_pool[:LIVE, 8:], 0.0)
+
+        nc.sync.dma_start(slots[:], offs)
+        nc.sync.dma_start(kb_pool[LIVE:, :], kb[0:1, :])
+        for quad in range(4):
+            nc.sync.dma_start(
+                ks_pool[32 * quad + K_PLANE : 32 * quad + K_PLANE + 4, :],
+                k_scales[0, 4 * quad : 4 * quad + 4, :].bitcast(I32),
+            )
+        nc.sync.dma_start(kw_pool[:], k_words[0].rearrange("p n r -> p (n r)").bitcast(I32))
+        nc.sync.dma_start(qw[:], q_words[0, 0].rearrange("p n r -> p (n r)").bitcast(I32))
+        for quad in range(4):
+            nc.sync.dma_start(
+                qs[32 * quad + Q_PLANE : 32 * quad + Q_PLANE + 4, :],
+                q_scales[0, 0, 4 * quad : 4 * quad + 4, :].bitcast(I32),
+            )
+        nc.scalar.dma_start(vs_pool[LIVE:, :], vs[0:1, :])
+        nc.sync.dma_start(vcols[:], voffs)
+        nc.sync.dma_start(
+            vw_pool[:].rearrange("p (u e) -> p u e", u=POOL_PAGES),
+            v_words.rearrange("u p e r -> p u (e r)").bitcast(I32),
+        )
+        for quad in range(4):
+            nc.sync.dma_start(
+                vsc_pool[32 * quad + V_PLANE : 32 * quad + V_PLANE + 4, :].rearrange(
+                    "p (u e) -> p u e", u=POOL_PAGES
+                ),
+                v_scales[:, 4 * quad : 4 * quad + 4, :].rearrange("u f e -> f u e").bitcast(I32),
+            )
+
+        def gather(name, pool_view, entries, page, width, dtype):
+            picked = sbuf("%s%d" % (name, page), [P, width], dtype)
+            cols = width // LIST_ROWS
+            nc.vector.tensor_copy(picked[:], pool_view.indirect(entries[:, page * cols : (page + 1) * cols]))
+            return picked
+
+        def to_columns(name, row_tile, page):
+            bank = ps.tile([P, PACK, P], F32, name="col_bank", tag="col_bank", bufs=2)
+            for t in range(PACK):
+                nc.tensor.transpose(bank[:, t, :], row_tile[:, t::PACK], ident[:])
+            columns = sbuf("%s%d" % (name, page), [P, PACK], F32)
+            nc.scalar.copy(columns[:], bank[:, :, LIVE])
+            return columns
+
+        kb_cols = [to_columns("kb_col", gather("kb_row", kb_pool[:], slots, u, PAGE, F32), u) for u in range(PAGES)]
+        ks = [gather("ks", ks_pool[:].bitcast(U8), slots, u, PAGE, U8) for u in range(PAGES)]
+
+        silu = []
+        for u in range(PAGES):
+            kw = gather("kw", kw_pool[:].bitcast(U32), slots, u, PAGE, U32)
+            score_bank = ps.tile([P, PAGE], F32, name="score_bank", tag="score_bank", bufs=2)
+            nc.tensor.matmul_mx(
+                score_bank[:],
+                lhsT=qw[:].bitcast(FP8X4),
+                lhsT_scale=qs[:].bitcast(U8)[Q_PLANE:, :],
+                rhs=kw[:].bitcast(FP8X4),
+                rhs_scale=ks[u][K_PLANE:, :],
+                start=True,
+                stop=True,
+            )
+            score = sbuf("score%d" % u, [P, PACK, P], F32)
+            nc.scalar.copy(score[:], score_bank[:].rearrange("q (m t) -> q t m", t=PACK))
+            turned = ps.tile([P, PACK, NQ], F32, name="turned", tag="turned", bufs=2)
+            for t in range(PACK):
+                nc.tensor.transpose(turned[:, t, :], score[:, t, :], ident[:])
+            p_tile = sbuf("silu%d" % u, [P, PACK, NQ], F32)
+            for t in range(PACK):
+                nc.scalar.activation(p_tile[:, t, :], turned[:, t, :], ACT.Silu, bias=kb_cols[u][:, t : t + 1])
+            silu.append(p_tile)
+
+        vs_cols = [to_columns("vs_col", gather("vs_row", vs_pool[:], slots, u, PAGE, F32), u) for u in range(PAGES)]
+        vsc = [gather("vsc", vsc_pool[:].bitcast(U8), vcols, u, DV, U8) for u in range(PAGES)]
+
+        acc = ps.tile([NQ, DV], F32, name="acc")
+        for u in range(PAGES):
+            w = sbuf("w%d" % u, [P, NQ, PACK], BF16)
+            nc.vector.tensor_tensor(
+                w[:],
+                silu[u][:].rearrange("p t q -> p q t"),
+                vs_cols[u][:].unsqueeze(1).to_broadcast([P, NQ, PACK]),
+                MULT,
+            )
+            vw = gather("vw", vw_pool[:].bitcast(U32), vcols, u, DV, U32)
+            w_codes = sbuf("w_codes%d" % u, [P, NQ], U32)
+            w_scales = sbuf("w_scales%d" % u, [P, NQ], U8)
+            nc.vector.quantize_mx(
+                out=w_codes[:].bitcast(FP8X4), scales=w_scales[:], in_=w[:].rearrange("p q t -> p (q t)")
+            )
+            nc.tensor.matmul_mx(
+                acc[:],
+                lhsT=w_codes[:].bitcast(FP8X4),
+                lhsT_scale=w_scales[:],
+                rhs=vw[:].bitcast(FP8X4),
+                rhs_scale=vsc[u][V_PLANE:, :],
+                start=(u == 0),
+                stop=(u == PAGES - 1),
+            )
+
+        result = sbuf("result", [NQ, DV], F32)
+        nc.scalar.activation(result[:], acc[:], ACT.Copy, scale=1.0 / 16.0)
+        nc.sync.dma_start(out[0], result[:])

@@ -43,45 +43,47 @@ def tile_attend_pkv8q_silu_kb_kernel(
         vcols = sb.tile([P, PAGES * DV // LIST_ROWS], U16, name="vcols")
         kw_pool = sbuf("kw_pool", [P, POOL_TOKENS], I32)
         ks_pool = sbuf("ks_pool", [P, POOL_TOKENS // 4], I32)
-        vw_pool = sbuf("vw_pool", [P, POOL_PAGES * DV], I32)
         vsc_pool = sbuf("vsc_pool", [P, POOL_PAGES * DV // 4], I32)
-        kb_pool = sbuf("kb_pool", [P, POOL_TOKENS], F32)
+        kb_pool = sb.tile([P, POOL_TOKENS], F32, name="kb_pool", tag="kb_then_vw", align_bytes=64)
         vs_pool = sbuf("vs_pool", [P, POOL_TOKENS], F32)
+        vs_head = sbuf("vs_head", [P, 8], F32)
         qw = sbuf("qw", [P, NQ], I32)
         qs = sbuf("qs", [P, NQ // 4], I32)
         ident = sbuf("ident", [P, P], F32)
+        zero = sbuf("zero", [P, 1], F32)
         warm = sbuf("warm", [P, 1], F32)
 
-        make_identity(nc, ident[:])
-        nc.scalar.activation(warm[:], ident[:, 0:1], ACT.Silu)
-
+        nc.vector.memset(zero[:], 0.0)
+        nc.scalar.activation(warm[:], zero[:], ACT.Silu)
         nc.vector.memset(ks_pool[:], 0)
+        nc.vector.memset(kb_pool[:LIVE, :], 0.0)
         nc.vector.memset(qs[:], 0)
         nc.vector.memset(vsc_pool[:], 0)
-        nc.vector.memset(kb_pool[:LIVE, :], 0.0)
-        nc.vector.memset(vs_pool[:LIVE, :16], 0.0)
-        nc.gpsimd.memset(vs_pool[:LIVE, 8:], 0.0)
+        nc.vector.memset(ident[:], 0.0)
+        make_identity(nc, ident[:], nomemset=True)
 
         nc.sync.dma_start(slots[:], offs)
         nc.sync.dma_start(kb_pool[LIVE:, :], kb[0:1, :])
+        nc.sync.dma_start(vs_head[:], vs[:, :8])
+        nc.sync.dma_start(kw_pool[:], k_words[0].rearrange("p n r -> p (n r)").bitcast(I32))
+        nc.sync.dma_start(qw[:], q_words[0, 0].rearrange("p n r -> p (n r)").bitcast(I32))
+        nc.sync.dma_start(vs_pool[LIVE:, :], vs[0:1, :])
+        nc.sync.dma_start(vcols[:], voffs)
         for quad in range(4):
-            nc.sync.dma_start(
+            nc.scalar.dma_start(
                 ks_pool[32 * quad + K_PLANE : 32 * quad + K_PLANE + 4, :],
                 k_scales[0, 4 * quad : 4 * quad + 4, :].bitcast(I32),
             )
-        nc.sync.dma_start(kw_pool[:], k_words[0].rearrange("p n r -> p (n r)").bitcast(I32))
-        nc.sync.dma_start(qw[:], q_words[0, 0].rearrange("p n r -> p (n r)").bitcast(I32))
+        nc.scalar.activation(
+            vs_pool[:LIVE, :].rearrange("p (a b) -> p a b", b=8),
+            vs_head[:LIVE, :].unsqueeze(1).to_broadcast([LIVE, POOL_TOKENS // 8, 8]),
+            ACT.Copy,
+        )
         for quad in range(4):
             nc.sync.dma_start(
                 qs[32 * quad + Q_PLANE : 32 * quad + Q_PLANE + 4, :],
                 q_scales[0, 0, 4 * quad : 4 * quad + 4, :].bitcast(I32),
             )
-        nc.scalar.dma_start(vs_pool[LIVE:, :], vs[0:1, :])
-        nc.sync.dma_start(vcols[:], voffs)
-        nc.sync.dma_start(
-            vw_pool[:].rearrange("p (u e) -> p u e", u=POOL_PAGES),
-            v_words.rearrange("u p e r -> p u (e r)").bitcast(I32),
-        )
         for quad in range(4):
             nc.sync.dma_start(
                 vsc_pool[32 * quad + V_PLANE : 32 * quad + V_PLANE + 4, :].rearrange(
@@ -90,51 +92,61 @@ def tile_attend_pkv8q_silu_kb_kernel(
                 v_scales[:, 4 * quad : 4 * quad + 4, :].rearrange("u f e -> f u e").bitcast(I32),
             )
 
-        def gather(name, pool_view, entries, page, width, dtype):
-            picked = sbuf("%s%d" % (name, page), [P, width], dtype)
-            cols = width // LIST_ROWS
-            nc.vector.tensor_copy(picked[:], pool_view.indirect(entries[:, page * cols : (page + 1) * cols]))
+        def gather(name, pool_view, entries, first, count, dtype):
+            picked = sbuf(name, [P, count], dtype)
+            columns = entries[:, first // LIST_ROWS : (first + count) // LIST_ROWS]
+            nc.vector.tensor_copy(picked[:], pool_view.indirect(columns))
             return picked
 
-        def to_columns(name, row_tile, page):
-            bank = ps.tile([P, PACK, P], F32, name="col_bank", tag="col_bank", bufs=2)
-            for t in range(PACK):
-                nc.tensor.transpose(bank[:, t, :], row_tile[:, t::PACK], ident[:])
-            columns = sbuf("%s%d" % (name, page), [P, PACK], F32)
-            nc.scalar.copy(columns[:], bank[:, :, LIVE])
+        def to_columns(name, row):
+            columns = sbuf(name, [P, PACK], F32)
+            nc.sync.dma_start(columns[:], row.rearrange("o (m t) -> o m t", t=PACK))
             return columns
 
-        kb_cols = [to_columns("kb_col", gather("kb_row", kb_pool[:], slots, u, PAGE, F32), u) for u in range(PAGES)]
-        ks = [gather("ks", ks_pool[:].bitcast(U8), slots, u, PAGE, U8) for u in range(PAGES)]
-
-        silu = []
+        kb_row = gather("kb_row", kb_pool[:], slots, 0, PAGES * PAGE, F32)
+        kb_cols = [to_columns("kb_cols%d" % u, kb_row[LIVE:, u * PAGE : (u + 1) * PAGE]) for u in range(PAGES)]
+        vw_pool = sb.tile([P, POOL_PAGES * DV], I32, name="vw_pool", tag="kb_then_vw", align_bytes=64)
+        nc.sync.dma_start(
+            vw_pool[:].rearrange("p (u e) -> p u e", u=POOL_PAGES),
+            v_words.rearrange("u p e r -> p u (e r)").bitcast(I32),
+        )
+        ks = gather("ks", ks_pool[:].bitcast(U8), slots, 0, PAGES * PAGE, U8)
+        kw = gather("kw", kw_pool[:].bitcast(U32), slots, 0, PAGES * PAGE, U32)
+        vs_cols = []
         for u in range(PAGES):
-            kw = gather("kw", kw_pool[:].bitcast(U32), slots, u, PAGE, U32)
-            score_bank = ps.tile([P, PAGE], F32, name="score_bank", tag="score_bank", bufs=2)
+            vs_row = gather("vs_row%d" % u, vs_pool[:], slots, u * PAGE, PAGE, F32)
+            vs_cols.append(to_columns("vs_cols%d" % u, vs_row[LIVE:, :]))
+        vsc = gather("vsc", vsc_pool[:].bitcast(U8), vcols, 0, PAGES * DV, U8)
+        vw = gather("vw", vw_pool[:].bitcast(U32), vcols, 0, PAGES * DV, U32)
+
+        scores = []
+        for u in range(PAGES):
+            page = slice(u * PAGE, (u + 1) * PAGE)
+            score_bank = ps.tile([P, PAGE], F32, name="score_bank%d" % u)
             nc.tensor.matmul_mx(
                 score_bank[:],
                 lhsT=qw[:].bitcast(FP8X4),
                 lhsT_scale=qs[:].bitcast(U8)[Q_PLANE:, :],
-                rhs=kw[:].bitcast(FP8X4),
-                rhs_scale=ks[u][K_PLANE:, :],
+                rhs=kw[:, page].bitcast(FP8X4),
+                rhs_scale=ks[K_PLANE:, page],
                 start=True,
                 stop=True,
             )
             score = sbuf("score%d" % u, [P, PACK, P], F32)
             nc.scalar.copy(score[:], score_bank[:].rearrange("q (m t) -> q t m", t=PACK))
-            turned = ps.tile([P, PACK, NQ], F32, name="turned", tag="turned", bufs=2)
+            scores.append(score)
+
+        silu = []
+        for u in range(PAGES):
+            turned = ps.tile([P, PACK, NQ], F32, name="turned%d" % u)
             for t in range(PACK):
-                nc.tensor.transpose(turned[:, t, :], score[:, t, :], ident[:])
+                nc.tensor.transpose(turned[:, t, :], scores[u][:, t, :], ident[:])
             p_tile = sbuf("silu%d" % u, [P, PACK, NQ], F32)
             for t in range(PACK):
                 nc.scalar.activation(p_tile[:, t, :], turned[:, t, :], ACT.Silu, bias=kb_cols[u][:, t : t + 1])
             silu.append(p_tile)
 
-        vs_cols = [to_columns("vs_col", gather("vs_row", vs_pool[:], slots, u, PAGE, F32), u) for u in range(PAGES)]
-        vsc = [gather("vsc", vsc_pool[:].bitcast(U8), vcols, u, DV, U8) for u in range(PAGES)]
-
-        acc = ps.tile([NQ, DV], F32, name="acc")
-        for u in range(PAGES):
+        def weigh(u):
             w = sbuf("w%d" % u, [P, NQ, PACK], BF16)
             nc.vector.tensor_tensor(
                 w[:],
@@ -142,21 +154,32 @@ def tile_attend_pkv8q_silu_kb_kernel(
                 vs_cols[u][:].unsqueeze(1).to_broadcast([P, NQ, PACK]),
                 MULT,
             )
-            vw = gather("vw", vw_pool[:].bitcast(U32), vcols, u, DV, U32)
+            return w
+
+        acc = ps.tile([NQ, DV], F32, name="acc")
+
+        def multiply(u, w):
             w_codes = sbuf("w_codes%d" % u, [P, NQ], U32)
             w_scales = sbuf("w_scales%d" % u, [P, NQ], U8)
             nc.vector.quantize_mx(
                 out=w_codes[:].bitcast(FP8X4), scales=w_scales[:], in_=w[:].rearrange("p q t -> p (q t)")
             )
+            cols = slice(u * DV, (u + 1) * DV)
             nc.tensor.matmul_mx(
                 acc[:],
                 lhsT=w_codes[:].bitcast(FP8X4),
                 lhsT_scale=w_scales[:],
-                rhs=vw[:].bitcast(FP8X4),
-                rhs_scale=vsc[u][V_PLANE:, :],
+                rhs=vw[:, cols].bitcast(FP8X4),
+                rhs_scale=vsc[V_PLANE:, cols],
                 start=(u == 0),
                 stop=(u == PAGES - 1),
             )
+
+        weights = [weigh(0)]
+        for u in range(PAGES):
+            if u + 1 < PAGES:
+                weights.append(weigh(u + 1))
+            multiply(u, weights[u])
 
         result = sbuf("result", [NQ, DV], F32)
         nc.scalar.activation(result[:], acc[:], ACT.Copy, scale=1.0 / 16.0)

@@ -14,6 +14,7 @@ NQ = 128
 LIST_ROWS = 16
 LIVE = P - 1
 K_PLANE, V_PLANE, Q_PLANE = 0, 4, 8
+KB_SPLIT = 2048
 
 FLOPS = 2 * NQ * PAGES * PAGE * (512 + DV)
 
@@ -41,49 +42,29 @@ def tile_attend_pkv8q_silu_kb_kernel(
 
         slots = sb.tile([P, PAGES * PAGE // LIST_ROWS], U16, name="slots")
         vcols = sb.tile([P, PAGES * DV // LIST_ROWS], U16, name="vcols")
-        kw_pool = sbuf("kw_pool", [P, POOL_TOKENS], I32)
-        ks_pool = sbuf("ks_pool", [P, POOL_TOKENS // 4], I32)
+        ks_pool = sb.tile([P, POOL_TOKENS // 4], I32, name="ks_pool", tag="ks_then_vs", align_bytes=64)
         vsc_pool = sbuf("vsc_pool", [P, POOL_PAGES * DV // 4], I32)
         kb_pool = sb.tile([P, POOL_TOKENS], F32, name="kb_pool", tag="kb_then_vw", align_bytes=64)
-        vs_pool = sbuf("vs_pool", [P, POOL_TOKENS], F32)
-        vs_head = sbuf("vs_head", [P, 8], F32)
         qw = sbuf("qw", [P, NQ], I32)
         qs = sbuf("qs", [P, NQ // 4], I32)
         ident = sbuf("ident", [P, P], F32)
-        zero = sbuf("zero", [P, 1], F32)
+        zero = sb.tile([P, 1], F32, name="zero", tag="zero_then_kw", align_bytes=64)
         warm = sbuf("warm", [P, 1], F32)
 
+        nc.vector.memset(vsc_pool[:], 0)
+        nc.vector.memset(ks_pool[:], 0)
         nc.vector.memset(zero[:], 0.0)
         nc.scalar.activation(warm[:], zero[:], ACT.Silu)
-        nc.vector.memset(ks_pool[:], 0)
-        nc.vector.memset(kb_pool[:LIVE, :], 0.0)
-        nc.vector.memset(qs[:], 0)
-        nc.vector.memset(vsc_pool[:], 0)
         nc.vector.memset(ident[:], 0.0)
+        nc.vector.memset(kb_pool[:LIVE, :KB_SPLIT], 0.0)
+        nc.vector.memset(qs[:], 0)
+        nc.gpsimd.memset(kb_pool[:LIVE, KB_SPLIT - 8 :], 0.0)
         make_identity(nc, ident[:], nomemset=True)
 
+        nc.sync.dma_start(vcols[:], voffs)
         nc.sync.dma_start(slots[:], offs)
         nc.sync.dma_start(kb_pool[LIVE:, :], kb[0:1, :])
-        nc.sync.dma_start(vs_head[:], vs[:, :8])
-        nc.sync.dma_start(kw_pool[:], k_words[0].rearrange("p n r -> p (n r)").bitcast(I32))
         nc.sync.dma_start(qw[:], q_words[0, 0].rearrange("p n r -> p (n r)").bitcast(I32))
-        nc.sync.dma_start(vs_pool[LIVE:, :], vs[0:1, :])
-        nc.sync.dma_start(vcols[:], voffs)
-        for quad in range(4):
-            nc.scalar.dma_start(
-                ks_pool[32 * quad + K_PLANE : 32 * quad + K_PLANE + 4, :],
-                k_scales[0, 4 * quad : 4 * quad + 4, :].bitcast(I32),
-            )
-        nc.scalar.activation(
-            vs_pool[:LIVE, :].rearrange("p (a b) -> p a b", b=8),
-            vs_head[:LIVE, :].unsqueeze(1).to_broadcast([LIVE, POOL_TOKENS // 8, 8]),
-            ACT.Copy,
-        )
-        for quad in range(4):
-            nc.sync.dma_start(
-                qs[32 * quad + Q_PLANE : 32 * quad + Q_PLANE + 4, :],
-                q_scales[0, 0, 4 * quad : 4 * quad + 4, :].bitcast(I32),
-            )
         for quad in range(4):
             nc.sync.dma_start(
                 vsc_pool[32 * quad + V_PLANE : 32 * quad + V_PLANE + 4, :].rearrange(
@@ -91,95 +72,102 @@ def tile_attend_pkv8q_silu_kb_kernel(
                 ),
                 v_scales[:, 4 * quad : 4 * quad + 4, :].rearrange("u f e -> f u e").bitcast(I32),
             )
+        for quad in range(4):
+            nc.sync.dma_start(
+                ks_pool[32 * quad + K_PLANE : 32 * quad + K_PLANE + 4, :],
+                k_scales[0, 4 * quad : 4 * quad + 4, :].bitcast(I32),
+            )
+        kw_pool = sb.tile([P, POOL_TOKENS], I32, name="kw_pool", tag="zero_then_kw", align_bytes=64)
+        nc.sync.dma_start(kw_pool[:], k_words[0].rearrange("p n r -> p (n r)").bitcast(I32))
+        for quad in range(4):
+            nc.sync.dma_start(
+                qs[32 * quad + Q_PLANE : 32 * quad + Q_PLANE + 4, :],
+                q_scales[0, 0, 4 * quad : 4 * quad + 4, :].bitcast(I32),
+            )
 
-        def gather(name, pool_view, entries, first, count, dtype):
+        def entries(list_tile, first, count):
+            return list_tile[:, first // LIST_ROWS : (first + count) // LIST_ROWS]
+
+        def gather(name, pool_view, list_tile, first, count, dtype):
             picked = sbuf(name, [P, count], dtype)
-            columns = entries[:, first // LIST_ROWS : (first + count) // LIST_ROWS]
-            nc.vector.tensor_copy(picked[:], pool_view.indirect(columns))
+            nc.vector.tensor_copy(picked[:], pool_view.indirect(entries(list_tile, first, count)))
             return picked
 
-        def to_columns(name, row):
-            columns = sbuf(name, [P, PACK], F32)
-            nc.sync.dma_start(columns[:], row.rearrange("o (m t) -> o m t", t=PACK))
-            return columns
+        def bank(tag, bufs):
+            return ps.tile([P, PACK, P], F32, name=tag, tag=tag, bufs=bufs)
 
-        kb_row = gather("kb_row", kb_pool[:], slots, 0, PAGES * PAGE, F32)
-        kb_cols = [to_columns("kb_cols%d" % u, kb_row[LIVE:, u * PAGE : (u + 1) * PAGE]) for u in range(PAGES)]
+        vsc = gather("vsc", vsc_pool[:].bitcast(U8), vcols, 0, PAGES * DV, U8)
+        ks = gather("ks", ks_pool[:].bitcast(U8), slots, 0, PAGES * PAGE, U8)
+        vs_pool = sb.tile([P, POOL_TOKENS], F32, name="vs_pool", tag="ks_then_vs", align_bytes=64)
+        nc.sync.dma_start(vs_pool[:], vs)
+
+        kb_cols = []
+        for u in range(PAGES):
+            kb_row = gather("kb_row%d" % u, kb_pool[:], slots, u * PAGE, PAGE, F32)
+            kb_bank = bank("kb_then_w_bank", 2)
+            for b in range(PACK):
+                nc.tensor.transpose(kb_bank[:, b, :], kb_row[:, b * P : (b + 1) * P], ident[:])
+            columns = sbuf("kb_cols%d" % u, [P, PACK], F32)
+            nc.scalar.copy(columns[:], kb_bank[:, :, LIVE])
+            kb_cols.append(columns)
         vw_pool = sb.tile([P, POOL_PAGES * DV], I32, name="vw_pool", tag="kb_then_vw", align_bytes=64)
         nc.sync.dma_start(
             vw_pool[:].rearrange("p (u e) -> p u e", u=POOL_PAGES),
             v_words.rearrange("u p e r -> p u (e r)").bitcast(I32),
         )
-        ks = gather("ks", ks_pool[:].bitcast(U8), slots, 0, PAGES * PAGE, U8)
-        kw = gather("kw", kw_pool[:].bitcast(U32), slots, 0, PAGES * PAGE, U32)
-        vs_cols = []
-        for u in range(PAGES):
-            vs_row = gather("vs_row%d" % u, vs_pool[:], slots, u * PAGE, PAGE, F32)
-            vs_cols.append(to_columns("vs_cols%d" % u, vs_row[LIVE:, :]))
-        vsc = gather("vsc", vsc_pool[:].bitcast(U8), vcols, 0, PAGES * DV, U8)
-        vw = gather("vw", vw_pool[:].bitcast(U32), vcols, 0, PAGES * DV, U32)
-
-        scores = []
-        for u in range(PAGES):
-            page = slice(u * PAGE, (u + 1) * PAGE)
-            score_bank = ps.tile([P, PAGE], F32, name="score_bank%d" % u)
-            nc.tensor.matmul_mx(
-                score_bank[:],
-                lhsT=qw[:].bitcast(FP8X4),
-                lhsT_scale=qs[:].bitcast(U8)[Q_PLANE:, :],
-                rhs=kw[:, page].bitcast(FP8X4),
-                rhs_scale=ks[K_PLANE:, page],
-                start=True,
-                stop=True,
-            )
-            score = sbuf("score%d" % u, [P, PACK, P], F32)
-            nc.scalar.copy(score[:], score_bank[:].rearrange("q (m t) -> q t m", t=PACK))
-            scores.append(score)
 
         silu = []
         for u in range(PAGES):
-            turned = ps.tile([P, PACK, NQ], F32, name="turned%d" % u)
-            for t in range(PACK):
-                nc.tensor.transpose(turned[:, t, :], scores[u][:, t, :], ident[:])
-            p_tile = sbuf("silu%d" % u, [P, PACK, NQ], F32)
-            for t in range(PACK):
-                nc.scalar.activation(p_tile[:, t, :], turned[:, t, :], ACT.Silu, bias=kb_cols[u][:, t : t + 1])
-            silu.append(p_tile)
+            kw = gather("kw%d" % u, kw_pool[:].bitcast(U32), slots, u * PAGE, PAGE, U32)
+            score_bank = bank("score_bank", 3)
+            for b in range(PACK):
+                nc.tensor.matmul_mx(
+                    score_bank[:, b, :],
+                    lhsT=kw[:, b * P : (b + 1) * P].bitcast(FP8X4),
+                    lhsT_scale=ks[K_PLANE:, u * PAGE + b * P : u * PAGE + (b + 1) * P],
+                    rhs=qw[:].bitcast(FP8X4),
+                    rhs_scale=qs[:].bitcast(U8)[Q_PLANE:, :],
+                    start=True,
+                    stop=True,
+                )
+            by_slot = sbuf("silu_by_slot%d" % u, [P, PACK, NQ], F32)
+            for b in range(PACK):
+                nc.scalar.activation(by_slot[:, b, :], score_bank[:, b, :], ACT.Silu, bias=kb_cols[u][:, b : b + 1])
+            silu_bank = bank("silu_bank", 2)
+            for b in range(PACK):
+                nc.tensor.transpose(silu_bank[:, b, :], by_slot[:, b, :], ident[:])
+            by_query = sbuf("silu_by_query%d" % u, [NQ, PAGE], F32)
+            nc.scalar.copy(by_query[:], silu_bank[:].rearrange("q b m -> q (b m)"))
+            silu.append(by_query)
 
-        def weigh(u):
-            w = sbuf("w%d" % u, [P, NQ, PACK], BF16)
-            nc.vector.tensor_tensor(
-                w[:],
-                silu[u][:].rearrange("p t q -> p q t"),
-                vs_cols[u][:].unsqueeze(1).to_broadcast([P, NQ, PACK]),
-                MULT,
-            )
-            return w
+        weights = []
+        for u in range(PAGES):
+            w = sbuf("w%d" % u, [NQ, PAGE], F32)
+            nc.vector.tensor_tensor(w[:], vs_pool[:].indirect(entries(slots, u * PAGE, PAGE)), silu[u][:], MULT)
+            w_bank = bank("kb_then_w_bank", 2)
+            for t in range(PACK):
+                nc.tensor.transpose(w_bank[:, t, :], w[:, t::PACK], ident[:])
+            grouped = sbuf("grouped%d" % u, [P, NQ, PACK], BF16)
+            nc.scalar.copy(grouped[:], w_bank[:].rearrange("p t q -> p q t"))
+            weights.append(grouped)
 
         acc = ps.tile([NQ, DV], F32, name="acc")
-
-        def multiply(u, w):
+        for u in range(PAGES):
+            vw = gather("vw%d" % u, vw_pool[:].bitcast(U32), vcols, u * DV, DV, U32)
             w_codes = sbuf("w_codes%d" % u, [P, NQ], U32)
             w_scales = sbuf("w_scales%d" % u, [P, NQ], U8)
             nc.vector.quantize_mx(
-                out=w_codes[:].bitcast(FP8X4), scales=w_scales[:], in_=w[:].rearrange("p q t -> p (q t)")
+                out=w_codes[:].bitcast(FP8X4), scales=w_scales[:], in_=weights[u][:].rearrange("p q t -> p (q t)")
             )
-            cols = slice(u * DV, (u + 1) * DV)
             nc.tensor.matmul_mx(
                 acc[:],
                 lhsT=w_codes[:].bitcast(FP8X4),
                 lhsT_scale=w_scales[:],
-                rhs=vw[:, cols].bitcast(FP8X4),
-                rhs_scale=vsc[V_PLANE:, cols],
+                rhs=vw[:].bitcast(FP8X4),
+                rhs_scale=vsc[V_PLANE:, u * DV : (u + 1) * DV],
                 start=(u == 0),
                 stop=(u == PAGES - 1),
             )
-
-        weights = [weigh(0)]
-        for u in range(PAGES):
-            if u + 1 < PAGES:
-                weights.append(weigh(u + 1))
-            multiply(u, weights[u])
 
         result = sbuf("result", [NQ, DV], F32)
         nc.scalar.activation(result[:], acc[:], ACT.Copy, scale=1.0 / 16.0)

@@ -6,6 +6,7 @@ from concourse.masks import make_identity
 P = 128
 PACK = 4
 PAGE = P * PACK
+HALF = PAGE // 2
 PAGES = 3
 POOL_TOKENS = 4096
 POOL_PAGES = POOL_TOKENS // PAGE
@@ -14,7 +15,7 @@ NQ = 128
 LIST_ROWS = 16
 LIVE = P - 1
 K_PLANE, V_PLANE, Q_PLANE = 0, 4, 8
-KB_SPLIT = 2048
+KB_SPLIT = 512
 
 FLOPS = 2 * NQ * PAGES * PAGE * (512 + DV)
 
@@ -35,6 +36,8 @@ def tile_attend_pkv8q_silu_kb_kernel(
     nc = tc.nc
     with ExitStack() as ctx:
         sb = ctx.enter_context(tc.tile_pool(name="sb", bufs=1))
+        reused = ctx.enter_context(tc.tile_pool(name="reused", bufs=1))
+        early = ctx.enter_context(tc.tile_pool(name="early", bufs=1))
         ps = ctx.enter_context(tc.psum_pool(name="ps", bufs=1))
 
         def sbuf(name, shape, dtype):
@@ -42,14 +45,13 @@ def tile_attend_pkv8q_silu_kb_kernel(
 
         slots = sb.tile([P, PAGES * PAGE // LIST_ROWS], U16, name="slots")
         vcols = sb.tile([P, PAGES * DV // LIST_ROWS], U16, name="vcols")
-        ks_pool = sb.tile([P, POOL_TOKENS // 4], I32, name="ks_pool", tag="ks_then_vs", align_bytes=64)
+        ks_pool = reused.tile([P, POOL_TOKENS // 4], I32, name="ks_pool", offset=8 * PAGE, align_bytes=64)
         vsc_pool = sbuf("vsc_pool", [P, POOL_PAGES * DV // 4], I32)
         kb_pool = sb.tile([P, POOL_TOKENS], F32, name="kb_pool", tag="kb_then_vw", align_bytes=64)
-        qw = sbuf("qw", [P, NQ], I32)
         qs = sbuf("qs", [P, NQ // 4], I32)
         ident = sbuf("ident", [P, P], F32)
-        zero = sb.tile([P, 1], F32, name="zero", tag="zero_then_kw", align_bytes=64)
-        warm = sbuf("warm", [P, 1], F32)
+        zero = early.tile([P, 32], F32, name="zero", offset=4 * POOL_TOKENS - 64, align_bytes=64)
+        warm = sbuf("warm", [P, 32], F32)
 
         nc.vector.memset(vsc_pool[:], 0)
         nc.vector.memset(ks_pool[:], 0)
@@ -63,8 +65,7 @@ def tile_attend_pkv8q_silu_kb_kernel(
 
         nc.sync.dma_start(vcols[:], voffs)
         nc.sync.dma_start(slots[:], offs)
-        nc.sync.dma_start(kb_pool[LIVE:, :], kb[0:1, :])
-        nc.sync.dma_start(qw[:], q_words[0, 0].rearrange("p n r -> p (n r)").bitcast(I32))
+        nc.gpsimd.dma_start(kb_pool[LIVE:, :], kb[0:1, :])
         for quad in range(4):
             nc.sync.dma_start(
                 vsc_pool[32 * quad + V_PLANE : 32 * quad + V_PLANE + 4, :].rearrange(
@@ -77,8 +78,10 @@ def tile_attend_pkv8q_silu_kb_kernel(
                 ks_pool[32 * quad + K_PLANE : 32 * quad + K_PLANE + 4, :],
                 k_scales[0, 4 * quad : 4 * quad + 4, :].bitcast(I32),
             )
-        kw_pool = sb.tile([P, POOL_TOKENS], I32, name="kw_pool", tag="zero_then_kw", align_bytes=64)
+        kw_pool = early.tile([P, POOL_TOKENS], I32, name="kw_pool", offset=0, align_bytes=64)
         nc.sync.dma_start(kw_pool[:], k_words[0].rearrange("p n r -> p (n r)").bitcast(I32))
+        qw = early.tile([P, NQ], I32, name="qw", offset=4 * POOL_TOKENS, align_bytes=64)
+        nc.sync.dma_start(qw[:], q_words[0, 0].rearrange("p n r -> p (n r)").bitcast(I32))
         for quad in range(4):
             nc.sync.dma_start(
                 qs[32 * quad + Q_PLANE : 32 * quad + Q_PLANE + 4, :],
@@ -93,65 +96,74 @@ def tile_attend_pkv8q_silu_kb_kernel(
             nc.vector.tensor_copy(picked[:], pool_view.indirect(entries(list_tile, first, count)))
             return picked
 
-        def bank(tag, bufs):
-            return ps.tile([P, PACK, P], F32, name=tag, tag=tag, bufs=bufs)
+        def bank(tag, blocks, bufs):
+            return ps.tile([P, blocks, P], F32, name=tag, tag=tag, bufs=bufs)
 
         vsc = gather("vsc", vsc_pool[:].bitcast(U8), vcols, 0, PAGES * DV, U8)
         ks = gather("ks", ks_pool[:].bitcast(U8), slots, 0, PAGES * PAGE, U8)
-        vs_pool = sb.tile([P, POOL_TOKENS], F32, name="vs_pool", tag="ks_then_vs", align_bytes=64)
+        vs_pool = reused.tile([P, POOL_TOKENS], F32, name="vs_pool", offset=12 * PAGE, align_bytes=64)
         nc.sync.dma_start(vs_pool[:], vs)
 
-        kb_cols = []
+        kb_rows = reused.tile([P, PAGES * PAGE], F32, name="kb_rows", offset=0, align_bytes=64)
+        silu = []
         for u in range(PAGES):
-            kb_row = gather("kb_row%d" % u, kb_pool[:], slots, u * PAGE, PAGE, F32)
-            kb_bank = bank("kb_then_w_bank", 2)
+            kb_row = kb_rows[:, u * PAGE : (u + 1) * PAGE]
+            nc.vector.tensor_copy(kb_row, kb_pool[:].indirect(entries(slots, u * PAGE, PAGE)))
+            kb_bank = bank("kb_then_w_bank", PACK, 2)
             for b in range(PACK):
                 nc.tensor.transpose(kb_bank[:, b, :], kb_row[:, b * P : (b + 1) * P], ident[:])
-            columns = sbuf("kb_cols%d" % u, [P, PACK], F32)
-            nc.scalar.copy(columns[:], kb_bank[:, :, LIVE])
-            kb_cols.append(columns)
+            kb_cols = sbuf("kb_cols%d" % u, [P, PACK], F32)
+            nc.scalar.copy(kb_cols[:], kb_bank[:, :, LIVE])
+
+            kw = gather("kw%d" % u, kw_pool[:].bitcast(U32), slots, u * PAGE, PAGE, U32)
+            for half in range(2):
+                score_bank = bank("score_bank", 2, 3)
+                for j in range(2):
+                    b = 2 * half + j
+                    nc.tensor.matmul_mx(
+                        score_bank[:, j, :],
+                        lhsT=kw[:, b * P : (b + 1) * P].bitcast(FP8X4),
+                        lhsT_scale=ks[K_PLANE:, u * PAGE + b * P : u * PAGE + (b + 1) * P],
+                        rhs=qw[:].bitcast(FP8X4),
+                        rhs_scale=qs[:].bitcast(U8)[Q_PLANE:, :],
+                        start=True,
+                        stop=True,
+                    )
+                by_slot = sbuf("silu_by_slot%d_%d" % (u, half), [P, 2, NQ], F32)
+                for j in range(2):
+                    b = 2 * half + j
+                    nc.scalar.activation(by_slot[:, j, :], score_bank[:, j, :], ACT.Silu, bias=kb_cols[:, b : b + 1])
+                silu_bank = bank("silu_bank", 2, 2)
+                for j in range(2):
+                    nc.tensor.transpose(silu_bank[:, j, :], by_slot[:, j, :], ident[:])
+                by_query = sbuf("silu_by_query%d_%d" % (u, half), [NQ, HALF], F32)
+                nc.scalar.copy(by_query[:], silu_bank[:].rearrange("q b m -> q (b m)"))
+                silu.append(by_query)
+
         vw_pool = sb.tile([P, POOL_PAGES * DV], I32, name="vw_pool", tag="kb_then_vw", align_bytes=64)
         nc.sync.dma_start(
             vw_pool[:].rearrange("p (u e) -> p u e", u=POOL_PAGES),
             v_words.rearrange("u p e r -> p u (e r)").bitcast(I32),
         )
 
-        silu = []
-        for u in range(PAGES):
-            kw = gather("kw%d" % u, kw_pool[:].bitcast(U32), slots, u * PAGE, PAGE, U32)
-            score_bank = bank("score_bank", 3)
-            for b in range(PACK):
-                nc.tensor.matmul_mx(
-                    score_bank[:, b, :],
-                    lhsT=kw[:, b * P : (b + 1) * P].bitcast(FP8X4),
-                    lhsT_scale=ks[K_PLANE:, u * PAGE + b * P : u * PAGE + (b + 1) * P],
-                    rhs=qw[:].bitcast(FP8X4),
-                    rhs_scale=qs[:].bitcast(U8)[Q_PLANE:, :],
-                    start=True,
-                    stop=True,
-                )
-            by_slot = sbuf("silu_by_slot%d" % u, [P, PACK, NQ], F32)
-            for b in range(PACK):
-                nc.scalar.activation(by_slot[:, b, :], score_bank[:, b, :], ACT.Silu, bias=kb_cols[u][:, b : b + 1])
-            silu_bank = bank("silu_bank", 2)
-            for b in range(PACK):
-                nc.tensor.transpose(silu_bank[:, b, :], by_slot[:, b, :], ident[:])
-            by_query = sbuf("silu_by_query%d" % u, [NQ, PAGE], F32)
-            nc.scalar.copy(by_query[:], silu_bank[:].rearrange("q b m -> q (b m)"))
-            silu.append(by_query)
-
         weights = []
         for u in range(PAGES):
             w = sbuf("w%d" % u, [NQ, PAGE], F32)
-            nc.vector.tensor_tensor(w[:], vs_pool[:].indirect(entries(slots, u * PAGE, PAGE)), silu[u][:], MULT)
-            w_bank = bank("kb_then_w_bank", 2)
+            for half in range(2):
+                nc.vector.tensor_tensor(
+                    w[:, half * HALF : (half + 1) * HALF],
+                    vs_pool[:].indirect(entries(slots, u * PAGE + half * HALF, HALF)),
+                    silu[2 * u + half][:],
+                    MULT,
+                )
+            w_bank = bank("kb_then_w_bank", PACK, 2)
             for t in range(PACK):
                 nc.tensor.transpose(w_bank[:, t, :], w[:, t::PACK], ident[:])
             grouped = sbuf("grouped%d" % u, [P, NQ, PACK], BF16)
             nc.scalar.copy(grouped[:], w_bank[:].rearrange("p t q -> p q t"))
             weights.append(grouped)
 
-        acc = ps.tile([NQ, DV], F32, name="acc")
+        acc = [bank("silu_bank", 2, 2) for side in range(2)]
         for u in range(PAGES):
             vw = gather("vw%d" % u, vw_pool[:].bitcast(U32), vcols, u * DV, DV, U32)
             w_codes = sbuf("w_codes%d" % u, [P, NQ], U32)
@@ -159,16 +171,20 @@ def tile_attend_pkv8q_silu_kb_kernel(
             nc.vector.quantize_mx(
                 out=w_codes[:].bitcast(FP8X4), scales=w_scales[:], in_=weights[u][:].rearrange("p q t -> p (q t)")
             )
-            nc.tensor.matmul_mx(
-                acc[:],
-                lhsT=w_codes[:].bitcast(FP8X4),
-                lhsT_scale=w_scales[:],
-                rhs=vw[:].bitcast(FP8X4),
-                rhs_scale=vsc[V_PLANE:, u * DV : (u + 1) * DV],
-                start=(u == 0),
-                stop=(u == PAGES - 1),
-            )
+            for side in range(2):
+                nc.tensor.matmul_mx(
+                    acc[side][:, 0, :],
+                    lhsT=w_codes[:].bitcast(FP8X4),
+                    lhsT_scale=w_scales[:],
+                    rhs=vw[:, side * P : (side + 1) * P].bitcast(FP8X4),
+                    rhs_scale=vsc[V_PLANE:, u * DV + side * P : u * DV + (side + 1) * P],
+                    start=(u == 0),
+                    stop=(u == PAGES - 1),
+                )
 
-        result = sbuf("result", [NQ, DV], F32)
-        nc.scalar.activation(result[:], acc[:], ACT.Copy, scale=1.0 / 16.0)
-        nc.sync.dma_start(out[0], result[:])
+        left = sbuf("left", [NQ, P], F32)
+        nc.vector.tensor_scalar_mul(left[:], acc[0][:, 0, :], 1.0 / 16.0)
+        nc.sync.dma_start(out[0, :, :P], left[:])
+        right = sbuf("right", [NQ, P], F32)
+        nc.scalar.activation(right[:], acc[1][:, 0, :], ACT.Copy, scale=1.0 / 16.0)
+        nc.scalar.dma_start(out[0, :, P:], right[:])

@@ -16,6 +16,7 @@ LIST_ROWS = 16
 LIVE = P - 1
 K_PLANE, V_PLANE, Q_PLANE = 0, 4, 8
 KB_SPLIT = 512
+QUAD = 32
 
 FLOPS = 2 * NQ * PAGES * PAGE * (512 + DV)
 
@@ -66,27 +67,19 @@ def tile_attend_pkv8q_silu_kb_kernel(
         nc.sync.dma_start(vcols[:], voffs)
         nc.sync.dma_start(slots[:], offs)
         nc.gpsimd.dma_start(kb_pool[LIVE:, :], kb[0:1, :])
-        for quad in range(4):
+        for j in range(4):
             nc.sync.dma_start(
-                vsc_pool[32 * quad + V_PLANE : 32 * quad + V_PLANE + 4, :].rearrange(
-                    "p (u e) -> p u e", u=POOL_PAGES
-                ),
-                v_scales[:, 4 * quad : 4 * quad + 4, :].rearrange("u f e -> f u e").bitcast(I32),
+                vsc_pool[V_PLANE + j : P : QUAD, :].rearrange("p (u e) -> p u e", u=POOL_PAGES),
+                v_scales[:, j::4, :].rearrange("u f e -> f u e").bitcast(I32),
             )
-        for quad in range(4):
-            nc.sync.dma_start(
-                ks_pool[32 * quad + K_PLANE : 32 * quad + K_PLANE + 4, :],
-                k_scales[0, 4 * quad : 4 * quad + 4, :].bitcast(I32),
-            )
+        for j in range(4):
+            nc.sync.dma_start(ks_pool[K_PLANE + j : P : QUAD, :], k_scales[0, j::4, :].bitcast(I32))
         kw_pool = early.tile([P, POOL_TOKENS], I32, name="kw_pool", offset=0, align_bytes=64)
         nc.sync.dma_start(kw_pool[:], k_words[0].rearrange("p n r -> p (n r)").bitcast(I32))
         qw = early.tile([P, NQ], I32, name="qw", offset=4 * POOL_TOKENS, align_bytes=64)
         nc.sync.dma_start(qw[:], q_words[0, 0].rearrange("p n r -> p (n r)").bitcast(I32))
-        for quad in range(4):
-            nc.sync.dma_start(
-                qs[32 * quad + Q_PLANE : 32 * quad + Q_PLANE + 4, :],
-                q_scales[0, 0, 4 * quad : 4 * quad + 4, :].bitcast(I32),
-            )
+        for j in range(4):
+            nc.sync.dma_start(qs[Q_PLANE + j : P : QUAD, :], q_scales[0, 0, j::4, :].bitcast(I32))
 
         def entries(list_tile, first, count):
             return list_tile[:, first // LIST_ROWS : (first + count) // LIST_ROWS]
@@ -99,7 +92,7 @@ def tile_attend_pkv8q_silu_kb_kernel(
         def bank(tag, blocks, bufs):
             return ps.tile([P, blocks, P], F32, name=tag, tag=tag, bufs=bufs)
 
-        vsc = gather("vsc", vsc_pool[:].bitcast(U8), vcols, 0, PAGES * DV, U8)
+        vsc_early = gather("vsc_early", vsc_pool[:].bitcast(U8), vcols, 0, (PAGES - 1) * DV, U8)
         ks = gather("ks", ks_pool[:].bitcast(U8), slots, 0, PAGES * PAGE, U8)
         vs_pool = reused.tile([P, POOL_TOKENS], F32, name="vs_pool", offset=12 * PAGE, align_bytes=64)
         nc.sync.dma_start(vs_pool[:], vs)
@@ -146,21 +139,33 @@ def tile_attend_pkv8q_silu_kb_kernel(
             v_words.rearrange("u p e r -> p u (e r)").bitcast(I32),
         )
 
+        vsc_late = early.tile([P, DV], U8, name="vsc_late", offset=0, align_bytes=64)
+        nc.vector.tensor_copy(vsc_late[:], vsc_pool[:].bitcast(U8).indirect(entries(vcols, (PAGES - 1) * DV, DV)))
+        vsc = [vsc_early[:, :DV], vsc_early[:, DV:], vsc_late[:]]
+
         weights = []
         for u in range(PAGES):
-            w = sbuf("w%d" % u, [NQ, PAGE], F32)
+            pairs = sbuf("pairs%d" % u, [NQ, 2, P, 2], BF16)
             for half in range(2):
+                w = sbuf("w%d_%d" % (u, half), [NQ, HALF], F32)
                 nc.vector.tensor_tensor(
-                    w[:, half * HALF : (half + 1) * HALF],
+                    w[:],
                     vs_pool[:].indirect(entries(slots, u * PAGE + half * HALF, HALF)),
                     silu[2 * u + half][:],
                     MULT,
                 )
-            w_bank = bank("kb_then_w_bank", PACK, 2)
-            for t in range(PACK):
-                nc.tensor.transpose(w_bank[:, t, :], w[:, t::PACK], ident[:])
-            grouped = sbuf("grouped%d" % u, [P, NQ, PACK], BF16)
-            nc.scalar.copy(grouped[:], w_bank[:].rearrange("p t q -> p q t"))
+                nc.scalar.copy(
+                    pairs[:, :, half * P // 2 : (half + 1) * P // 2, :].rearrange("q h p e -> q p h e"),
+                    w[:].rearrange("q (p h e) -> q p h e", h=2, e=2),
+                )
+            pair_words = pairs[:].rearrange("q h p e -> q (h p e)").bitcast(F32)
+            w_bank = bank("kb_then_w_bank", 2, 2)
+            for h in range(2):
+                nc.tensor.transpose(w_bank[:, h, :], pair_words[:, h * P : (h + 1) * P], ident[:])
+            grouped = sbuf("grouped%d" % u, [P, NQ * PACK], BF16)
+            nc.scalar.copy(
+                grouped[:].bitcast(F32).rearrange("p (q h) -> p q h", h=2), w_bank[:].rearrange("p h q -> p q h")
+            )
             weights.append(grouped)
 
         acc = [bank("silu_bank", 2, 2) for side in range(2)]
@@ -169,7 +174,7 @@ def tile_attend_pkv8q_silu_kb_kernel(
             w_codes = sbuf("w_codes%d" % u, [P, NQ], U32)
             w_scales = sbuf("w_scales%d" % u, [P, NQ], U8)
             nc.vector.quantize_mx(
-                out=w_codes[:].bitcast(FP8X4), scales=w_scales[:], in_=weights[u][:].rearrange("p q t -> p (q t)")
+                out=w_codes[:].bitcast(FP8X4), scales=w_scales[:], in_=weights[u][:]
             )
             for side in range(2):
                 nc.tensor.matmul_mx(
@@ -177,7 +182,7 @@ def tile_attend_pkv8q_silu_kb_kernel(
                     lhsT=w_codes[:].bitcast(FP8X4),
                     lhsT_scale=w_scales[:],
                     rhs=vw[:, side * P : (side + 1) * P].bitcast(FP8X4),
-                    rhs_scale=vsc[V_PLANE:, u * DV + side * P : u * DV + (side + 1) * P],
+                    rhs_scale=vsc[u][V_PLANE:, side * P : (side + 1) * P],
                     start=(u == 0),
                     stop=(u == PAGES - 1),
                 )

@@ -1,13 +1,12 @@
 from contextlib import ExitStack
 
 import concourse.mybir as mybir
-from concourse.masks import make_identity
 
 P = 128
 PACK = 4
 PAGE = P * PACK
-HALF = PAGE // 2
 PAGES = 3
+SLOTS = PAGES * PAGE
 POOL_TOKENS = 4096
 POOL_PAGES = POOL_TOKENS // PAGE
 DV = 256
@@ -15,10 +14,10 @@ NQ = 128
 LIST_ROWS = 16
 LIVE = P - 1
 K_PLANE, V_PLANE, Q_PLANE = 0, 4, 8
-KB_SPLIT = 512
 QUAD = 32
+VS_SPLIT = 768
 
-FLOPS = 2 * NQ * PAGES * PAGE * (512 + DV)
+FLOPS = 2 * NQ * SLOTS * (512 + DV)
 
 F32 = mybir.dt.float32
 BF16 = mybir.dt.bfloat16
@@ -28,7 +27,7 @@ U16 = mybir.dt.uint16
 U8 = mybir.dt.uint8
 FP8X4 = mybir.dt.float8_e4m3fn_x4
 ACT = mybir.ActivationFunctionType
-MULT = mybir.AluOpType.mult
+ALU = mybir.AluOpType
 
 
 def tile_attend_pkv8q_silu_kb_kernel(
@@ -37,144 +36,138 @@ def tile_attend_pkv8q_silu_kb_kernel(
     nc = tc.nc
     with ExitStack() as ctx:
         sb = ctx.enter_context(tc.tile_pool(name="sb", bufs=1))
-        reused = ctx.enter_context(tc.tile_pool(name="reused", bufs=1))
-        early = ctx.enter_context(tc.tile_pool(name="early", bufs=1))
+        after_ramp = ctx.enter_context(tc.tile_pool(name="after_ramp", bufs=1))
+        after_ks = ctx.enter_context(tc.tile_pool(name="after_ks", bufs=1))
+        after_deal = ctx.enter_context(tc.tile_pool(name="after_deal", bufs=1))
         ps = ctx.enter_context(tc.psum_pool(name="ps", bufs=1))
 
         def sbuf(name, shape, dtype):
             return sb.tile(shape, dtype, name=name, align_bytes=64)
 
-        slots = sb.tile([P, PAGES * PAGE // LIST_ROWS], U16, name="slots")
-        vcols = sb.tile([P, PAGES * DV // LIST_ROWS], U16, name="vcols")
-        ks_pool = reused.tile([P, POOL_TOKENS // 4], I32, name="ks_pool", offset=8 * PAGE, align_bytes=64)
-        vsc_pool = sbuf("vsc_pool", [P, POOL_PAGES * DV // 4], I32)
-        kb_pool = sb.tile([P, POOL_TOKENS], F32, name="kb_pool", tag="kb_then_vw", align_bytes=64)
-        qs = sbuf("qs", [P, NQ // 4], I32)
-        ident = sbuf("ident", [P, P], F32)
-        zero = early.tile([P, 32], F32, name="zero", offset=4 * POOL_TOKENS - 64, align_bytes=64)
-        warm = sbuf("warm", [P, 32], F32)
-
-        nc.vector.memset(vsc_pool[:], 0)
-        nc.vector.memset(ks_pool[:], 0)
-        nc.vector.memset(zero[:], 0.0)
-        nc.scalar.activation(warm[:], zero[:], ACT.Silu)
-        nc.vector.memset(ident[:], 0.0)
-        nc.vector.memset(kb_pool[:LIVE, :KB_SPLIT], 0.0)
-        nc.vector.memset(qs[:], 0)
-        nc.gpsimd.memset(kb_pool[:LIVE, KB_SPLIT - 8 :], 0.0)
-        make_identity(nc, ident[:], nomemset=True)
-
-        nc.sync.dma_start(vcols[:], voffs)
-        nc.sync.dma_start(slots[:], offs)
-        nc.gpsimd.dma_start(kb_pool[LIVE:, :], kb[0:1, :])
-        for j in range(4):
-            nc.sync.dma_start(
-                vsc_pool[V_PLANE + j : P : QUAD, :].rearrange("p (u e) -> p u e", u=POOL_PAGES),
-                v_scales[:, j::4, :].rearrange("u f e -> f u e").bitcast(I32),
-            )
-        for j in range(4):
-            nc.sync.dma_start(ks_pool[K_PLANE + j : P : QUAD, :], k_scales[0, j::4, :].bitcast(I32))
-        kw_pool = early.tile([P, POOL_TOKENS], I32, name="kw_pool", offset=0, align_bytes=64)
-        nc.sync.dma_start(kw_pool[:], k_words[0].rearrange("p n r -> p (n r)").bitcast(I32))
-        qw = early.tile([P, NQ], I32, name="qw", offset=4 * POOL_TOKENS, align_bytes=64)
-        nc.sync.dma_start(qw[:], q_words[0, 0].rearrange("p n r -> p (n r)").bitcast(I32))
-        for j in range(4):
-            nc.sync.dma_start(qs[Q_PLANE + j : P : QUAD, :], q_scales[0, 0, j::4, :].bitcast(I32))
+        def placed(pool, name, shape, dtype, offset):
+            return pool.tile(shape, dtype, name=name, offset=offset, align_bytes=64)
 
         def entries(list_tile, first, count):
             return list_tile[:, first // LIST_ROWS : (first + count) // LIST_ROWS]
 
-        def gather(name, pool_view, list_tile, first, count, dtype):
-            picked = sbuf(name, [P, count], dtype)
-            nc.vector.tensor_copy(picked[:], pool_view.indirect(entries(list_tile, first, count)))
-            return picked
+        def bank(tag, bufs):
+            return ps.tile([P, PACK, P], F32, name=tag, tag=tag, bufs=bufs)
 
-        def bank(tag, blocks, bufs):
-            return ps.tile([P, blocks, P], F32, name=tag, tag=tag, bufs=bufs)
+        slots = sb.tile([P, SLOTS // LIST_ROWS], U16, name="slots")
+        vcols = sb.tile([P, PAGES * DV // LIST_ROWS], U16, name="vcols")
+        nc.sync.dma_start(slots[:], offs)
+        nc.sync.dma_start(vcols[:], voffs)
+        kb_pool = sbuf("kb_pool", [P, POOL_TOKENS], F32)
+        nc.sync.dma_start(kb_pool[LIVE:, :], kb[0:1, :])
 
-        vsc_early = gather("vsc_early", vsc_pool[:].bitcast(U8), vcols, 0, (PAGES - 1) * DV, U8)
-        ks = gather("ks", ks_pool[:].bitcast(U8), slots, 0, PAGES * PAGE, U8)
-        vs_pool = reused.tile([P, POOL_TOKENS], F32, name="vs_pool", offset=12 * PAGE, align_bytes=64)
-        nc.sync.dma_start(vs_pool[:], vs)
+        vw_bytes = 4 * POOL_PAGES * DV
+        ks_pool = placed(after_ks, "ks_pool", [P, POOL_TOKENS // 4], I32, vw_bytes - 1024)
+        nc.vector.memset(ks_pool[:], 0)
+        for j in range(4):
+            nc.sync.dma_start(ks_pool[K_PLANE + j : P : QUAD, :], k_scales[0, j::4, :].bitcast(I32))
 
-        kb_rows = reused.tile([P, PAGES * PAGE], F32, name="kb_rows", offset=0, align_bytes=64)
-        silu = []
-        for u in range(PAGES):
-            kb_row = kb_rows[:, u * PAGE : (u + 1) * PAGE]
-            nc.vector.tensor_copy(kb_row, kb_pool[:].indirect(entries(slots, u * PAGE, PAGE)))
-            kb_bank = bank("kb_then_w_bank", PACK, 2)
-            for b in range(PACK):
-                nc.tensor.transpose(kb_bank[:, b, :], kb_row[:, b * P : (b + 1) * P], ident[:])
-            kb_cols = sbuf("kb_cols%d" % u, [P, PACK], F32)
-            nc.scalar.copy(kb_cols[:], kb_bank[:, :, LIVE])
+        ramp = placed(after_ramp, "ramp", [P, P], I32, 4 * POOL_TOKENS - 256)
+        nc.gpsimd.iota(ramp[:], pattern=[[1, P]], base=0, channel_multiplier=-1)
+        ident = sbuf("ident", [P, P], F32)
+        nc.vector.tensor_scalar(ident[:], ramp[:], 0.0, None, ALU.is_equal)
+        warm = sbuf("warm", [P, 32], F32)
+        nc.scalar.activation(warm[:], ident[:, :32], ACT.Silu)
 
-            kw = gather("kw%d" % u, kw_pool[:].bitcast(U32), slots, u * PAGE, PAGE, U32)
-            for half in range(2):
-                score_bank = bank("score_bank", 2, 3)
-                for j in range(2):
-                    b = 2 * half + j
-                    nc.tensor.matmul_mx(
-                        score_bank[:, j, :],
-                        lhsT=kw[:, b * P : (b + 1) * P].bitcast(FP8X4),
-                        lhsT_scale=ks[K_PLANE:, u * PAGE + b * P : u * PAGE + (b + 1) * P],
-                        rhs=qw[:].bitcast(FP8X4),
-                        rhs_scale=qs[:].bitcast(U8)[Q_PLANE:, :],
-                        start=True,
-                        stop=True,
-                    )
-                by_slot = sbuf("silu_by_slot%d_%d" % (u, half), [P, 2, NQ], F32)
-                for j in range(2):
-                    b = 2 * half + j
-                    nc.scalar.activation(by_slot[:, j, :], score_bank[:, j, :], ACT.Silu, bias=kb_cols[:, b : b + 1])
-                silu_bank = bank("silu_bank", 2, 2)
-                for j in range(2):
-                    nc.tensor.transpose(silu_bank[:, j, :], by_slot[:, j, :], ident[:])
-                by_query = sbuf("silu_by_query%d_%d" % (u, half), [NQ, HALF], F32)
-                nc.scalar.copy(by_query[:], silu_bank[:].rearrange("q b m -> q (b m)"))
-                silu.append(by_query)
+        kw_pool = placed(after_ramp, "kw_pool", [P, POOL_TOKENS], I32, 0)
+        nc.sync.dma_start(kw_pool[:], k_words[0].rearrange("p n r -> p (n r)").bitcast(I32))
+        qw = placed(after_ramp, "qw", [P, NQ], I32, 4 * POOL_TOKENS)
+        nc.sync.dma_start(qw[:], q_words[0, 0].rearrange("p n r -> p (n r)").bitcast(I32))
 
-        vw_pool = sb.tile([P, POOL_PAGES * DV], I32, name="vw_pool", tag="kb_then_vw", align_bytes=64)
+        qs = sbuf("qs", [P, NQ // 4], I32)
+        nc.vector.memset(qs[:], 0)
+        for j in range(4):
+            nc.scalar.dma_start(qs[Q_PLANE + j : P : QUAD, :], q_scales[0, 0, j::4, :].bitcast(I32))
+        nc.vector.memset(kb_pool[:LIVE, :], 0.0)
+        vs_pool = sbuf("vs_pool", [P, POOL_TOKENS], F32)
+        nc.vector.memset(vs_pool[:, :VS_SPLIT], 0.0)
+        nc.gpsimd.memset(vs_pool[:LIVE, VS_SPLIT - 8 :], 0.0)
+        nc.scalar.dma_start(vs_pool[LIVE:, :], vs[0:1, :])
+
+        def dealt(ap):
+            return ap.rearrange("p (u r s) -> p u s r", r=PACK, s=P)
+
+        def columns(name, rows):
+            turned = bank("turn_bank", 3)
+            for r in range(PACK):
+                nc.tensor.transpose(turned[:, r, :], rows[:, r * P : (r + 1) * P].bitcast(F32), ident[:])
+            cols = sbuf(name, [P, PACK], F32)
+            nc.scalar.copy(cols[:], turned[:, :, LIVE])
+            return cols
+
+        page_bytes = 4 * PAGE
+        ks_listed = placed(after_deal, "ks_listed", [P, (1 + 2 * PAGES) * page_bytes], U8, 0)[:, :SLOTS]
+        nc.vector.tensor_copy(ks_listed, ks_pool[:].bitcast(U8).indirect(slots[:]))
+        vw_pool = placed(after_ks, "vw_pool", [P, POOL_PAGES * DV], I32, 0)
         nc.sync.dma_start(
             vw_pool[:].rearrange("p (u e) -> p u e", u=POOL_PAGES),
             v_words.rearrange("u p e r -> p u (e r)").bitcast(I32),
         )
 
-        vsc_late = early.tile([P, DV], U8, name="vsc_late", offset=0, align_bytes=64)
-        nc.vector.tensor_copy(vsc_late[:], vsc_pool[:].bitcast(U8).indirect(entries(vcols, (PAGES - 1) * DV, DV)))
-        vsc = [vsc_early[:, :DV], vsc_early[:, DV:], vsc_late[:]]
+        kb_rows = sbuf("kb_rows", [P, SLOTS], U32)
+        nc.vector.tensor_copy(dealt(kb_rows[:]), kb_pool[:].bitcast(U32).indirect(slots[:]))
+        kb_cols = [columns("kb_cols%d" % u, kb_rows[:, u * PAGE : (u + 1) * PAGE]) for u in range(PAGES)]
 
-        weights = []
-        for u in range(PAGES):
-            pairs = sbuf("pairs%d" % u, [NQ, 2, P, 2], BF16)
-            for half in range(2):
-                w = sbuf("w%d_%d" % (u, half), [NQ, HALF], F32)
-                nc.vector.tensor_tensor(
-                    w[:],
-                    vs_pool[:].indirect(entries(slots, u * PAGE + half * HALF, HALF)),
-                    silu[2 * u + half][:],
-                    MULT,
-                )
-                nc.scalar.copy(
-                    pairs[:, :, half * P // 2 : (half + 1) * P // 2, :].rearrange("q h p e -> q p h e"),
-                    w[:].rearrange("q (p h e) -> q p h e", h=2, e=2),
-                )
-            pair_words = pairs[:].rearrange("q h p e -> q (h p e)").bitcast(F32)
-            w_bank = bank("kb_then_w_bank", 2, 2)
-            for h in range(2):
-                nc.tensor.transpose(w_bank[:, h, :], pair_words[:, h * P : (h + 1) * P], ident[:])
-            grouped = sbuf("grouped%d" % u, [P, NQ * PACK], BF16)
-            nc.scalar.copy(
-                grouped[:].bitcast(F32).rearrange("p (q h) -> p q h", h=2), w_bank[:].rearrange("p h q -> p q h")
+        ks = sbuf("ks", [P, SLOTS], U8)
+        nc.vector.tensor_copy(
+            ks[:].rearrange("p (u r s) -> p r u s", r=PACK, s=P),
+            ks_listed.rearrange("p (u s r) -> p r u s", r=PACK, s=P),
+        )
+        vsc_pool = placed(after_deal, "vsc_pool", [P, POOL_PAGES * DV // 4], I32, 0)
+        nc.gpsimd.memset(vsc_pool[:], 0)
+        for j in range(4):
+            nc.sync.dma_start(
+                vsc_pool[V_PLANE + j : P : QUAD, :].rearrange("p (u e) -> p u e", u=POOL_PAGES),
+                v_scales[:, j::4, :].rearrange("u f e -> f u e").bitcast(I32),
             )
-            weights.append(grouped)
 
-        acc = [bank("silu_bank", 2, 2) for side in range(2)]
+        silu = []
+        vs_cols = []
         for u in range(PAGES):
-            vw = gather("vw%d" % u, vw_pool[:].bitcast(U32), vcols, u * DV, DV, U32)
+            page = entries(slots, u * PAGE, PAGE)
+            kw = placed(after_deal, "kw%d" % u, [P, PAGE], U32, (1 + u) * page_bytes)
+            nc.vector.tensor_copy(dealt(kw[:]), kw_pool[:].bitcast(U32).indirect(page))
+            scores = bank("score_bank", 3)
+            for r in range(PACK):
+                nc.tensor.matmul_mx(
+                    scores[:, r, :],
+                    lhsT=kw[:, r * P : (r + 1) * P].bitcast(FP8X4),
+                    lhsT_scale=ks[K_PLANE:, u * PAGE + r * P : u * PAGE + (r + 1) * P],
+                    rhs=qw[:].bitcast(FP8X4),
+                    rhs_scale=qs[:].bitcast(U8)[Q_PLANE:, :],
+                    start=True,
+                    stop=True,
+                )
+            p = sbuf("p%d" % u, [P, PACK, NQ], F32)
+            for r in range(PACK):
+                nc.scalar.activation(p[:, r, :], scores[:, r, :], ACT.Silu, bias=kb_cols[u][:, r : r + 1])
+            silu.append(p)
+            vs_rows = placed(after_deal, "vs_rows%d" % u, [P, PAGE], U32, (1 + PAGES + u) * page_bytes)
+            nc.vector.tensor_copy(dealt(vs_rows[:]), vs_pool[:].bitcast(U32).indirect(page))
+            vs_cols.append(columns("vs_cols%d" % u, vs_rows[:]))
+
+        vsc = sbuf("vsc", [P, PAGES * DV], U8)
+        nc.vector.tensor_copy(vsc[:], vsc_pool[:].bitcast(U8).indirect(vcols[:]))
+
+        acc = [bank("acc%d" % side, 1) for side in range(2)]
+        for u in range(PAGES):
+            w = sbuf("w%d" % u, [P, NQ, PACK], BF16)
+            nc.vector.tensor_tensor(
+                w[:],
+                silu[u][:].rearrange("p r q -> p q r"),
+                vs_cols[u][:].unsqueeze(1).broadcast_to([P, NQ, PACK]),
+                ALU.mult,
+            )
+            vw = sbuf("vw%d" % u, [P, DV], U32)
+            nc.vector.tensor_copy(vw[:], vw_pool[:].bitcast(U32).indirect(entries(vcols, u * DV, DV)))
             w_codes = sbuf("w_codes%d" % u, [P, NQ], U32)
             w_scales = sbuf("w_scales%d" % u, [P, NQ], U8)
             nc.vector.quantize_mx(
-                out=w_codes[:].bitcast(FP8X4), scales=w_scales[:], in_=weights[u][:]
+                out=w_codes[:].bitcast(FP8X4), scales=w_scales[:], in_=w[:].rearrange("p q r -> p (q r)")
             )
             for side in range(2):
                 nc.tensor.matmul_mx(
@@ -182,7 +175,7 @@ def tile_attend_pkv8q_silu_kb_kernel(
                     lhsT=w_codes[:].bitcast(FP8X4),
                     lhsT_scale=w_scales[:],
                     rhs=vw[:, side * P : (side + 1) * P].bitcast(FP8X4),
-                    rhs_scale=vsc[u][V_PLANE:, side * P : (side + 1) * P],
+                    rhs_scale=vsc[V_PLANE:, u * DV + side * P : u * DV + (side + 1) * P],
                     start=(u == 0),
                     stop=(u == PAGES - 1),
                 )

@@ -38,7 +38,6 @@ def tile_attend_pkv8q_silu_kb_kernel(
         sb = ctx.enter_context(tc.tile_pool(name="sb", bufs=1))
         after_ramp = ctx.enter_context(tc.tile_pool(name="after_ramp", bufs=1))
         after_ks = ctx.enter_context(tc.tile_pool(name="after_ks", bufs=1))
-        after_deal = ctx.enter_context(tc.tile_pool(name="after_deal", bufs=1))
         ps = ctx.enter_context(tc.psum_pool(name="ps", bufs=1))
 
         def sbuf(name, shape, dtype):
@@ -88,36 +87,25 @@ def tile_attend_pkv8q_silu_kb_kernel(
         nc.gpsimd.memset(vs_pool[:LIVE, VS_SPLIT - 8 :], 0.0)
         nc.scalar.dma_start(vs_pool[LIVE:, :], vs[0:1, :])
 
-        def dealt(ap):
-            return ap.rearrange("p (u r s) -> p u s r", r=PACK, s=P)
-
-        def columns(name, rows):
-            turned = bank("turn_bank", 3)
+        kb_cols = []
+        for u in range(PAGES):
+            kb_row = sbuf("kb_row%d" % u, [P, PAGE], F32)
+            nc.vector.tensor_copy(kb_row[:], kb_pool[:].indirect(entries(slots, u * PAGE, PAGE)))
+            turned = bank("kb_then_acc_bank", 2)
             for r in range(PACK):
-                nc.tensor.transpose(turned[:, r, :], rows[:, r * P : (r + 1) * P].bitcast(F32), ident[:])
-            cols = sbuf(name, [P, PACK], F32)
+                nc.tensor.transpose(turned[:, r, :], kb_row[:, r::PACK], ident[:])
+            cols = sbuf("kb_cols%d" % u, [P, PACK], F32)
             nc.scalar.copy(cols[:], turned[:, :, LIVE])
-            return cols
+            kb_cols.append(cols)
 
-        page_bytes = 4 * PAGE
-        ks_listed = placed(after_deal, "ks_listed", [P, (1 + 2 * PAGES) * page_bytes], U8, 0)[:, :SLOTS]
-        nc.vector.tensor_copy(ks_listed, ks_pool[:].bitcast(U8).indirect(slots[:]))
+        ks = sbuf("ks", [P, SLOTS], U8)
+        nc.vector.tensor_copy(ks[:], ks_pool[:].bitcast(U8).indirect(slots[:]))
         vw_pool = placed(after_ks, "vw_pool", [P, POOL_PAGES * DV], I32, 0)
         nc.sync.dma_start(
             vw_pool[:].rearrange("p (u e) -> p u e", u=POOL_PAGES),
             v_words.rearrange("u p e r -> p u (e r)").bitcast(I32),
         )
-
-        kb_rows = sbuf("kb_rows", [P, SLOTS], U32)
-        nc.vector.tensor_copy(dealt(kb_rows[:]), kb_pool[:].bitcast(U32).indirect(slots[:]))
-        kb_cols = [columns("kb_cols%d" % u, kb_rows[:, u * PAGE : (u + 1) * PAGE]) for u in range(PAGES)]
-
-        ks = sbuf("ks", [P, SLOTS], U8)
-        nc.vector.tensor_copy(
-            ks[:].rearrange("p (u r s) -> p r u s", r=PACK, s=P),
-            ks_listed.rearrange("p (u s r) -> p r u s", r=PACK, s=P),
-        )
-        vsc_pool = placed(after_deal, "vsc_pool", [P, POOL_PAGES * DV // 4], I32, 0)
+        vsc_pool = placed(after_ks, "vsc_pool", [P, POOL_PAGES * DV // 4], I32, vw_bytes)
         nc.gpsimd.memset(vsc_pool[:], 0)
         for j in range(4):
             nc.sync.dma_start(
@@ -126,34 +114,41 @@ def tile_attend_pkv8q_silu_kb_kernel(
             )
 
         silu = []
-        vs_cols = []
         for u in range(PAGES):
-            page = entries(slots, u * PAGE, PAGE)
-            kw = placed(after_deal, "kw%d" % u, [P, PAGE], U32, (1 + u) * page_bytes)
-            nc.vector.tensor_copy(dealt(kw[:]), kw_pool[:].bitcast(U32).indirect(page))
+            kw = sbuf("kw%d" % u, [P, PAGE], U32)
+            nc.vector.tensor_copy(kw[:], kw_pool[:].bitcast(U32).indirect(entries(slots, u * PAGE, PAGE)))
             scores = bank("score_bank", 3)
+            nc.tensor.matmul_mx(
+                scores[:].rearrange("q r s -> q (r s)"),
+                lhsT=qw[:].bitcast(FP8X4),
+                lhsT_scale=qs[:].bitcast(U8)[Q_PLANE:, :],
+                rhs=kw[:].bitcast(FP8X4),
+                rhs_scale=ks[K_PLANE:, u * PAGE : (u + 1) * PAGE],
+                start=True,
+                stop=True,
+            )
+            dealt = sbuf("dealt%d" % u, [NQ, PACK, P], F32)
+            nc.scalar.copy(dealt[:], scores[:].rearrange("q r s -> q (r s)").rearrange("q (s r) -> q r s", r=PACK))
+            by_slot = bank("by_slot_bank", 3)
             for r in range(PACK):
-                nc.tensor.matmul_mx(
-                    scores[:, r, :],
-                    lhsT=kw[:, r * P : (r + 1) * P].bitcast(FP8X4),
-                    lhsT_scale=ks[K_PLANE:, u * PAGE + r * P : u * PAGE + (r + 1) * P],
-                    rhs=qw[:].bitcast(FP8X4),
-                    rhs_scale=qs[:].bitcast(U8)[Q_PLANE:, :],
-                    start=True,
-                    stop=True,
-                )
+                nc.tensor.transpose(by_slot[:, r, :], dealt[:, r, :], ident[:])
             p = sbuf("p%d" % u, [P, PACK, NQ], F32)
             for r in range(PACK):
-                nc.scalar.activation(p[:, r, :], scores[:, r, :], ACT.Silu, bias=kb_cols[u][:, r : r + 1])
+                nc.scalar.activation(p[:, r, :], by_slot[:, r, :], ACT.Silu, bias=kb_cols[u][:, r : r + 1])
             silu.append(p)
-            vs_rows = placed(after_deal, "vs_rows%d" % u, [P, PAGE], U32, (1 + PAGES + u) * page_bytes)
-            nc.vector.tensor_copy(dealt(vs_rows[:]), vs_pool[:].bitcast(U32).indirect(page))
-            vs_cols.append(columns("vs_cols%d" % u, vs_rows[:]))
+
+        vs_cols = []
+        for u in range(PAGES):
+            vs_row = sbuf("vs_row%d" % u, [P, PAGE], F32)
+            nc.vector.tensor_copy(vs_row[:], vs_pool[:].indirect(entries(slots, u * PAGE, PAGE)))
+            cols = sbuf("vs_cols%d" % u, [P, PACK], F32)
+            nc.sync.dma_start(cols[:], vs_row[LIVE:, :])
+            vs_cols.append(cols)
 
         vsc = sbuf("vsc", [P, PAGES * DV], U8)
         nc.vector.tensor_copy(vsc[:], vsc_pool[:].bitcast(U8).indirect(vcols[:]))
 
-        acc = [bank("acc%d" % side, 1) for side in range(2)]
+        acc = [bank("kb_then_acc_bank", 2) for side in range(2)]
         for u in range(PAGES):
             w = sbuf("w%d" % u, [P, NQ, PACK], BF16)
             nc.vector.tensor_tensor(

@@ -15,7 +15,7 @@ LIST_ROWS = 16
 LIVE = P - 1
 K_PLANE, V_PLANE, Q_PLANE = 0, 4, 8
 QUAD = 32
-VS_SPLIT = 768
+FILL = 8
 
 FLOPS = 2 * NQ * SLOTS * (512 + DV)
 
@@ -58,6 +58,10 @@ def tile_attend_pkv8q_silu_kb_kernel(
         nc.sync.dma_start(vcols[:], voffs)
         kb_pool = sbuf("kb_pool", [P, POOL_TOKENS], F32)
         nc.sync.dma_start(kb_pool[LIVE:, :], kb[0:1, :])
+        vs_head = sbuf("vs_head", [P, FILL], F32)
+        nc.sync.dma_start(vs_head[:], vs[:, :FILL])
+        vs_pool = sbuf("vs_pool", [P, POOL_TOKENS], F32)
+        nc.sync.dma_start(vs_pool[LIVE:, :], vs[0:1, :])
 
         vw_bytes = 4 * POOL_PAGES * DV
         ks_pool = placed(after_ks, "ks_pool", [P, POOL_TOKENS // 4], I32, vw_bytes - 1024)
@@ -80,12 +84,13 @@ def tile_attend_pkv8q_silu_kb_kernel(
         qs = sbuf("qs", [P, NQ // 4], I32)
         nc.vector.memset(qs[:], 0)
         for j in range(4):
-            nc.scalar.dma_start(qs[Q_PLANE + j : P : QUAD, :], q_scales[0, 0, j::4, :].bitcast(I32))
+            nc.sync.dma_start(qs[Q_PLANE + j : P : QUAD, :], q_scales[0, 0, j::4, :].bitcast(I32))
         nc.vector.memset(kb_pool[:LIVE, :], 0.0)
-        vs_pool = sbuf("vs_pool", [P, POOL_TOKENS], F32)
-        nc.vector.memset(vs_pool[:, :VS_SPLIT], 0.0)
-        nc.gpsimd.memset(vs_pool[:LIVE, VS_SPLIT - 8 :], 0.0)
-        nc.scalar.dma_start(vs_pool[LIVE:, :], vs[0:1, :])
+        nc.scalar.activation(
+            vs_pool[:LIVE, :].rearrange("p (a b) -> p a b", b=FILL),
+            vs_head[:LIVE, :].unsqueeze(1).broadcast_to([LIVE, POOL_TOKENS // FILL, FILL]),
+            ACT.Copy,
+        )
 
         kb_cols = []
         for u in range(PAGES):
@@ -106,7 +111,7 @@ def tile_attend_pkv8q_silu_kb_kernel(
             v_words.rearrange("u p e r -> p u (e r)").bitcast(I32),
         )
         vsc_pool = placed(after_ks, "vsc_pool", [P, POOL_PAGES * DV // 4], I32, vw_bytes)
-        nc.gpsimd.memset(vsc_pool[:], 0)
+        nc.vector.memset(vsc_pool[:], 0)
         for j in range(4):
             nc.sync.dma_start(
                 vsc_pool[V_PLANE + j : P : QUAD, :].rearrange("p (u e) -> p u e", u=POOL_PAGES),

@@ -16,6 +16,7 @@ LIVE = P - 1
 K_PLANE, V_PLANE, Q_PLANE = 0, 4, 8
 QUAD = 32
 FILL = 8
+LINE = 4
 
 FLOPS = 2 * NQ * SLOTS * (512 + DV)
 
@@ -157,9 +158,9 @@ def tile_attend_pkv8q_silu_kb_kernel(
         for u in range(PAGES):
             w = sbuf("w%d" % u, [P, NQ, PACK], BF16)
             nc.vector.tensor_tensor(
-                w[:],
-                silu[u][:].rearrange("p r q -> p q r"),
-                vs_cols[u][:].unsqueeze(1).broadcast_to([P, NQ, PACK]),
+                w[:].rearrange("p (c i) r -> p c r i", i=LINE),
+                silu[u][:].rearrange("p r (c i) -> p c r i", i=LINE),
+                vs_cols[u][:].unsqueeze(1).unsqueeze(3).broadcast_to([P, NQ // LINE, PACK, LINE]),
                 ALU.mult,
             )
             vw = sbuf("vw%d" % u, [P, DV], U32)

@@ -38,6 +38,7 @@ def tile_attend_pkv8q_silu_kb_kernel(
     with ExitStack() as ctx:
         sb = ctx.enter_context(tc.tile_pool(name="sb", bufs=1))
         after_ramp = ctx.enter_context(tc.tile_pool(name="after_ramp", bufs=1))
+        reused = ctx.enter_context(tc.tile_pool(name="reused", bufs=1))
         after_ks = ctx.enter_context(tc.tile_pool(name="after_ks", bufs=1))
         ps = ctx.enter_context(tc.psum_pool(name="ps", bufs=1))
 
@@ -119,9 +120,10 @@ def tile_attend_pkv8q_silu_kb_kernel(
                 v_scales[:, j::4, :].rearrange("u f e -> f u e").bitcast(I32),
             )
 
+        page_bytes = 4 * PAGE
         silu = []
         for u in range(PAGES):
-            kw = sbuf("kw%d" % u, [P, PAGE], U32)
+            kw = placed(reused, "kw%d" % u, [P, PAGE], U32, page_bytes * u)
             nc.vector.tensor_copy(kw[:], kw_pool[:].bitcast(U32).indirect(entries(slots, u * PAGE, PAGE)))
             scores = bank("score_bank", 3)
             nc.tensor.matmul_mx(
@@ -133,8 +135,11 @@ def tile_attend_pkv8q_silu_kb_kernel(
                 start=True,
                 stop=True,
             )
-            dealt = sbuf("dealt%d" % u, [NQ, PACK, P], F32)
-            nc.scalar.copy(dealt[:], scores[:].rearrange("q r s -> q (r s)").rearrange("q (s r) -> q r s", r=PACK))
+            dealt = placed(reused, "dealt%d" % u, [NQ, PACK, P], F32, page_bytes * (PAGES + u))
+            nc.scalar.copy(
+                dealt[:].rearrange("q r s -> q s r"),
+                scores[:].rearrange("q a b -> q (a b)").rearrange("q (s r) -> q s r", r=PACK),
+            )
             by_slot = bank("by_slot_bank", 3)
             for r in range(PACK):
                 nc.tensor.transpose(by_slot[:, r, :], dealt[:, r, :], ident[:])
@@ -145,13 +150,16 @@ def tile_attend_pkv8q_silu_kb_kernel(
 
         vs_cols = []
         for u in range(PAGES):
-            vs_row = sbuf("vs_row%d" % u, [P, PAGE], F32)
+            if u < PAGES - 1:
+                vs_row = sbuf("vs_row%d" % u, [P, PAGE], F32)
+            else:
+                vs_row = placed(reused, "vs_row%d" % u, [P, PAGE], F32, 0)
             nc.vector.tensor_copy(vs_row[:], vs_pool[:].indirect(entries(slots, u * PAGE, PAGE)))
             cols = sbuf("vs_cols%d" % u, [P, PACK], F32)
             nc.sync.dma_start(cols[:], vs_row[LIVE:, :])
             vs_cols.append(cols)
 
-        vsc = sbuf("vsc", [P, PAGES * DV], U8)
+        vsc = placed(reused, "vsc", [P, PAGES * DV], U8, page_bytes * PAGES)
         nc.vector.tensor_copy(vsc[:], vsc_pool[:].bitcast(U8).indirect(vcols[:]))
 
         acc = [bank("kb_then_acc_bank", 2) for side in range(2)]
@@ -163,7 +171,7 @@ def tile_attend_pkv8q_silu_kb_kernel(
                 vs_cols[u][:].unsqueeze(1).unsqueeze(3).broadcast_to([P, NQ // LINE, PACK, LINE]),
                 ALU.mult,
             )
-            vw = sbuf("vw%d" % u, [P, DV], U32)
+            vw = placed(reused, "vw%d" % u, [P, DV], U32, page_bytes * PAGES + 4 * DV * (u + 1))
             nc.vector.tensor_copy(vw[:], vw_pool[:].bitcast(U32).indirect(entries(vcols, u * DV, DV)))
             w_codes = sbuf("w_codes%d" % u, [P, NQ], U32)
             w_scales = sbuf("w_scales%d" % u, [P, NQ], U8)

@@ -15,7 +15,7 @@ LIST_ROWS = 16
 LIVE = P - 1
 K_PLANE, V_PLANE, Q_PLANE = 0, 4, 8
 QUAD = 32
-FILL = 8
+FILL = 64
 LINE = 4
 
 FLOPS = 2 * NQ * SLOTS * (512 + DV)
@@ -64,6 +64,9 @@ def tile_attend_pkv8q_silu_kb_kernel(
         nc.sync.dma_start(vs_head[:], vs[:, :FILL])
         vs_pool = sbuf("vs_pool", [P, POOL_TOKENS], F32)
         nc.sync.dma_start(vs_pool[LIVE:, :], vs[0:1, :])
+        nc.vector.memset(vs_pool[:LIVE, :32], 0.0)
+        warm = sbuf("warm", [P, 32], F32)
+        nc.scalar.activation(warm[:LIVE, :], vs_pool[:LIVE, :32], ACT.Silu)
 
         vw_bytes = 4 * POOL_PAGES * DV
         ks_pool = placed(after_ks, "ks_pool", [P, POOL_TOKENS // 4], I32, vw_bytes - 1024)
@@ -75,8 +78,6 @@ def tile_attend_pkv8q_silu_kb_kernel(
         nc.gpsimd.iota(ramp[:], pattern=[[1, P]], base=0, channel_multiplier=-1)
         ident = sbuf("ident", [P, P], F32)
         nc.vector.tensor_scalar(ident[:], ramp[:], 0.0, None, ALU.is_equal)
-        warm = sbuf("warm", [P, 32], F32)
-        nc.scalar.activation(warm[:], ident[:, :32], ACT.Silu)
 
         kw_pool = placed(after_ramp, "kw_pool", [P, POOL_TOKENS], I32, 0)
         nc.sync.dma_start(kw_pool[:], k_words[0].rearrange("p n r -> p (n r)").bitcast(I32))
@@ -98,7 +99,7 @@ def tile_attend_pkv8q_silu_kb_kernel(
         for u in range(PAGES):
             kb_row = sbuf("kb_row%d" % u, [P, PAGE], F32)
             nc.vector.tensor_copy(kb_row[:], kb_pool[:].indirect(entries(slots, u * PAGE, PAGE)))
-            turned = bank("kb_then_acc_bank", 2)
+            turned = bank("kb_then_acc_bank", 3)
             for r in range(PACK):
                 nc.tensor.transpose(turned[:, r, :], kb_row[:, r::PACK], ident[:])
             cols = sbuf("kb_cols%d" % u, [P, PACK], F32)
@@ -125,7 +126,7 @@ def tile_attend_pkv8q_silu_kb_kernel(
         for u in range(PAGES):
             kw = placed(reused, "kw%d" % u, [P, PAGE], U32, page_bytes * u)
             nc.vector.tensor_copy(kw[:], kw_pool[:].bitcast(U32).indirect(entries(slots, u * PAGE, PAGE)))
-            scores = bank("score_bank", 3)
+            scores = bank("score_bank", 2)
             nc.tensor.matmul_mx(
                 scores[:].rearrange("q r s -> q (r s)"),
                 lhsT=qw[:].bitcast(FP8X4),
@@ -162,7 +163,7 @@ def tile_attend_pkv8q_silu_kb_kernel(
         vsc = placed(reused, "vsc", [P, PAGES * DV], U8, page_bytes * PAGES)
         nc.vector.tensor_copy(vsc[:], vsc_pool[:].bitcast(U8).indirect(vcols[:]))
 
-        acc = [bank("kb_then_acc_bank", 2) for side in range(2)]
+        acc = [bank("kb_then_acc_bank", 3) for side in range(2)]
         for u in range(PAGES):
             w = sbuf("w%d" % u, [P, NQ, PACK], BF16)
             nc.vector.tensor_tensor(

@@ -1,6 +1,7 @@
 from contextlib import ExitStack
 
 import concourse.mybir as mybir
+from concourse.masks import make_identity
 
 P = 128
 PACK = 4
@@ -15,7 +16,7 @@ LIST_ROWS = 16
 LIVE = P - 1
 K_PLANE, V_PLANE, Q_PLANE = 0, 4, 8
 QUAD = 32
-FILL = 64
+FILL = 8
 LINE = 4
 
 FLOPS = 2 * NQ * SLOTS * (512 + DV)
@@ -37,9 +38,7 @@ def tile_attend_pkv8q_silu_kb_kernel(
     nc = tc.nc
     with ExitStack() as ctx:
         sb = ctx.enter_context(tc.tile_pool(name="sb", bufs=1))
-        after_ramp = ctx.enter_context(tc.tile_pool(name="after_ramp", bufs=1))
         reused = ctx.enter_context(tc.tile_pool(name="reused", bufs=1))
-        after_ks = ctx.enter_context(tc.tile_pool(name="after_ks", bufs=1))
         ps = ctx.enter_context(tc.psum_pool(name="ps", bufs=1))
 
         def sbuf(name, shape, dtype):
@@ -58,31 +57,28 @@ def tile_attend_pkv8q_silu_kb_kernel(
         vcols = sb.tile([P, PAGES * DV // LIST_ROWS], U16, name="vcols")
         nc.sync.dma_start(slots[:], offs)
         nc.sync.dma_start(vcols[:], voffs)
-        kb_pool = sbuf("kb_pool", [P, POOL_TOKENS], F32)
+        kb_pool = sb.tile([P, POOL_TOKENS], F32, name="kb_pool", tag="kb_then_vw", align_bytes=64)
         nc.sync.dma_start(kb_pool[LIVE:, :], kb[0:1, :])
         vs_head = sbuf("vs_head", [P, FILL], F32)
         nc.sync.dma_start(vs_head[:], vs[:, :FILL])
         vs_pool = sbuf("vs_pool", [P, POOL_TOKENS], F32)
         nc.sync.dma_start(vs_pool[LIVE:, :], vs[0:1, :])
+        qw = sbuf("qw", [P, NQ], I32)
+        nc.sync.dma_start(qw[:], q_words[0, 0].rearrange("p n r -> p (n r)").bitcast(I32))
+        kw_pool = sbuf("kw_pool", [P, POOL_TOKENS], I32)
+        nc.sync.dma_start(kw_pool[:], k_words[0].rearrange("p n r -> p (n r)").bitcast(I32))
+
         nc.vector.memset(vs_pool[:LIVE, :32], 0.0)
         warm = sbuf("warm", [P, 32], F32)
         nc.scalar.activation(warm[:LIVE, :], vs_pool[:LIVE, :32], ACT.Silu)
 
-        vw_bytes = 4 * POOL_PAGES * DV
-        ks_pool = placed(after_ks, "ks_pool", [P, POOL_TOKENS // 4], I32, vw_bytes - 1024)
+        ks_pool = sb.tile([P, POOL_TOKENS // 4], I32, name="ks_pool", tag="ks_then_vsc", align_bytes=64)
         nc.vector.memset(ks_pool[:], 0)
         for j in range(4):
-            nc.sync.dma_start(ks_pool[K_PLANE + j : P : QUAD, :], k_scales[0, j::4, :].bitcast(I32))
+            nc.scalar.dma_start(ks_pool[K_PLANE + j : P : QUAD, :], k_scales[0, j::4, :].bitcast(I32))
 
-        ramp = placed(after_ramp, "ramp", [P, P], I32, 4 * POOL_TOKENS - 256)
-        nc.gpsimd.iota(ramp[:], pattern=[[1, P]], base=0, channel_multiplier=-1)
         ident = sbuf("ident", [P, P], F32)
-        nc.vector.tensor_scalar(ident[:], ramp[:], 0.0, None, ALU.is_equal)
-
-        kw_pool = placed(after_ramp, "kw_pool", [P, POOL_TOKENS], I32, 0)
-        nc.sync.dma_start(kw_pool[:], k_words[0].rearrange("p n r -> p (n r)").bitcast(I32))
-        qw = placed(after_ramp, "qw", [P, NQ], I32, 4 * POOL_TOKENS)
-        nc.sync.dma_start(qw[:], q_words[0, 0].rearrange("p n r -> p (n r)").bitcast(I32))
+        make_identity(nc, ident[:])
 
         qs = sbuf("qs", [P, NQ // 4], I32)
         nc.vector.memset(qs[:], 0)
@@ -95,38 +91,42 @@ def tile_attend_pkv8q_silu_kb_kernel(
             ACT.Copy,
         )
 
-        kb_cols = []
-        for u in range(PAGES):
-            kb_row = sbuf("kb_row%d" % u, [P, PAGE], F32)
-            nc.vector.tensor_copy(kb_row[:], kb_pool[:].indirect(entries(slots, u * PAGE, PAGE)))
-            turned = bank("kb_then_acc_bank", 3)
-            for r in range(PACK):
-                nc.tensor.transpose(turned[:, r, :], kb_row[:, r::PACK], ident[:])
-            cols = sbuf("kb_cols%d" % u, [P, PACK], F32)
-            nc.scalar.copy(cols[:], turned[:, :, LIVE])
-            kb_cols.append(cols)
+        def columns(name, queue, row):
+            cols = sbuf(name, [P, PACK], F32)
+            queue.dma_start(cols[:], row)
+            return cols
 
-        ks = sbuf("ks", [P, SLOTS], U8)
-        nc.vector.tensor_copy(ks[:], ks_pool[:].bitcast(U8).indirect(slots[:]))
-        vw_pool = placed(after_ks, "vw_pool", [P, POOL_PAGES * DV], I32, 0)
+        kb_rows = sbuf("kb_rows", [P, SLOTS], F32)
+        nc.vector.tensor_copy(kb_rows[:], kb_pool[:].indirect(slots[:]))
+        vw_pool = sb.tile([P, POOL_PAGES * DV], I32, name="vw_pool", tag="kb_then_vw", align_bytes=64)
         nc.sync.dma_start(
             vw_pool[:].rearrange("p (u e) -> p u e", u=POOL_PAGES),
             v_words.rearrange("u p e r -> p u (e r)").bitcast(I32),
         )
-        vsc_pool = placed(after_ks, "vsc_pool", [P, POOL_PAGES * DV // 4], I32, vw_bytes)
-        nc.vector.memset(vsc_pool[:], 0)
+        kb_cols = [
+            columns("kb_cols%d" % u, nc.scalar, kb_rows[LIVE:, u * PAGE : (u + 1) * PAGE]) for u in range(PAGES)
+        ]
+
+        ks = sbuf("ks", [P, SLOTS], U8)
+        nc.vector.tensor_copy(ks[:], ks_pool[:].bitcast(U8).indirect(slots[:]))
+        vsc_pool = sb.tile([P, POOL_PAGES * DV // 4], I32, name="vsc_pool", tag="ks_then_vsc", align_bytes=64)
+        nc.gpsimd.memset(vsc_pool[:], 0)
         for j in range(4):
             nc.sync.dma_start(
                 vsc_pool[V_PLANE + j : P : QUAD, :].rearrange("p (u e) -> p u e", u=POOL_PAGES),
                 v_scales[:, j::4, :].rearrange("u f e -> f u e").bitcast(I32),
             )
 
+        vs_first = sbuf("vs_first", [P, PAGE], F32)
+        nc.vector.tensor_copy(vs_first[:], vs_pool[:].indirect(entries(slots, 0, PAGE)))
+        vs_cols = [columns("vs_cols0", nc.sync, vs_first[LIVE:, :])]
+
         page_bytes = 4 * PAGE
         silu = []
         for u in range(PAGES):
-            kw = placed(reused, "kw%d" % u, [P, PAGE], U32, page_bytes * u)
+            kw = placed(reused, "kw%d" % u, [P, PAGE], U32, page_bytes * (1 + u))
             nc.vector.tensor_copy(kw[:], kw_pool[:].bitcast(U32).indirect(entries(slots, u * PAGE, PAGE)))
-            scores = bank("score_bank", 2)
+            scores = bank("score_bank", 3)
             nc.tensor.matmul_mx(
                 scores[:].rearrange("q r s -> q (r s)"),
                 lhsT=qw[:].bitcast(FP8X4),
@@ -136,7 +136,7 @@ def tile_attend_pkv8q_silu_kb_kernel(
                 start=True,
                 stop=True,
             )
-            dealt = placed(reused, "dealt%d" % u, [NQ, PACK, P], F32, page_bytes * (PAGES + u))
+            dealt = placed(reused, "dealt%d" % u, [NQ, PACK, P], F32, page_bytes * (2 + PAGES + u))
             nc.scalar.copy(
                 dealt[:].rearrange("q r s -> q s r"),
                 scores[:].rearrange("q a b -> q (a b)").rearrange("q (s r) -> q s r", r=PACK),
@@ -149,21 +149,17 @@ def tile_attend_pkv8q_silu_kb_kernel(
                 nc.scalar.activation(p[:, r, :], by_slot[:, r, :], ACT.Silu, bias=kb_cols[u][:, r : r + 1])
             silu.append(p)
 
-        vs_cols = []
-        for u in range(PAGES):
-            if u < PAGES - 1:
-                vs_row = sbuf("vs_row%d" % u, [P, PAGE], F32)
-            else:
-                vs_row = placed(reused, "vs_row%d" % u, [P, PAGE], F32, 0)
-            nc.vector.tensor_copy(vs_row[:], vs_pool[:].indirect(entries(slots, u * PAGE, PAGE)))
-            cols = sbuf("vs_cols%d" % u, [P, PACK], F32)
-            nc.sync.dma_start(cols[:], vs_row[LIVE:, :])
-            vs_cols.append(cols)
+        vs_rest = placed(reused, "vs_rest", [P, SLOTS - PAGE], F32, 0)
+        nc.vector.tensor_copy(vs_rest[:], vs_pool[:].indirect(entries(slots, PAGE, SLOTS - PAGE)))
+        for u in range(1, PAGES):
+            vs_cols.append(columns("vs_cols%d" % u, nc.sync, vs_rest[LIVE:, (u - 1) * PAGE : u * PAGE]))
 
-        vsc = placed(reused, "vsc", [P, PAGES * DV], U8, page_bytes * PAGES)
+        vw = placed(reused, "vw", [P, PAGES * DV], U32, page_bytes * (1 + PAGES))
+        nc.vector.tensor_copy(vw[:], vw_pool[:].bitcast(U32).indirect(vcols[:]))
+        vsc = placed(reused, "vsc", [P, PAGES * DV], U8, page_bytes * (1 + PAGES) + 4 * PAGES * DV)
         nc.vector.tensor_copy(vsc[:], vsc_pool[:].bitcast(U8).indirect(vcols[:]))
 
-        acc = [bank("kb_then_acc_bank", 3) for side in range(2)]
+        acc = [bank("acc_bank", 2) for side in range(2)]
         for u in range(PAGES):
             w = sbuf("w%d" % u, [P, NQ, PACK], BF16)
             nc.vector.tensor_tensor(
@@ -172,8 +168,6 @@ def tile_attend_pkv8q_silu_kb_kernel(
                 vs_cols[u][:].unsqueeze(1).unsqueeze(3).broadcast_to([P, NQ // LINE, PACK, LINE]),
                 ALU.mult,
             )
-            vw = placed(reused, "vw%d" % u, [P, DV], U32, page_bytes * PAGES + 4 * DV * (u + 1))
-            nc.vector.tensor_copy(vw[:], vw_pool[:].bitcast(U32).indirect(entries(vcols, u * DV, DV)))
             w_codes = sbuf("w_codes%d" % u, [P, NQ], U32)
             w_scales = sbuf("w_scales%d" % u, [P, NQ], U8)
             nc.vector.quantize_mx(
@@ -184,7 +178,7 @@ def tile_attend_pkv8q_silu_kb_kernel(
                     acc[side][:, 0, :],
                     lhsT=w_codes[:].bitcast(FP8X4),
                     lhsT_scale=w_scales[:],
-                    rhs=vw[:, side * P : (side + 1) * P].bitcast(FP8X4),
+                    rhs=vw[:, u * DV + side * P : u * DV + (side + 1) * P].bitcast(FP8X4),
                     rhs_scale=vsc[V_PLANE:, u * DV + side * P : u * DV + (side + 1) * P],
                     start=(u == 0),
                     stop=(u == PAGES - 1),

@@ -17,6 +17,7 @@ LIVE = P - 1
 K_PLANE, V_PLANE, Q_PLANE = 0, 4, 8
 QUAD = 32
 FILL = 8
+ZEROED = 32
 LINE = 4
 
 FLOPS = 2 * NQ * SLOTS * (512 + DV)
@@ -68,9 +69,9 @@ def tile_attend_pkv8q_silu_kb_kernel(
         kw_pool = sbuf("kw_pool", [P, POOL_TOKENS], I32)
         nc.sync.dma_start(kw_pool[:], k_words[0].rearrange("p n r -> p (n r)").bitcast(I32))
 
-        nc.vector.memset(vs_pool[:LIVE, :32], 0.0)
-        warm = sbuf("warm", [P, 32], F32)
-        nc.scalar.activation(warm[:LIVE, :], vs_pool[:LIVE, :32], ACT.Silu)
+        nc.vector.memset(vs_pool[:LIVE, :ZEROED], 0.0)
+        warm = sbuf("warm", [P, ZEROED], F32)
+        nc.scalar.activation(warm[:LIVE, :], vs_pool[:LIVE, :ZEROED], ACT.Silu)
 
         ks_pool = sb.tile([P, POOL_TOKENS // 4], I32, name="ks_pool", tag="ks_then_vsc", align_bytes=64)
         nc.vector.memset(ks_pool[:], 0)
@@ -83,11 +84,12 @@ def tile_attend_pkv8q_silu_kb_kernel(
         qs = sbuf("qs", [P, NQ // 4], I32)
         nc.vector.memset(qs[:], 0)
         for j in range(4):
-            nc.sync.dma_start(qs[Q_PLANE + j : P : QUAD, :], q_scales[0, 0, j::4, :].bitcast(I32))
+            queue = nc.sync if j < 3 else nc.gpsimd
+            queue.dma_start(qs[Q_PLANE + j : P : QUAD, :], q_scales[0, 0, j::4, :].bitcast(I32))
         nc.vector.memset(kb_pool[:LIVE, :], 0.0)
         nc.scalar.activation(
-            vs_pool[:LIVE, :].rearrange("p (a b) -> p a b", b=FILL),
-            vs_head[:LIVE, :].unsqueeze(1).broadcast_to([LIVE, POOL_TOKENS // FILL, FILL]),
+            vs_pool[:LIVE, ZEROED - FILL :].rearrange("p (a b) -> p a b", b=FILL),
+            vs_head[:LIVE, :].unsqueeze(1).broadcast_to([LIVE, (POOL_TOKENS - ZEROED) // FILL + 1, FILL]),
             ACT.Copy,
         )
 
@@ -117,14 +119,10 @@ def tile_attend_pkv8q_silu_kb_kernel(
                 v_scales[:, j::4, :].rearrange("u f e -> f u e").bitcast(I32),
             )
 
-        vs_first = sbuf("vs_first", [P, PAGE], F32)
-        nc.vector.tensor_copy(vs_first[:], vs_pool[:].indirect(entries(slots, 0, PAGE)))
-        vs_cols = [columns("vs_cols0", nc.sync, vs_first[LIVE:, :])]
-
         page_bytes = 4 * PAGE
         silu = []
         for u in range(PAGES):
-            kw = placed(reused, "kw%d" % u, [P, PAGE], U32, page_bytes * (1 + u))
+            kw = placed(reused, "kw%d" % u, [P, PAGE], U32, page_bytes * u)
             nc.vector.tensor_copy(kw[:], kw_pool[:].bitcast(U32).indirect(entries(slots, u * PAGE, PAGE)))
             scores = bank("score_bank", 3)
             nc.tensor.matmul_mx(
@@ -136,7 +134,7 @@ def tile_attend_pkv8q_silu_kb_kernel(
                 start=True,
                 stop=True,
             )
-            dealt = placed(reused, "dealt%d" % u, [NQ, PACK, P], F32, page_bytes * (2 + PAGES + u))
+            dealt = placed(reused, "dealt%d" % u, [NQ, PACK, P], F32, page_bytes * (1 + PAGES + u))
             nc.scalar.copy(
                 dealt[:].rearrange("q r s -> q s r"),
                 scores[:].rearrange("q a b -> q (a b)").rearrange("q (s r) -> q s r", r=PACK),
@@ -149,14 +147,15 @@ def tile_attend_pkv8q_silu_kb_kernel(
                 nc.scalar.activation(p[:, r, :], by_slot[:, r, :], ACT.Silu, bias=kb_cols[u][:, r : r + 1])
             silu.append(p)
 
-        vs_rest = placed(reused, "vs_rest", [P, SLOTS - PAGE], F32, 0)
-        nc.vector.tensor_copy(vs_rest[:], vs_pool[:].indirect(entries(slots, PAGE, SLOTS - PAGE)))
-        for u in range(1, PAGES):
-            vs_cols.append(columns("vs_cols%d" % u, nc.sync, vs_rest[LIVE:, (u - 1) * PAGE : u * PAGE]))
+        vs_cols = []
+        for u in range(PAGES):
+            vs_row = placed(reused, "vs_row%d" % u, [P, PAGE], F32, page_bytes * u)
+            nc.vector.tensor_copy(vs_row[:], vs_pool[:].indirect(entries(slots, u * PAGE, PAGE)))
+            vs_cols.append(columns("vs_cols%d" % u, nc.sync, vs_row[LIVE:, :]))
 
-        vw = placed(reused, "vw", [P, PAGES * DV], U32, page_bytes * (1 + PAGES))
+        vw = placed(reused, "vw", [P, PAGES * DV], U32, page_bytes * PAGES)
         nc.vector.tensor_copy(vw[:], vw_pool[:].bitcast(U32).indirect(vcols[:]))
-        vsc = placed(reused, "vsc", [P, PAGES * DV], U8, page_bytes * (1 + PAGES) + 4 * PAGES * DV)
+        vsc = placed(reused, "vsc", [P, PAGES * DV], U8, page_bytes * PAGES + 4 * PAGES * DV)
         nc.vector.tensor_copy(vsc[:], vsc_pool[:].bitcast(U8).indirect(vcols[:]))
 
         acc = [bank("acc_bank", 2) for side in range(2)]

@@ -1,7 +1,6 @@
 from contextlib import ExitStack
 
 import concourse.mybir as mybir
-from concourse.masks import make_identity
 
 P = 128
 PACK = 4
@@ -13,11 +12,15 @@ POOL_PAGES = POOL_TOKENS // PAGE
 DV = 256
 NQ = 128
 LIST_ROWS = 16
+SCALE_ROWS = 16
 LIVE = P - 1
-K_PLANE, V_PLANE, Q_PLANE = 0, 4, 8
 QUAD = 32
+QUADS = P // QUAD
+V_PLANE = 4
 FILL = 8
 ZEROED = 32
+POOL_SHARE = 1664
+EARLY_FILL = 768
 LINE = 4
 
 FLOPS = 2 * NQ * SLOTS * (512 + DV)
@@ -42,124 +45,137 @@ def tile_attend_pkv8q_silu_kb_kernel(
         reused = ctx.enter_context(tc.tile_pool(name="reused", bufs=1))
         ps = ctx.enter_context(tc.psum_pool(name="ps", bufs=1))
 
-        def sbuf(name, shape, dtype):
-            return sb.tile(shape, dtype, name=name, align_bytes=64)
-
-        def placed(pool, name, shape, dtype, offset):
-            return pool.tile(shape, dtype, name=name, offset=offset, align_bytes=64)
+        def sbuf(name, shape, dtype, tag=None):
+            return sb.tile(shape, dtype, name=name, tag=tag or name, align_bytes=64)
 
         def entries(list_tile, first, count):
             return list_tile[:, first // LIST_ROWS : (first + count) // LIST_ROWS]
 
-        def bank(tag, bufs):
-            return ps.tile([P, PACK, P], F32, name=tag, tag=tag, bufs=bufs)
+        def fill(dst, src):
+            cols = dst.shape[1]
+            nc.scalar.activation(
+                dst.rearrange("p (a b) -> p a b", b=FILL),
+                src.unsqueeze(1).broadcast_to([LIVE, cols // FILL, FILL]),
+                ACT.Copy,
+            )
 
         slots = sb.tile([P, SLOTS // LIST_ROWS], U16, name="slots")
-        vcols = sb.tile([P, PAGES * DV // LIST_ROWS], U16, name="vcols")
         nc.sync.dma_start(slots[:], offs)
-        nc.sync.dma_start(vcols[:], voffs)
-        kb_pool = sb.tile([P, POOL_TOKENS], F32, name="kb_pool", tag="kb_then_vw", align_bytes=64)
+        kb_pool = sbuf("kb_pool", [P, POOL_TOKENS], F32, "kb_then_vw")
         nc.sync.dma_start(kb_pool[LIVE:, :], kb[0:1, :])
-        vs_head = sbuf("vs_head", [P, FILL], F32)
-        nc.sync.dma_start(vs_head[:], vs[:, :FILL])
-        vs_pool = sbuf("vs_pool", [P, POOL_TOKENS], F32)
+        vcols = sb.tile([P, PAGES * DV // LIST_ROWS], U16, name="vcols")
+        nc.sync.dma_start(vcols[:], voffs)
+        vs_pool = sbuf("vs_pool", [P, POOL_TOKENS], F32, "vs_then_vplane")
         nc.sync.dma_start(vs_pool[LIVE:, :], vs[0:1, :])
+        vs_head = sbuf("vs_head", [P, FILL], F32, "head_then_kb_rows")
+        nc.sync.dma_start(vs_head[:], vs[:, :FILL])
+        kq_plane = sbuf("kq_plane", [P, (SLOTS + NQ) // 4], I32)
+        nc.gpsimd.dma_start(
+            kq_plane[:, SLOTS // 4 :],
+            q_scales[0, 0].bitcast(I32).unsqueeze(0).broadcast_to([P // SCALE_ROWS, SCALE_ROWS, NQ // 4]),
+        )
         qw = sbuf("qw", [P, NQ], I32)
         nc.sync.dma_start(qw[:], q_words[0, 0].rearrange("p n r -> p (n r)").bitcast(I32))
         kw_pool = sbuf("kw_pool", [P, POOL_TOKENS], I32)
         nc.sync.dma_start(kw_pool[:], k_words[0].rearrange("p n r -> p (n r)").bitcast(I32))
 
+        ks_pool = sbuf("ks_pool", [P, POOL_TOKENS // 4], I32)
+        nc.vector.memset(ks_pool[:], 0)
+        nc.scalar.dma_start(ks_pool[:SCALE_ROWS, :], k_scales[0].bitcast(I32))
         nc.vector.memset(vs_pool[:LIVE, :ZEROED], 0.0)
         warm = sbuf("warm", [P, ZEROED], F32)
         nc.scalar.activation(warm[:LIVE, :], vs_pool[:LIVE, :ZEROED], ACT.Silu)
-
-        ks_pool = sb.tile([P, POOL_TOKENS // 4], I32, name="ks_pool", tag="ks_then_vsc", align_bytes=64)
-        nc.vector.memset(ks_pool[:], 0)
-        for j in range(4):
-            nc.scalar.dma_start(ks_pool[K_PLANE + j : P : QUAD, :], k_scales[0, j::4, :].bitcast(I32))
-
-        ident = sbuf("ident", [P, P], F32)
-        make_identity(nc, ident[:])
-
-        qs = sbuf("qs", [P, NQ // 4], I32)
-        nc.vector.memset(qs[:], 0)
-        for j in range(4):
-            queue = nc.sync if j < 3 else nc.gpsimd
-            queue.dma_start(qs[Q_PLANE + j : P : QUAD, :], q_scales[0, 0, j::4, :].bitcast(I32))
-        nc.vector.memset(kb_pool[:LIVE, :], 0.0)
-        nc.scalar.activation(
-            vs_pool[:LIVE, ZEROED - FILL :].rearrange("p (a b) -> p a b", b=FILL),
-            vs_head[:LIVE, :].unsqueeze(1).broadcast_to([LIVE, (POOL_TOKENS - ZEROED) // FILL + 1, FILL]),
-            ACT.Copy,
+        vsc_pool = sbuf("vsc_pool", [P, POOL_PAGES * DV // 4], I32)
+        nc.vector.memset(vsc_pool[:], 0)
+        nc.scalar.dma_start(
+            vsc_pool[:SCALE_ROWS, :].rearrange("p (u e) -> p u e", u=POOL_PAGES),
+            v_scales.rearrange("u f e -> f u e").bitcast(I32),
         )
+        nc.vector.memset(kb_pool[:LIVE, :], 0.0)
 
-        def columns(name, queue, row):
-            cols = sbuf(name, [P, PACK], F32)
-            queue.dma_start(cols[:], row)
-            return cols
+        pool_end = ZEROED - FILL + POOL_SHARE
+        nc.gpsimd.memset(vs_pool[:LIVE, ZEROED - FILL : pool_end], 0.0)
+        kept_head = sbuf("kept_head", [P, FILL], F32)
+        nc.scalar.activation(kept_head[:LIVE, :], vs_head[:LIVE, :], ACT.Copy)
+        fill(vs_pool[:LIVE, POOL_TOKENS - EARLY_FILL :], vs_head[:LIVE, :])
 
-        kb_rows = sbuf("kb_rows", [P, SLOTS], F32)
-        nc.vector.tensor_copy(kb_rows[:], kb_pool[:].indirect(slots[:]))
-        vw_pool = sb.tile([P, POOL_PAGES * DV], I32, name="vw_pool", tag="kb_then_vw", align_bytes=64)
-        nc.sync.dma_start(
+        kb_rows = sbuf("kb_rows", [P, SLOTS], F32, "head_then_kb_rows")
+        nc.scalar.activation(kb_rows[:], kb_pool[:].indirect(slots[:]), ACT.Copy)
+        kb_cols = []
+        for u in range(PAGES):
+            cols = sbuf("kb_cols%d" % u, [P, PACK], F32)
+            queue = nc.sync if u == 0 else nc.gpsimd
+            queue.dma_start(cols[:], kb_rows[LIVE:, u * PAGE : (u + 1) * PAGE])
+            kb_cols.append(cols)
+        vw_pool = sbuf("vw_pool", [P, POOL_PAGES * DV], I32, "kb_then_vw")
+        nc.scalar.dma_start(
             vw_pool[:].rearrange("p (u e) -> p u e", u=POOL_PAGES),
             v_words.rearrange("u p e r -> p u (e r)").bitcast(I32),
         )
-        kb_cols = [
-            columns("kb_cols%d" % u, nc.scalar, kb_rows[LIVE:, u * PAGE : (u + 1) * PAGE]) for u in range(PAGES)
-        ]
+        fill(vs_pool[:LIVE, pool_end - FILL : POOL_TOKENS - EARLY_FILL], kept_head[:LIVE, :])
 
-        ks = sbuf("ks", [P, SLOTS], U8)
+        ks = reused.tile([P, SLOTS], U8, name="ks", offset=0, align_bytes=64)
         nc.vector.tensor_copy(ks[:], ks_pool[:].bitcast(U8).indirect(slots[:]))
-        vsc_pool = sb.tile([P, POOL_PAGES * DV // 4], I32, name="vsc_pool", tag="ks_then_vsc", align_bytes=64)
-        nc.gpsimd.memset(vsc_pool[:], 0)
-        for j in range(4):
+        kq_bytes = kq_plane[:].bitcast(U8)
+        nc.vector.tensor_copy(
+            kq_bytes[:, :SLOTS].rearrange("p (r n) -> p r n", r=PACK),
+            ks[:].rearrange("p (n r) -> p r n", r=PACK),
+        )
+        for quad in range(1, QUADS):
             nc.sync.dma_start(
-                vsc_pool[V_PLANE + j : P : QUAD, :].rearrange("p (u e) -> p u e", u=POOL_PAGES),
-                v_scales[:, j::4, :].rearrange("u f e -> f u e").bitcast(I32),
+                kq_plane[QUAD * quad : QUAD * quad + PACK, :], kq_plane[PACK * quad : PACK * (quad + 1), :]
             )
-
-        page_bytes = 4 * PAGE
-        silu = []
-        for u in range(PAGES):
-            kw = placed(reused, "kw%d" % u, [P, PAGE], U32, page_bytes * u)
-            nc.vector.tensor_copy(kw[:], kw_pool[:].bitcast(U32).indirect(entries(slots, u * PAGE, PAGE)))
-            scores = bank("score_bank", 3)
-            nc.tensor.matmul_mx(
-                scores[:].rearrange("q r s -> q (r s)"),
-                lhsT=qw[:].bitcast(FP8X4),
-                lhsT_scale=qs[:].bitcast(U8)[Q_PLANE:, :],
-                rhs=kw[:].bitcast(FP8X4),
-                rhs_scale=ks[K_PLANE:, u * PAGE : (u + 1) * PAGE],
-                start=True,
-                stop=True,
-            )
-            dealt = placed(reused, "dealt%d" % u, [NQ, PACK, P], F32, page_bytes * (1 + PAGES + u))
-            nc.scalar.copy(
-                dealt[:].rearrange("q r s -> q s r"),
-                scores[:].rearrange("q a b -> q (a b)").rearrange("q (s r) -> q s r", r=PACK),
-            )
-            by_slot = bank("by_slot_bank", 3)
-            for r in range(PACK):
-                nc.tensor.transpose(by_slot[:, r, :], dealt[:, r, :], ident[:])
-            p = sbuf("p%d" % u, [P, PACK, NQ], F32)
-            for r in range(PACK):
-                nc.scalar.activation(p[:, r, :], by_slot[:, r, :], ACT.Silu, bias=kb_cols[u][:, r : r + 1])
-            silu.append(p)
+        vsc = sbuf("vsc", [P, PAGES * DV], U8)
+        nc.vector.tensor_copy(vsc[:], vsc_pool[:].bitcast(U8).indirect(vcols[:]))
 
         vs_cols = []
         for u in range(PAGES):
-            vs_row = placed(reused, "vs_row%d" % u, [P, PAGE], F32, page_bytes * u)
-            nc.vector.tensor_copy(vs_row[:], vs_pool[:].indirect(entries(slots, u * PAGE, PAGE)))
-            vs_cols.append(columns("vs_cols%d" % u, nc.sync, vs_row[LIVE:, :]))
+            vs_row = sbuf("vs_row%d" % u, [P, PAGE], F32)
+            nc.scalar.activation(vs_row[:], vs_pool[:].indirect(entries(slots, u * PAGE, PAGE)), ACT.Copy)
+            cols = reused.tile([P, PACK], F32, name="vs_cols%d" % u, offset=64 * u, align_bytes=64)
+            nc.sync.dma_start(cols[:], vs_row[LIVE:, :])
+            vs_cols.append(cols)
 
-        vw = placed(reused, "vw", [P, PAGES * DV], U32, page_bytes * PAGES)
-        nc.vector.tensor_copy(vw[:], vw_pool[:].bitcast(U32).indirect(vcols[:]))
-        vsc = placed(reused, "vsc", [P, PAGES * DV], U8, page_bytes * PAGES + 4 * PAGES * DV)
-        nc.vector.tensor_copy(vsc[:], vsc_pool[:].bitcast(U8).indirect(vcols[:]))
+        v_plane = sbuf("v_plane", [P, PAGES * DV // 4], I32, "vs_then_vplane")
+        nc.gpsimd.memset(v_plane[:], 0)
+        for quad in range(QUADS):
+            first = QUAD * quad + V_PLANE
+            nc.sync.dma_start(v_plane[first : first + PACK, :], vsc[PACK * quad : PACK * (quad + 1), :].bitcast(I32))
 
-        acc = [bank("acc_bank", 2) for side in range(2)]
+        silu = []
         for u in range(PAGES):
+            kw = reused.tile([P, PAGE], U32, name="kw%d" % u, offset=4 * PAGE * (1 + 2 * u), align_bytes=64)
+            nc.vector.tensor_copy(
+                kw[:].rearrange("p (r s) -> p s r", r=PACK),
+                kw_pool[:].bitcast(U32).indirect(entries(slots, u * PAGE, PAGE)),
+            )
+            p = sbuf("p%d" % u, [P, PACK, NQ], F32)
+            for half in range(2):
+                scores = ps.tile([P, 2, NQ], F32, name="scores", tag="scores", bufs=2 * PAGES)
+                for i in range(2):
+                    r = 2 * half + i
+                    first = (r * PAGES + u) * P
+                    nc.tensor.matmul_mx(
+                        scores[:, i, :],
+                        lhsT=kw[:, r * P : (r + 1) * P].bitcast(FP8X4),
+                        lhsT_scale=kq_bytes[:, first : first + P],
+                        rhs=qw[:].bitcast(FP8X4),
+                        rhs_scale=kq_bytes[:, SLOTS:],
+                        start=True,
+                        stop=True,
+                    )
+                for i in range(2):
+                    r = 2 * half + i
+                    nc.scalar.activation(p[:, r, :], scores[:, i, :], ACT.Silu, bias=kb_cols[u][:, r : r + 1])
+            silu.append(p)
+
+        vw = reused.tile([P, PAGES * DV], U32, name="vw", offset=4 * PAGE, align_bytes=64)
+        nc.vector.tensor_copy(vw[:], vw_pool[:].bitcast(U32).indirect(vcols[:]))
+
+        acc = [ps.tile([NQ, P], F32, name="acc", tag="acc", bufs=2) for side in range(2)]
+        v_bytes = v_plane[:].bitcast(U8)
+
+        def weigh(u):
             w = sbuf("w%d" % u, [P, NQ, PACK], BF16)
             nc.vector.tensor_tensor(
                 w[:].rearrange("p (c i) r -> p c r i", i=LINE),
@@ -167,25 +183,35 @@ def tile_attend_pkv8q_silu_kb_kernel(
                 vs_cols[u][:].unsqueeze(1).unsqueeze(3).broadcast_to([P, NQ // LINE, PACK, LINE]),
                 ALU.mult,
             )
+            return w
+
+        def multiply(u, w):
             w_codes = sbuf("w_codes%d" % u, [P, NQ], U32)
             w_scales = sbuf("w_scales%d" % u, [P, NQ], U8)
             nc.vector.quantize_mx(
                 out=w_codes[:].bitcast(FP8X4), scales=w_scales[:], in_=w[:].rearrange("p q r -> p (q r)")
             )
             for side in range(2):
+                cols = slice(u * DV + side * P, u * DV + (side + 1) * P)
                 nc.tensor.matmul_mx(
-                    acc[side][:, 0, :],
+                    acc[side][:],
                     lhsT=w_codes[:].bitcast(FP8X4),
                     lhsT_scale=w_scales[:],
-                    rhs=vw[:, u * DV + side * P : u * DV + (side + 1) * P].bitcast(FP8X4),
-                    rhs_scale=vsc[V_PLANE:, u * DV + side * P : u * DV + (side + 1) * P],
+                    rhs=vw[:, cols].bitcast(FP8X4),
+                    rhs_scale=v_bytes[V_PLANE:, cols],
                     start=(u == 0),
                     stop=(u == PAGES - 1),
                 )
 
+        weights = [weigh(0)]
+        for u in range(PAGES):
+            if u + 1 < PAGES:
+                weights.append(weigh(u + 1))
+            multiply(u, weights[u])
+
         left = sbuf("left", [NQ, P], F32)
-        nc.vector.tensor_scalar_mul(left[:], acc[0][:, 0, :], 1.0 / 16.0)
+        nc.vector.tensor_scalar_mul(left[:], acc[0][:], 1.0 / 16.0)
         nc.sync.dma_start(out[0, :, :P], left[:])
         right = sbuf("right", [NQ, P], F32)
-        nc.scalar.activation(right[:], acc[1][:, 0, :], ACT.Copy, scale=1.0 / 16.0)
+        nc.scalar.activation(right[:], acc[1][:], ACT.Copy, scale=1.0 / 16.0)
         nc.scalar.dma_start(out[0, :, P:], right[:])

@@ -43,6 +43,7 @@ def tile_attend_pkv8q_silu_kb_kernel(
     with ExitStack() as ctx:
         sb = ctx.enter_context(tc.tile_pool(name="sb", bufs=1))
         reused = ctx.enter_context(tc.tile_pool(name="reused", bufs=1))
+        shared = ctx.enter_context(tc.tile_pool(name="shared", bufs=1))
         ps = ctx.enter_context(tc.psum_pool(name="ps", bufs=1))
 
         def sbuf(name, shape, dtype, tag=None):
@@ -61,7 +62,7 @@ def tile_attend_pkv8q_silu_kb_kernel(
 
         slots = sb.tile([P, SLOTS // LIST_ROWS], U16, name="slots")
         nc.sync.dma_start(slots[:], offs)
-        kb_pool = sbuf("kb_pool", [P, POOL_TOKENS], F32, "kb_then_vw")
+        kb_pool = shared.tile([P, POOL_TOKENS], F32, name="kb_pool", offset=0, align_bytes=64)
         nc.sync.dma_start(kb_pool[LIVE:, :], kb[0:1, :])
         vcols = sb.tile([P, PAGES * DV // LIST_ROWS], U16, name="vcols")
         nc.sync.dma_start(vcols[:], voffs)
@@ -107,12 +108,14 @@ def tile_attend_pkv8q_silu_kb_kernel(
             queue = nc.sync if u == 0 else nc.gpsimd
             queue.dma_start(cols[:], kb_rows[LIVE:, u * PAGE : (u + 1) * PAGE])
             kb_cols.append(cols)
-        vw_pool = sbuf("vw_pool", [P, POOL_PAGES * DV], I32, "kb_then_vw")
+        late_head = shared.tile([P, FILL], F32, name="late_head", offset=4 * POOL_PAGES * DV, align_bytes=64)
+        nc.scalar.activation(late_head[:LIVE, :], kept_head[:LIVE, :], ACT.Copy)
+        vw_pool = shared.tile([P, POOL_PAGES * DV], I32, name="vw_pool", offset=0, align_bytes=64)
         nc.scalar.dma_start(
             vw_pool[:].rearrange("p (u e) -> p u e", u=POOL_PAGES),
             v_words.rearrange("u p e r -> p u (e r)").bitcast(I32),
         )
-        fill(vs_pool[:LIVE, pool_end - FILL : POOL_TOKENS - EARLY_FILL], kept_head[:LIVE, :])
+        fill(vs_pool[:LIVE, pool_end - FILL : POOL_TOKENS - EARLY_FILL], late_head[:LIVE, :])
 
         ks = reused.tile([P, SLOTS], U8, name="ks", offset=0, align_bytes=64)
         nc.vector.tensor_copy(ks[:], ks_pool[:].bitcast(U8).indirect(slots[:]))

@@ -19,7 +19,6 @@ QUADS = P // QUAD
 V_PLANE = 4
 FILL = 8
 ZEROED = 32
-POOL_SHARE = 1664
 EARLY_FILL = 768
 LINE = 4
 
@@ -66,7 +65,7 @@ def tile_attend_pkv8q_silu_kb_kernel(
         nc.sync.dma_start(kb_pool[LIVE:, :], kb[0:1, :])
         vcols = sb.tile([P, PAGES * DV // LIST_ROWS], U16, name="vcols")
         nc.sync.dma_start(vcols[:], voffs)
-        vs_pool = sbuf("vs_pool", [P, POOL_TOKENS], F32, "vs_then_vplane")
+        vs_pool = shared.tile([P, POOL_TOKENS], F32, name="vs_pool", offset=4 * POOL_TOKENS, align_bytes=64)
         nc.sync.dma_start(vs_pool[LIVE:, :], vs[0:1, :])
         vs_head = sbuf("vs_head", [P, FILL], F32, "head_then_kb_rows")
         nc.sync.dma_start(vs_head[:], vs[:, :FILL])
@@ -94,8 +93,6 @@ def tile_attend_pkv8q_silu_kb_kernel(
         )
         nc.vector.memset(kb_pool[:LIVE, :], 0.0)
 
-        pool_end = ZEROED - FILL + POOL_SHARE
-        nc.gpsimd.memset(vs_pool[:LIVE, ZEROED - FILL : pool_end], 0.0)
         kept_head = sbuf("kept_head", [P, FILL], F32)
         nc.scalar.activation(kept_head[:LIVE, :], vs_head[:LIVE, :], ACT.Copy)
         fill(vs_pool[:LIVE, POOL_TOKENS - EARLY_FILL :], vs_head[:LIVE, :])
@@ -115,7 +112,7 @@ def tile_attend_pkv8q_silu_kb_kernel(
             vw_pool[:].rearrange("p (u e) -> p u e", u=POOL_PAGES),
             v_words.rearrange("u p e r -> p u (e r)").bitcast(I32),
         )
-        fill(vs_pool[:LIVE, pool_end - FILL : POOL_TOKENS - EARLY_FILL], late_head[:LIVE, :])
+        fill(vs_pool[:LIVE, ZEROED : POOL_TOKENS - EARLY_FILL], late_head[:LIVE, :])
 
         ks = reused.tile([P, SLOTS], U8, name="ks", offset=0, align_bytes=64)
         nc.vector.tensor_copy(ks[:], ks_pool[:].bitcast(U8).indirect(slots[:]))
@@ -139,7 +136,7 @@ def tile_attend_pkv8q_silu_kb_kernel(
             nc.sync.dma_start(cols[:], vs_row[LIVE:, :])
             vs_cols.append(cols)
 
-        v_plane = sbuf("v_plane", [P, PAGES * DV // 4], I32, "vs_then_vplane")
+        v_plane = shared.tile([P, PAGES * DV // 4], I32, name="v_plane", offset=4 * POOL_TOKENS, align_bytes=64)
         nc.gpsimd.memset(v_plane[:], 0)
         for quad in range(QUADS):
             first = QUAD * quad + V_PLANE
@@ -152,7 +149,9 @@ def tile_attend_pkv8q_silu_kb_kernel(
                 kw[:].rearrange("p (r s) -> p s r", r=PACK),
                 kw_pool[:].bitcast(U32).indirect(entries(slots, u * PAGE, PAGE)),
             )
-            p = sbuf("p%d" % u, [P, PACK, NQ], F32)
+            p = shared.tile(
+                [P, PACK, NQ], F32, name="p%d" % u, offset=4 * (POOL_TOKENS + (1 + u) * PAGE), align_bytes=64
+            )
             for half in range(2):
                 scores = ps.tile([P, 2, NQ], F32, name="scores", tag="scores", bufs=2 * PAGES)
                 for i in range(2):

@@ -19,7 +19,9 @@ QUADS = P // QUAD
 V_PLANE = 4
 FILL = 8
 ZEROED = 32
-EARLY_FILL = 768
+VECTOR_END = 1632
+EARLY_FILL = 512
+SHORT_FILL = 128
 LINE = 4
 
 FLOPS = 2 * NQ * SLOTS * (512 + DV)
@@ -59,51 +61,43 @@ def tile_attend_pkv8q_silu_kb_kernel(
                 ACT.Copy,
             )
 
+        vs_pool = shared.tile([P, POOL_TOKENS], F32, name="vs_pool", offset=4 * POOL_TOKENS, align_bytes=64)
+        nc.scalar.dma_start(vs_pool[LIVE:, :], vs[0:1, :])
         slots = sb.tile([P, SLOTS // LIST_ROWS], U16, name="slots")
         nc.sync.dma_start(slots[:], offs)
-        kb_pool = shared.tile([P, POOL_TOKENS], F32, name="kb_pool", offset=0, align_bytes=64)
-        nc.sync.dma_start(kb_pool[LIVE:, :], kb[0:1, :])
         vcols = sb.tile([P, PAGES * DV // LIST_ROWS], U16, name="vcols")
         nc.sync.dma_start(vcols[:], voffs)
-        vs_pool = shared.tile([P, POOL_TOKENS], F32, name="vs_pool", offset=4 * POOL_TOKENS, align_bytes=64)
-        nc.sync.dma_start(vs_pool[LIVE:, :], vs[0:1, :])
         vs_head = sbuf("vs_head", [P, FILL], F32, "head_then_kb_rows")
-        nc.sync.dma_start(vs_head[:], vs[:, :FILL])
+        nc.sync.dma_start(vs_head[:], vs[0].rearrange("(p f) -> p f", p=P)[:, :FILL])
+        qw = sbuf("qw", [P, NQ], I32)
+        nc.sync.dma_start(qw[:], q_words[0, 0].rearrange("p n r -> p (n r)").bitcast(I32))
+        kb_pool = shared.tile([P, POOL_TOKENS], F32, name="kb_pool", offset=0, align_bytes=64)
+        nc.sync.dma_start(kb_pool[LIVE:, :], kb[0:1, :])
         kq_plane = sbuf("kq_plane", [P, (SLOTS + NQ) // 4], I32)
         nc.gpsimd.dma_start(
             kq_plane[:, SLOTS // 4 :],
             q_scales[0, 0].bitcast(I32).unsqueeze(0).broadcast_to([P // SCALE_ROWS, SCALE_ROWS, NQ // 4]),
         )
-        qw = sbuf("qw", [P, NQ], I32)
-        nc.sync.dma_start(qw[:], q_words[0, 0].rearrange("p n r -> p (n r)").bitcast(I32))
-        kw_pool = sbuf("kw_pool", [P, POOL_TOKENS], I32)
-        nc.sync.dma_start(kw_pool[:], k_words[0].rearrange("p n r -> p (n r)").bitcast(I32))
 
-        ks_pool = sbuf("ks_pool", [P, POOL_TOKENS // 4], I32)
-        nc.vector.memset(ks_pool[:], 0)
-        nc.scalar.dma_start(ks_pool[:SCALE_ROWS, :], k_scales[0].bitcast(I32))
         nc.vector.memset(vs_pool[:LIVE, :ZEROED], 0.0)
         warm = sbuf("warm", [P, ZEROED], F32)
         nc.scalar.activation(warm[:LIVE, :], vs_pool[:LIVE, :ZEROED], ACT.Silu)
-        vsc_pool = sbuf("vsc_pool", [P, POOL_PAGES * DV // 4], I32)
-        nc.vector.memset(vsc_pool[:], 0)
-        nc.scalar.dma_start(
-            vsc_pool[:SCALE_ROWS, :].rearrange("p (u e) -> p u e", u=POOL_PAGES),
-            v_scales.rearrange("u f e -> f u e").bitcast(I32),
-        )
+        ks_pool = sbuf("ks_pool", [P, POOL_TOKENS // 4], I32)
+        nc.vector.memset(ks_pool[:], 0)
+        nc.sync.dma_start(ks_pool[:SCALE_ROWS, :], k_scales[0].bitcast(I32))
+        kw_pool = sbuf("kw_pool", [P, POOL_TOKENS], I32)
+        nc.sync.dma_start(kw_pool[:], k_words[0].rearrange("p n r -> p (n r)").bitcast(I32))
         nc.vector.memset(kb_pool[:LIVE, :], 0.0)
 
         kept_head = sbuf("kept_head", [P, FILL], F32)
         nc.scalar.activation(kept_head[:LIVE, :], vs_head[:LIVE, :], ACT.Copy)
         fill(vs_pool[:LIVE, POOL_TOKENS - EARLY_FILL :], vs_head[:LIVE, :])
-
         kb_rows = sbuf("kb_rows", [P, SLOTS], F32, "head_then_kb_rows")
         nc.scalar.activation(kb_rows[:], kb_pool[:].indirect(slots[:]), ACT.Copy)
         kb_cols = []
         for u in range(PAGES):
             cols = sbuf("kb_cols%d" % u, [P, PACK], F32)
-            queue = nc.sync if u == 0 else nc.gpsimd
-            queue.dma_start(cols[:], kb_rows[LIVE:, u * PAGE : (u + 1) * PAGE])
+            nc.gpsimd.dma_start(cols[:], kb_rows[LIVE:, u * PAGE : (u + 1) * PAGE])
             kb_cols.append(cols)
         late_head = shared.tile([P, FILL], F32, name="late_head", offset=4 * POOL_PAGES * DV, align_bytes=64)
         nc.scalar.activation(late_head[:LIVE, :], kept_head[:LIVE, :], ACT.Copy)
@@ -112,7 +106,8 @@ def tile_attend_pkv8q_silu_kb_kernel(
             vw_pool[:].rearrange("p (u e) -> p u e", u=POOL_PAGES),
             v_words.rearrange("u p e r -> p u (e r)").bitcast(I32),
         )
-        fill(vs_pool[:LIVE, ZEROED : POOL_TOKENS - EARLY_FILL], late_head[:LIVE, :])
+        fill(vs_pool[:LIVE, VECTOR_END - FILL : VECTOR_END + SHORT_FILL], late_head[:LIVE, :])
+        fill(vs_pool[:LIVE, VECTOR_END + SHORT_FILL : POOL_TOKENS - EARLY_FILL], late_head[:LIVE, :])
 
         ks = reused.tile([P, SLOTS], U8, name="ks", offset=0, align_bytes=64)
         nc.vector.tensor_copy(ks[:], ks_pool[:].bitcast(U8).indirect(slots[:]))
@@ -125,8 +120,15 @@ def tile_attend_pkv8q_silu_kb_kernel(
             nc.sync.dma_start(
                 kq_plane[QUAD * quad : QUAD * quad + PACK, :], kq_plane[PACK * quad : PACK * (quad + 1), :]
             )
-        vsc = sbuf("vsc", [P, PAGES * DV], U8)
-        nc.vector.tensor_copy(vsc[:], vsc_pool[:].bitcast(U8).indirect(vcols[:]))
+        nc.vector.memset(vs_pool[:LIVE, ZEROED:VECTOR_END], 0.0)
+        vsc_pool = sbuf("vsc_pool", [P, POOL_PAGES * DV // 4], I32)
+        nc.vector.memset(vsc_pool[:], 0)
+        nc.sync.dma_start(
+            vsc_pool[:SCALE_ROWS, :].rearrange("p (u e) -> p u e", u=POOL_PAGES),
+            v_scales.rearrange("u f e -> f u e").bitcast(I32),
+        )
+        v_plane = sbuf("v_plane", [P, PAGES * DV // 4], I32)
+        nc.vector.memset(v_plane[:], 0)
 
         vs_cols = []
         for u in range(PAGES):
@@ -135,12 +137,6 @@ def tile_attend_pkv8q_silu_kb_kernel(
             cols = reused.tile([P, PACK], F32, name="vs_cols%d" % u, offset=64 * u, align_bytes=64)
             nc.sync.dma_start(cols[:], vs_row[LIVE:, :])
             vs_cols.append(cols)
-
-        v_plane = shared.tile([P, PAGES * DV // 4], I32, name="v_plane", offset=4 * POOL_TOKENS, align_bytes=64)
-        nc.gpsimd.memset(v_plane[:], 0)
-        for quad in range(QUADS):
-            first = QUAD * quad + V_PLANE
-            nc.sync.dma_start(v_plane[first : first + PACK, :], vsc[PACK * quad : PACK * (quad + 1), :].bitcast(I32))
 
         silu = []
         for u in range(PAGES):
@@ -171,7 +167,12 @@ def tile_attend_pkv8q_silu_kb_kernel(
                     nc.scalar.activation(p[:, r, :], scores[:, i, :], ACT.Silu, bias=kb_cols[u][:, r : r + 1])
             silu.append(p)
 
-        vw = reused.tile([P, PAGES * DV], U32, name="vw", offset=4 * PAGE, align_bytes=64)
+        vsc = reused.tile([P, PAGES * DV], U8, name="vsc", offset=4 * PAGE, align_bytes=64)
+        nc.vector.tensor_copy(vsc[:], vsc_pool[:].bitcast(U8).indirect(vcols[:]))
+        for quad in range(QUADS):
+            first = QUAD * quad + V_PLANE
+            nc.sync.dma_start(v_plane[first : first + PACK, :], vsc[PACK * quad : PACK * (quad + 1), :].bitcast(I32))
+        vw = reused.tile([P, PAGES * DV], U32, name="vw", offset=4 * PAGE + PAGES * DV, align_bytes=64)
         nc.vector.tensor_copy(vw[:], vw_pool[:].bitcast(U32).indirect(vcols[:]))
 
         acc = [ps.tile([NQ, P], F32, name="acc", tag="acc", bufs=2) for side in range(2)]

@@ -19,7 +19,7 @@ QUADS = P // QUAD
 V_PLANE = 4
 FILL = 8
 ZEROED = 32
-VECTOR_END = 1632
+VECTOR_END = 1184
 EARLY_FILL = 512
 SHORT_FILL = 128
 LINE = 4
@@ -97,7 +97,8 @@ def tile_attend_pkv8q_silu_kb_kernel(
         kb_cols = []
         for u in range(PAGES):
             cols = sbuf("kb_cols%d" % u, [P, PACK], F32)
-            nc.gpsimd.dma_start(cols[:], kb_rows[LIVE:, u * PAGE : (u + 1) * PAGE])
+            queue = nc.sync if u == 0 else nc.gpsimd
+            queue.dma_start(cols[:], kb_rows[LIVE:, u * PAGE : (u + 1) * PAGE])
             kb_cols.append(cols)
         late_head = shared.tile([P, FILL], F32, name="late_head", offset=4 * POOL_PAGES * DV, align_bytes=64)
         nc.scalar.activation(late_head[:LIVE, :], kept_head[:LIVE, :], ACT.Copy)

@@ -19,7 +19,7 @@ QUADS = P // QUAD
 V_PLANE = 4
 FILL = 8
 ZEROED = 32
-VECTOR_END = 1184
+VECTOR_END = 1408
 EARLY_FILL = 512
 SHORT_FILL = 128
 LINE = 4

@@ -19,10 +19,10 @@ QUADS = P // QUAD
 V_PLANE = 4
 FILL = 8
 ZEROED = 32
-VECTOR_END = 1408
-EARLY_FILL = 512
-SHORT_FILL = 128
+GPSIMD_END = 1920
+EARLY_FILL = 896
 LINE = 4
+WORD = 4
 
 FLOPS = 2 * NQ * SLOTS * (512 + DV)
 
@@ -43,12 +43,15 @@ def tile_attend_pkv8q_silu_kb_kernel(
     nc = tc.nc
     with ExitStack() as ctx:
         sb = ctx.enter_context(tc.tile_pool(name="sb", bufs=1))
-        reused = ctx.enter_context(tc.tile_pool(name="reused", bufs=1))
-        shared = ctx.enter_context(tc.tile_pool(name="shared", bufs=1))
+        after_deal = ctx.enter_context(tc.tile_pool(name="after_deal", bufs=1))
+        windows = ctx.enter_context(tc.tile_pool(name="windows", bufs=1))
         ps = ctx.enter_context(tc.psum_pool(name="ps", bufs=1))
 
-        def sbuf(name, shape, dtype, tag=None):
-            return sb.tile(shape, dtype, name=name, tag=tag or name, align_bytes=64)
+        def sbuf(name, shape, dtype):
+            return sb.tile(shape, dtype, name=name, tag=name, align_bytes=64)
+
+        def placed(pool, name, shape, dtype, offset):
+            return pool.tile(shape, dtype, name=name, offset=offset, align_bytes=64)
 
         def entries(list_tile, first, count):
             return list_tile[:, first // LIST_ROWS : (first + count) // LIST_ROWS]
@@ -61,94 +64,104 @@ def tile_attend_pkv8q_silu_kb_kernel(
                 ACT.Copy,
             )
 
-        vs_pool = shared.tile([P, POOL_TOKENS], F32, name="vs_pool", offset=4 * POOL_TOKENS, align_bytes=64)
+        window_bytes = WORD * POOL_TOKENS
+        page_bytes = WORD * PAGE
+
+        vs_pool = placed(windows, "vs_pool", [P, POOL_TOKENS], F32, window_bytes)
         nc.scalar.dma_start(vs_pool[LIVE:, :], vs[0:1, :])
         slots = sb.tile([P, SLOTS // LIST_ROWS], U16, name="slots")
         nc.sync.dma_start(slots[:], offs)
+        vs_head = sbuf("vs_head", [P, FILL], F32)
+        nc.sync.dma_start(vs_head[:], vs[0].rearrange("(p f) -> p f", p=P)[:, :FILL])
+        kb_pool = placed(windows, "kb_pool", [P, POOL_TOKENS], F32, 0)
+        nc.sync.dma_start(kb_pool[LIVE:, :], kb[0:1, :])
         vcols = sb.tile([P, PAGES * DV // LIST_ROWS], U16, name="vcols")
         nc.sync.dma_start(vcols[:], voffs)
-        vs_head = sbuf("vs_head", [P, FILL], F32, "head_then_kb_rows")
-        nc.sync.dma_start(vs_head[:], vs[0].rearrange("(p f) -> p f", p=P)[:, :FILL])
-        qw = sbuf("qw", [P, NQ], I32)
-        nc.sync.dma_start(qw[:], q_words[0, 0].rearrange("p n r -> p (n r)").bitcast(I32))
-        kb_pool = shared.tile([P, POOL_TOKENS], F32, name="kb_pool", offset=0, align_bytes=64)
-        nc.sync.dma_start(kb_pool[LIVE:, :], kb[0:1, :])
-        kq_plane = sbuf("kq_plane", [P, (SLOTS + NQ) // 4], I32)
+        kq_plane = sbuf("kq_plane", [P, (SLOTS + NQ) // WORD], I32)
         nc.gpsimd.dma_start(
-            kq_plane[:, SLOTS // 4 :],
-            q_scales[0, 0].bitcast(I32).unsqueeze(0).broadcast_to([P // SCALE_ROWS, SCALE_ROWS, NQ // 4]),
+            kq_plane[:, SLOTS // WORD :],
+            q_scales[0, 0].bitcast(I32).unsqueeze(0).broadcast_to([P // SCALE_ROWS, SCALE_ROWS, NQ // WORD]),
         )
 
         nc.vector.memset(vs_pool[:LIVE, :ZEROED], 0.0)
         warm = sbuf("warm", [P, ZEROED], F32)
         nc.scalar.activation(warm[:LIVE, :], vs_pool[:LIVE, :ZEROED], ACT.Silu)
-        ks_pool = sbuf("ks_pool", [P, POOL_TOKENS // 4], I32)
+        ks_pool = sbuf("ks_pool", [P, POOL_TOKENS // WORD], I32)
         nc.vector.memset(ks_pool[:], 0)
         nc.sync.dma_start(ks_pool[:SCALE_ROWS, :], k_scales[0].bitcast(I32))
-        kw_pool = sbuf("kw_pool", [P, POOL_TOKENS], I32)
-        nc.sync.dma_start(kw_pool[:], k_words[0].rearrange("p n r -> p (n r)").bitcast(I32))
-        nc.vector.memset(kb_pool[:LIVE, :], 0.0)
-
-        kept_head = sbuf("kept_head", [P, FILL], F32)
-        nc.scalar.activation(kept_head[:LIVE, :], vs_head[:LIVE, :], ACT.Copy)
-        fill(vs_pool[:LIVE, POOL_TOKENS - EARLY_FILL :], vs_head[:LIVE, :])
-        kb_rows = sbuf("kb_rows", [P, SLOTS], F32, "head_then_kb_rows")
-        nc.scalar.activation(kb_rows[:], kb_pool[:].indirect(slots[:]), ACT.Copy)
-        kb_cols = []
-        for u in range(PAGES):
-            cols = sbuf("kb_cols%d" % u, [P, PACK], F32)
-            queue = nc.sync if u == 0 else nc.gpsimd
-            queue.dma_start(cols[:], kb_rows[LIVE:, u * PAGE : (u + 1) * PAGE])
-            kb_cols.append(cols)
-        late_head = shared.tile([P, FILL], F32, name="late_head", offset=4 * POOL_PAGES * DV, align_bytes=64)
-        nc.scalar.activation(late_head[:LIVE, :], kept_head[:LIVE, :], ACT.Copy)
-        vw_pool = shared.tile([P, POOL_PAGES * DV], I32, name="vw_pool", offset=0, align_bytes=64)
-        nc.scalar.dma_start(
-            vw_pool[:].rearrange("p (u e) -> p u e", u=POOL_PAGES),
-            v_words.rearrange("u p e r -> p u (e r)").bitcast(I32),
-        )
-        fill(vs_pool[:LIVE, VECTOR_END - FILL : VECTOR_END + SHORT_FILL], late_head[:LIVE, :])
-        fill(vs_pool[:LIVE, VECTOR_END + SHORT_FILL : POOL_TOKENS - EARLY_FILL], late_head[:LIVE, :])
-
-        ks = reused.tile([P, SLOTS], U8, name="ks", offset=0, align_bytes=64)
-        nc.vector.tensor_copy(ks[:], ks_pool[:].bitcast(U8).indirect(slots[:]))
-        kq_bytes = kq_plane[:].bitcast(U8)
-        nc.vector.tensor_copy(
-            kq_bytes[:, :SLOTS].rearrange("p (r n) -> p r n", r=PACK),
-            ks[:].rearrange("p (n r) -> p r n", r=PACK),
-        )
-        for quad in range(1, QUADS):
-            nc.sync.dma_start(
-                kq_plane[QUAD * quad : QUAD * quad + PACK, :], kq_plane[PACK * quad : PACK * (quad + 1), :]
-            )
-        nc.vector.memset(vs_pool[:LIVE, ZEROED:VECTOR_END], 0.0)
-        vsc_pool = sbuf("vsc_pool", [P, POOL_PAGES * DV // 4], I32)
+        vsc_pool = sbuf("vsc_pool", [P, POOL_PAGES * DV // WORD], I32)
         nc.vector.memset(vsc_pool[:], 0)
         nc.sync.dma_start(
             vsc_pool[:SCALE_ROWS, :].rearrange("p (u e) -> p u e", u=POOL_PAGES),
             v_scales.rearrange("u f e -> f u e").bitcast(I32),
         )
-        v_plane = sbuf("v_plane", [P, PAGES * DV // 4], I32)
-        nc.vector.memset(v_plane[:], 0)
+        kw_pool = sbuf("kw_pool", [P, POOL_TOKENS], I32)
+        nc.sync.dma_start(kw_pool[:], k_words[0].rearrange("p n r -> p (n r)").bitcast(I32))
+        qw = sbuf("qw", [P, NQ], I32)
+        nc.sync.dma_start(qw[:], q_words[0, 0].rearrange("p n r -> p (n r)").bitcast(I32))
+        nc.vector.memset(kb_pool[:LIVE, :], 0.0)
+        nc.gpsimd.memset(vs_pool[:LIVE, ZEROED - FILL : GPSIMD_END], 0.0)
+
+        fill(vs_pool[:LIVE, POOL_TOKENS - EARLY_FILL :], vs_head[:LIVE, :])
+        kb_rows = []
+        for u in range(PAGES):
+            row = sbuf("kb_row%d" % u, [P, PAGE], F32)
+            nc.scalar.activation(row[:], kb_pool[:].indirect(entries(slots, u * PAGE, PAGE)), ACT.Copy)
+            kb_rows.append(row)
+        kb_cols = []
+        for u in range(PAGES - 1):
+            cols = sbuf("kb_cols%d" % u, [P, PACK], F32)
+            nc.sync.dma_start(cols[:], kb_rows[u][LIVE:, :])
+            kb_cols.append(cols)
+        late_head = placed(windows, "late_head", [P, FILL], F32, WORD * POOL_PAGES * DV)
+        nc.scalar.activation(late_head[:LIVE, :], vs_head[:LIVE, :], ACT.Copy)
+        vw_pool = placed(windows, "vw_pool", [P, POOL_PAGES * DV], I32, 0)
+        nc.scalar.dma_start(
+            vw_pool[:].rearrange("p (u e) -> p u e", u=POOL_PAGES),
+            v_words.rearrange("u p e r -> p u (e r)").bitcast(I32),
+        )
+        fill(vs_pool[:LIVE, GPSIMD_END : POOL_TOKENS - EARLY_FILL], late_head[:LIVE, :])
+
+        keys_at = 1024
+        ks = placed(after_deal, "ks", [P, keys_at + PAGES * page_bytes], U8, 0)
+        nc.vector.tensor_copy(ks[:, :SLOTS], ks_pool[:].bitcast(U8).indirect(slots[:]))
+        kq_bytes = kq_plane[:].bitcast(U8)
+        nc.vector.tensor_copy(
+            kq_bytes[:, :SLOTS].rearrange("p (r n) -> p r n", r=PACK),
+            ks[:, :SLOTS].rearrange("p (n r) -> p r n", r=PACK),
+        )
+        for quad in range(1, QUADS):
+            nc.sync.dma_start(
+                kq_plane[QUAD * quad : QUAD * quad + PACK, :], kq_plane[PACK * quad : PACK * (quad + 1), :]
+            )
+        last_cols = placed(after_deal, "kb_cols_last", [P, PACK], F32, 0)
+        nc.sync.dma_start(last_cols[:], kb_rows[PAGES - 1][LIVE:, :])
+        kb_cols.append(last_cols)
+        vsc = placed(after_deal, "vsc", [P, PAGES * DV], U8, 64)
+        nc.vector.tensor_copy(vsc[:], vsc_pool[:].bitcast(U8).indirect(vcols[:]))
 
         vs_cols = []
         for u in range(PAGES):
             vs_row = sbuf("vs_row%d" % u, [P, PAGE], F32)
             nc.scalar.activation(vs_row[:], vs_pool[:].indirect(entries(slots, u * PAGE, PAGE)), ACT.Copy)
-            cols = reused.tile([P, PACK], F32, name="vs_cols%d" % u, offset=64 * u, align_bytes=64)
+            cols = sbuf("vs_cols%d" % u, [P, PACK], F32)
             nc.sync.dma_start(cols[:], vs_row[LIVE:, :])
             vs_cols.append(cols)
 
+        v_plane = placed(windows, "v_plane", [P, PAGES * DV // WORD], I32, window_bytes)
+        nc.gpsimd.memset(v_plane[:], 0)
+        for quad in range(QUADS):
+            first = QUAD * quad + V_PLANE
+            nc.sync.dma_start(v_plane[first : first + PACK, :], vsc[PACK * quad : PACK * (quad + 1), :].bitcast(I32))
+
         silu = []
         for u in range(PAGES):
-            kw = reused.tile([P, PAGE], U32, name="kw%d" % u, offset=4 * PAGE * (1 + 2 * u), align_bytes=64)
+            kw = placed(after_deal, "kw%d" % u, [P, PAGE], U32, keys_at + page_bytes * ((u - 1) % PAGES))
             nc.vector.tensor_copy(
                 kw[:].rearrange("p (r s) -> p s r", r=PACK),
                 kw_pool[:].bitcast(U32).indirect(entries(slots, u * PAGE, PAGE)),
             )
-            p = shared.tile(
-                [P, PACK, NQ], F32, name="p%d" % u, offset=4 * (POOL_TOKENS + (1 + u) * PAGE), align_bytes=64
-            )
+            p = placed(windows, "p%d" % u, [P, PACK, NQ], F32, window_bytes + (1 + u) * page_bytes)
             for half in range(2):
                 scores = ps.tile([P, 2, NQ], F32, name="scores", tag="scores", bufs=2 * PAGES)
                 for i in range(2):
@@ -168,12 +181,7 @@ def tile_attend_pkv8q_silu_kb_kernel(
                     nc.scalar.activation(p[:, r, :], scores[:, i, :], ACT.Silu, bias=kb_cols[u][:, r : r + 1])
             silu.append(p)
 
-        vsc = reused.tile([P, PAGES * DV], U8, name="vsc", offset=4 * PAGE, align_bytes=64)
-        nc.vector.tensor_copy(vsc[:], vsc_pool[:].bitcast(U8).indirect(vcols[:]))
-        for quad in range(QUADS):
-            first = QUAD * quad + V_PLANE
-            nc.sync.dma_start(v_plane[first : first + PACK, :], vsc[PACK * quad : PACK * (quad + 1), :].bitcast(I32))
-        vw = reused.tile([P, PAGES * DV], U32, name="vw", offset=4 * PAGE + PAGES * DV, align_bytes=64)
+        vw = placed(after_deal, "vw", [P, PAGES * DV], U32, keys_at + page_bytes * (PAGES - 1))
         nc.vector.tensor_copy(vw[:], vw_pool[:].bitcast(U32).indirect(vcols[:]))
 
         acc = [ps.tile([NQ, P], F32, name="acc", tag="acc", bufs=2) for side in range(2)]

@@ -16,10 +16,10 @@ SCALE_ROWS = 16
 LIVE = P - 1
 QUAD = 32
 QUADS = P // QUAD
-V_PLANE = 4
 FILL = 8
 ZEROED = 32
-GPSIMD_END = 1920
+VECTOR_END = 1024
+SHORT_FILL = 128
 EARLY_FILL = 896
 LINE = 4
 WORD = 4
@@ -43,7 +43,6 @@ def tile_attend_pkv8q_silu_kb_kernel(
     nc = tc.nc
     with ExitStack() as ctx:
         sb = ctx.enter_context(tc.tile_pool(name="sb", bufs=1))
-        after_deal = ctx.enter_context(tc.tile_pool(name="after_deal", bufs=1))
         windows = ctx.enter_context(tc.tile_pool(name="windows", bufs=1))
         ps = ctx.enter_context(tc.psum_pool(name="ps", bufs=1))
 
@@ -100,7 +99,6 @@ def tile_attend_pkv8q_silu_kb_kernel(
         qw = sbuf("qw", [P, NQ], I32)
         nc.sync.dma_start(qw[:], q_words[0, 0].rearrange("p n r -> p (n r)").bitcast(I32))
         nc.vector.memset(kb_pool[:LIVE, :], 0.0)
-        nc.gpsimd.memset(vs_pool[:LIVE, ZEROED - FILL : GPSIMD_END], 0.0)
 
         fill(vs_pool[:LIVE, POOL_TOKENS - EARLY_FILL :], vs_head[:LIVE, :])
         kb_rows = []
@@ -120,10 +118,15 @@ def tile_attend_pkv8q_silu_kb_kernel(
             vw_pool[:].rearrange("p (u e) -> p u e", u=POOL_PAGES),
             v_words.rearrange("u p e r -> p u (e r)").bitcast(I32),
         )
-        fill(vs_pool[:LIVE, GPSIMD_END : POOL_TOKENS - EARLY_FILL], late_head[:LIVE, :])
+        fill(vs_pool[:LIVE, VECTOR_END - FILL : VECTOR_END + SHORT_FILL], late_head[:LIVE, :])
+        fill(vs_pool[:LIVE, VECTOR_END + SHORT_FILL : POOL_TOKENS - EARLY_FILL], late_head[:LIVE, :])
 
-        keys_at = 1024
-        ks = placed(after_deal, "ks", [P, keys_at + PAGES * page_bytes], U8, 0)
+        tail = 2 * window_bytes
+        vw_at = tail + PAGE
+        keys_at = [tail, vw_at + WORD * PAGES * DV, vw_at + WORD * PAGES * DV + page_bytes]
+        vsc_at = keys_at[-1] + page_bytes
+        cols_at = vsc_at + PAGES * DV
+        ks = placed(windows, "ks", [P, cols_at + 64 - tail], U8, tail)
         nc.vector.tensor_copy(ks[:, :SLOTS], ks_pool[:].bitcast(U8).indirect(slots[:]))
         kq_bytes = kq_plane[:].bitcast(U8)
         nc.vector.tensor_copy(
@@ -134,10 +137,11 @@ def tile_attend_pkv8q_silu_kb_kernel(
             nc.sync.dma_start(
                 kq_plane[QUAD * quad : QUAD * quad + PACK, :], kq_plane[PACK * quad : PACK * (quad + 1), :]
             )
-        last_cols = placed(after_deal, "kb_cols_last", [P, PACK], F32, 0)
+        last_cols = placed(windows, "kb_cols_last", [P, PACK], F32, cols_at)
         nc.sync.dma_start(last_cols[:], kb_rows[PAGES - 1][LIVE:, :])
         kb_cols.append(last_cols)
-        vsc = placed(after_deal, "vsc", [P, PAGES * DV], U8, 64)
+        nc.vector.memset(vs_pool[:LIVE, ZEROED:VECTOR_END], 0.0)
+        vsc = placed(windows, "vsc", [P, PAGES * DV], U8, vsc_at)
         nc.vector.tensor_copy(vsc[:], vsc_pool[:].bitcast(U8).indirect(vcols[:]))
 
         vs_cols = []
@@ -148,15 +152,9 @@ def tile_attend_pkv8q_silu_kb_kernel(
             nc.sync.dma_start(cols[:], vs_row[LIVE:, :])
             vs_cols.append(cols)
 
-        v_plane = placed(windows, "v_plane", [P, PAGES * DV // WORD], I32, window_bytes)
-        nc.gpsimd.memset(v_plane[:], 0)
-        for quad in range(QUADS):
-            first = QUAD * quad + V_PLANE
-            nc.sync.dma_start(v_plane[first : first + PACK, :], vsc[PACK * quad : PACK * (quad + 1), :].bitcast(I32))
-
         silu = []
         for u in range(PAGES):
-            kw = placed(after_deal, "kw%d" % u, [P, PAGE], U32, keys_at + page_bytes * ((u - 1) % PAGES))
+            kw = placed(windows, "kw%d" % u, [P, PAGE], U32, keys_at[u])
             nc.vector.tensor_copy(
                 kw[:].rearrange("p (r s) -> p s r", r=PACK),
                 kw_pool[:].bitcast(U32).indirect(entries(slots, u * PAGE, PAGE)),
@@ -181,7 +179,14 @@ def tile_attend_pkv8q_silu_kb_kernel(
                     nc.scalar.activation(p[:, r, :], scores[:, i, :], ACT.Silu, bias=kb_cols[u][:, r : r + 1])
             silu.append(p)
 
-        vw = placed(after_deal, "vw", [P, PAGES * DV], U32, keys_at + page_bytes * (PAGES - 1))
+        v_plane = placed(windows, "v_plane", [P, PAGES * DV // WORD], I32, tail - PAGES * DV // 2)
+        nc.vector.tensor_copy(v_plane[:], vsc[:].bitcast(I32))
+        for quad in range(1, QUADS):
+            nc.sync.dma_start(
+                v_plane[QUAD * quad : QUAD * quad + PACK, :], v_plane[PACK * quad : PACK * (quad + 1), :]
+            )
+
+        vw = placed(windows, "vw", [P, PAGES * DV], U32, vw_at)
         nc.vector.tensor_copy(vw[:], vw_pool[:].bitcast(U32).indirect(vcols[:]))
 
         acc = [ps.tile([NQ, P], F32, name="acc", tag="acc", bufs=2) for side in range(2)]
@@ -210,7 +215,7 @@ def tile_attend_pkv8q_silu_kb_kernel(
                     lhsT=w_codes[:].bitcast(FP8X4),
                     lhsT_scale=w_scales[:],
                     rhs=vw[:, cols].bitcast(FP8X4),
-                    rhs_scale=v_bytes[V_PLANE:, cols],
+                    rhs_scale=v_bytes[:, cols],
                     start=(u == 0),
                     stop=(u == PAGES - 1),
                 )

@@ -1,6 +1,7 @@
 from contextlib import ExitStack
 
 import concourse.mybir as mybir
+from concourse.masks import make_identity
 
 P = 128
 PACK = 4
@@ -88,6 +89,9 @@ def tile_attend_pkv8q_silu_kb_kernel(
         ks_pool = sbuf("ks_pool", [P, POOL_TOKENS // WORD], I32)
         nc.vector.memset(ks_pool[:], 0)
         nc.sync.dma_start(ks_pool[:SCALE_ROWS, :], k_scales[0].bitcast(I32))
+        ident = sbuf("ident", [P, P], F32)
+        nc.vector.memset(ident[:], 0.0)
+        make_identity(nc, ident[:], nomemset=True)
         vsc_pool = sbuf("vsc_pool", [P, POOL_PAGES * DV // WORD], I32)
         nc.vector.memset(vsc_pool[:], 0)
         nc.sync.dma_start(
@@ -101,16 +105,13 @@ def tile_attend_pkv8q_silu_kb_kernel(
         nc.vector.memset(kb_pool[:LIVE, :], 0.0)
 
         fill(vs_pool[:LIVE, POOL_TOKENS - EARLY_FILL :], vs_head[:LIVE, :])
-        kb_rows = []
+        turned = ps.tile([P, PAGE], F32, name="turned", tag="turned", bufs=1)
         for u in range(PAGES):
             row = sbuf("kb_row%d" % u, [P, PAGE], F32)
             nc.scalar.activation(row[:], kb_pool[:].indirect(entries(slots, u * PAGE, PAGE)), ACT.Copy)
-            kb_rows.append(row)
-        kb_cols = []
-        for u in range(PAGES - 1):
-            cols = sbuf("kb_cols%d" % u, [P, PACK], F32)
-            nc.sync.dma_start(cols[:], kb_rows[u][LIVE:, :])
-            kb_cols.append(cols)
+            for r in range(PACK):
+                first = 2 * (PAGES * PACK - 1 - (u * PACK + r))
+                nc.tensor.transpose(turned[:, first : first + P], row[:, r::PACK], ident[:])
         late_head = placed(windows, "late_head", [P, FILL], F32, WORD * POOL_PAGES * DV)
         nc.scalar.activation(late_head[:LIVE, :], vs_head[:LIVE, :], ACT.Copy)
         vw_pool = placed(windows, "vw_pool", [P, POOL_PAGES * DV], I32, 0)
@@ -125,8 +126,7 @@ def tile_attend_pkv8q_silu_kb_kernel(
         vw_at = tail + PAGE
         keys_at = [tail, vw_at + WORD * PAGES * DV, vw_at + WORD * PAGES * DV + page_bytes]
         vsc_at = keys_at[-1] + page_bytes
-        cols_at = vsc_at + PAGES * DV
-        ks = placed(windows, "ks", [P, cols_at + 64 - tail], U8, tail)
+        ks = placed(windows, "ks", [P, vsc_at + PAGES * DV - tail], U8, tail)
         nc.vector.tensor_copy(ks[:, :SLOTS], ks_pool[:].bitcast(U8).indirect(slots[:]))
         kq_bytes = kq_plane[:].bitcast(U8)
         nc.vector.tensor_copy(
@@ -137,9 +137,6 @@ def tile_attend_pkv8q_silu_kb_kernel(
             nc.sync.dma_start(
                 kq_plane[QUAD * quad : QUAD * quad + PACK, :], kq_plane[PACK * quad : PACK * (quad + 1), :]
             )
-        last_cols = placed(windows, "kb_cols_last", [P, PACK], F32, cols_at)
-        nc.sync.dma_start(last_cols[:], kb_rows[PAGES - 1][LIVE:, :])
-        kb_cols.append(last_cols)
         nc.vector.memset(vs_pool[:LIVE, ZEROED:VECTOR_END], 0.0)
         vsc = placed(windows, "vsc", [P, PAGES * DV], U8, vsc_at)
         nc.vector.tensor_copy(vsc[:], vsc_pool[:].bitcast(U8).indirect(vcols[:]))
@@ -152,6 +149,9 @@ def tile_attend_pkv8q_silu_kb_kernel(
             nc.sync.dma_start(cols[:], vs_row[LIVE:, :])
             vs_cols.append(cols)
 
+        kb_cols = placed(windows, "kb_cols", [P, PAGES * PACK], F32, window_bytes)
+        nc.scalar.activation(kb_cols[:], turned[:, LIVE : LIVE + 2 * PAGES * PACK : 2], ACT.Copy)
+
         silu = []
         for u in range(PAGES):
             kw = placed(windows, "kw%d" % u, [P, PAGE], U32, keys_at[u])
@@ -160,23 +160,21 @@ def tile_attend_pkv8q_silu_kb_kernel(
                 kw_pool[:].bitcast(U32).indirect(entries(slots, u * PAGE, PAGE)),
             )
             p = placed(windows, "p%d" % u, [P, PACK, NQ], F32, window_bytes + (1 + u) * page_bytes)
-            for half in range(2):
-                scores = ps.tile([P, 2, NQ], F32, name="scores", tag="scores", bufs=2 * PAGES)
-                for i in range(2):
-                    r = 2 * half + i
-                    first = (r * PAGES + u) * P
-                    nc.tensor.matmul_mx(
-                        scores[:, i, :],
-                        lhsT=kw[:, r * P : (r + 1) * P].bitcast(FP8X4),
-                        lhsT_scale=kq_bytes[:, first : first + P],
-                        rhs=qw[:].bitcast(FP8X4),
-                        rhs_scale=kq_bytes[:, SLOTS:],
-                        start=True,
-                        stop=True,
-                    )
-                for i in range(2):
-                    r = 2 * half + i
-                    nc.scalar.activation(p[:, r, :], scores[:, i, :], ACT.Silu, bias=kb_cols[u][:, r : r + 1])
+            scores = ps.tile([P, PACK, NQ], F32, name="scores", tag="scores", bufs=PAGES)
+            for r in range(PACK):
+                first = (r * PAGES + u) * P
+                nc.tensor.matmul_mx(
+                    scores[:, r, :],
+                    lhsT=kw[:, r * P : (r + 1) * P].bitcast(FP8X4),
+                    lhsT_scale=kq_bytes[:, first : first + P],
+                    rhs=qw[:].bitcast(FP8X4),
+                    rhs_scale=kq_bytes[:, SLOTS:],
+                    start=True,
+                    stop=True,
+                )
+            for r in range(PACK):
+                col = PAGES * PACK - 1 - (u * PACK + r)
+                nc.scalar.activation(p[:, r, :], scores[:, r, :], ACT.Silu, bias=kb_cols[:, col : col + 1])
             silu.append(p)
 
         v_plane = placed(windows, "v_plane", [P, PAGES * DV // WORD], I32, tail - PAGES * DV // 2)

@@ -20,8 +20,7 @@ QUADS = P // QUAD
 FILL = 8
 ZEROED = 32
 VECTOR_END = 1024
-SHORT_FILL = 128
-EARLY_FILL = 896
+EARLY_FILL = 1216
 LINE = 4
 WORD = 4
 
@@ -103,6 +102,7 @@ def tile_attend_pkv8q_silu_kb_kernel(
         qw = sbuf("qw", [P, NQ], I32)
         nc.sync.dma_start(qw[:], q_words[0, 0].rearrange("p n r -> p (n r)").bitcast(I32))
         nc.vector.memset(kb_pool[:LIVE, :], 0.0)
+        nc.vector.memset(vs_pool[:LIVE, ZEROED:VECTOR_END], 0.0)
 
         fill(vs_pool[:LIVE, POOL_TOKENS - EARLY_FILL :], vs_head[:LIVE, :])
         turned = ps.tile([P, PAGE], F32, name="turned", tag="turned", bufs=1)
@@ -119,26 +119,35 @@ def tile_attend_pkv8q_silu_kb_kernel(
             vw_pool[:].rearrange("p (u e) -> p u e", u=POOL_PAGES),
             v_words.rearrange("u p e r -> p u (e r)").bitcast(I32),
         )
-        fill(vs_pool[:LIVE, VECTOR_END - FILL : VECTOR_END + SHORT_FILL], late_head[:LIVE, :])
-        fill(vs_pool[:LIVE, VECTOR_END + SHORT_FILL : POOL_TOKENS - EARLY_FILL], late_head[:LIVE, :])
+        fill(vs_pool[:LIVE, VECTOR_END : POOL_TOKENS - EARLY_FILL], late_head[:LIVE, :])
 
         tail = 2 * window_bytes
         vw_at = tail + PAGE
         keys_at = [tail, vw_at + WORD * PAGES * DV, vw_at + WORD * PAGES * DV + page_bytes]
-        vsc_at = keys_at[-1] + page_bytes
-        ks = placed(windows, "ks", [P, vsc_at + PAGES * DV - tail], U8, tail)
-        nc.vector.tensor_copy(ks[:, :SLOTS], ks_pool[:].bitcast(U8).indirect(slots[:]))
+        ks = placed(windows, "ks", [P, keys_at[-1] + page_bytes - tail], U8, tail)
         kq_bytes = kq_plane[:].bitcast(U8)
-        nc.vector.tensor_copy(
-            kq_bytes[:, :SLOTS].rearrange("p (r n) -> p r n", r=PACK),
-            ks[:, :SLOTS].rearrange("p (n r) -> p r n", r=PACK),
-        )
+
+        def gather_scales(u):
+            nc.vector.tensor_copy(
+                ks[:, u * PAGE : (u + 1) * PAGE], ks_pool[:].bitcast(U8).indirect(entries(slots, u * PAGE, PAGE))
+            )
+
+        def deal_scales(u):
+            nc.vector.tensor_copy(
+                kq_bytes[:, u * PAGE : (u + 1) * PAGE].rearrange("p (r n) -> p r n", r=PACK),
+                ks[:, u * PAGE : (u + 1) * PAGE].rearrange("p (n r) -> p r n", r=PACK),
+            )
+
+        gather_scales(0)
+        for u in range(PAGES):
+            if u + 1 < PAGES:
+                gather_scales(u + 1)
+            deal_scales(u)
         for quad in range(1, QUADS):
             nc.sync.dma_start(
                 kq_plane[QUAD * quad : QUAD * quad + PACK, :], kq_plane[PACK * quad : PACK * (quad + 1), :]
             )
-        nc.vector.memset(vs_pool[:LIVE, ZEROED:VECTOR_END], 0.0)
-        vsc = placed(windows, "vsc", [P, PAGES * DV], U8, vsc_at)
+        vsc = sbuf("vsc", [P, PAGES * DV], U8)
         nc.vector.tensor_copy(vsc[:], vsc_pool[:].bitcast(U8).indirect(vcols[:]))
 
         vs_cols = []
@@ -162,7 +171,7 @@ def tile_attend_pkv8q_silu_kb_kernel(
             p = placed(windows, "p%d" % u, [P, PACK, NQ], F32, window_bytes + (1 + u) * page_bytes)
             scores = ps.tile([P, PACK, NQ], F32, name="scores", tag="scores", bufs=PAGES)
             for r in range(PACK):
-                first = (r * PAGES + u) * P
+                first = u * PAGE + r * P
                 nc.tensor.matmul_mx(
                     scores[:, r, :],
                     lhsT=kw[:, r * P : (r + 1) * P].bitcast(FP8X4),

@@ -20,6 +20,7 @@ QUADS = P // QUAD
 FILL = 8
 ZEROED = 32
 VECTOR_END = 1024
+SHORT_FILL = 512
 EARLY_FILL = 1216
 LINE = 4
 WORD = 4
@@ -66,11 +67,16 @@ def tile_attend_pkv8q_silu_kb_kernel(
         window_bytes = WORD * POOL_TOKENS
         page_bytes = WORD * PAGE
 
+        tail = 2 * window_bytes
+        vw_at = tail + PAGE
+        keys_at = [tail, vw_at + WORD * PAGES * DV, vw_at + WORD * PAGES * DV + page_bytes]
+
         vs_pool = placed(windows, "vs_pool", [P, POOL_TOKENS], F32, window_bytes)
         nc.scalar.dma_start(vs_pool[LIVE:, :], vs[0:1, :])
         slots = sb.tile([P, SLOTS // LIST_ROWS], U16, name="slots")
         nc.sync.dma_start(slots[:], offs)
-        vs_head = sbuf("vs_head", [P, FILL], F32)
+        values_at = 3 * window_bytes
+        vs_head = placed(windows, "vs_head", [P, FILL], F32, values_at)
         nc.sync.dma_start(vs_head[:], vs[0].rearrange("(p f) -> p f", p=P)[:, :FILL])
         kb_pool = placed(windows, "kb_pool", [P, POOL_TOKENS], F32, 0)
         nc.sync.dma_start(kb_pool[LIVE:, :], kb[0:1, :])
@@ -106,36 +112,41 @@ def tile_attend_pkv8q_silu_kb_kernel(
 
         fill(vs_pool[:LIVE, POOL_TOKENS - EARLY_FILL :], vs_head[:LIVE, :])
         turned = ps.tile([P, PAGE], F32, name="turned", tag="turned", bufs=1)
-        for u in range(PAGES):
+
+        def turn(u, r, cols):
+            first = 2 * (PAGES * PACK - 1 - (u * PACK + r))
+            nc.tensor.transpose(turned[:, first : first + P], cols, ident[:])
+
+        for u in range(PAGES - 1):
             row = sbuf("kb_row%d" % u, [P, PAGE], F32)
             nc.scalar.activation(row[:], kb_pool[:].indirect(entries(slots, u * PAGE, PAGE)), ACT.Copy)
             for r in range(PACK):
-                first = 2 * (PAGES * PACK - 1 - (u * PACK + r))
-                nc.tensor.transpose(turned[:, first : first + P], row[:, r::PACK], ident[:])
-        late_head = placed(windows, "late_head", [P, FILL], F32, WORD * POOL_PAGES * DV)
+                turn(u, r, row[:, r::PACK])
+        last_row = placed(windows, "kb_row_last", [P, PAGE], F32, tail)
+        nc.scalar.activation(last_row[:], kb_pool[:].indirect(entries(slots, SLOTS - PAGE, PAGE)), ACT.Copy)
+        late_head = placed(windows, "late_head", [P, FILL], F32, 0)
         nc.scalar.activation(late_head[:LIVE, :], vs_head[:LIVE, :], ACT.Copy)
-        vw_pool = placed(windows, "vw_pool", [P, POOL_PAGES * DV], I32, 0)
+        fill(vs_pool[:LIVE, VECTOR_END : VECTOR_END + SHORT_FILL], late_head[:LIVE, :])
+        vw_pool = placed(windows, "vw_pool", [P, POOL_PAGES * DV], I32, values_at)
         nc.scalar.dma_start(
             vw_pool[:].rearrange("p (u e) -> p u e", u=POOL_PAGES),
             v_words.rearrange("u p e r -> p u (e r)").bitcast(I32),
         )
-        fill(vs_pool[:LIVE, VECTOR_END : POOL_TOKENS - EARLY_FILL], late_head[:LIVE, :])
+        fill(vs_pool[:LIVE, VECTOR_END + SHORT_FILL : POOL_TOKENS - EARLY_FILL], late_head[:LIVE, :])
 
-        tail = 2 * window_bytes
-        vw_at = tail + PAGE
-        keys_at = [tail, vw_at + WORD * PAGES * DV, vw_at + WORD * PAGES * DV + page_bytes]
-        ks = placed(windows, "ks", [P, keys_at[-1] + page_bytes - tail], U8, tail)
+        dealt_at = keys_at[-1] + page_bytes
+        ks_first = placed(windows, "ks_first", [P, PAGE], U8, dealt_at)
+        ks_rest = placed(windows, "ks_rest", [P, keys_at[-1] - tail], U8, tail + page_bytes)
+        ks = [ks_first[:]] + [ks_rest[:, u * PAGE : (u + 1) * PAGE] for u in range(PAGES - 1)]
         kq_bytes = kq_plane[:].bitcast(U8)
 
         def gather_scales(u):
-            nc.vector.tensor_copy(
-                ks[:, u * PAGE : (u + 1) * PAGE], ks_pool[:].bitcast(U8).indirect(entries(slots, u * PAGE, PAGE))
-            )
+            nc.vector.tensor_copy(ks[u], ks_pool[:].bitcast(U8).indirect(entries(slots, u * PAGE, PAGE)))
 
         def deal_scales(u):
             nc.vector.tensor_copy(
                 kq_bytes[:, u * PAGE : (u + 1) * PAGE].rearrange("p (r n) -> p r n", r=PACK),
-                ks[:, u * PAGE : (u + 1) * PAGE].rearrange("p (n r) -> p r n", r=PACK),
+                ks[u].rearrange("p (n r) -> p r n", r=PACK),
             )
 
         gather_scales(0)
@@ -147,6 +158,12 @@ def tile_attend_pkv8q_silu_kb_kernel(
             nc.sync.dma_start(
                 kq_plane[QUAD * quad : QUAD * quad + PACK, :], kq_plane[PACK * quad : PACK * (quad + 1), :]
             )
+        last_dealt = placed(windows, "kb_row_dealt", [P, PACK, P], F32, dealt_at)
+        nc.vector.tensor_copy(
+            last_dealt[:].rearrange("p r n -> p n r"), last_row[:].rearrange("p (n r) -> p n r", r=PACK)
+        )
+        for r in range(PACK):
+            turn(PAGES - 1, r, last_dealt[:, r, :])
         vsc = sbuf("vsc", [P, PAGES * DV], U8)
         nc.vector.tensor_copy(vsc[:], vsc_pool[:].bitcast(U8).indirect(vcols[:]))
 
@@ -163,9 +180,9 @@ def tile_attend_pkv8q_silu_kb_kernel(
 
         silu = []
         for u in range(PAGES):
-            kw = placed(windows, "kw%d" % u, [P, PAGE], U32, keys_at[u])
+            kw = placed(windows, "kw%d" % u, [P, PAGE + (P if u == 0 else 0)], U32, keys_at[u])
             nc.vector.tensor_copy(
-                kw[:].rearrange("p (r s) -> p s r", r=PACK),
+                kw[:, :PAGE].rearrange("p (r s) -> p s r", r=PACK),
                 kw_pool[:].bitcast(U32).indirect(entries(slots, u * PAGE, PAGE)),
             )
             p = placed(windows, "p%d" % u, [P, PACK, NQ], F32, window_bytes + (1 + u) * page_bytes)

@@ -19,8 +19,8 @@ QUAD = 32
 QUADS = P // QUAD
 FILL = 8
 ZEROED = 32
-VECTOR_END = 1024
-SHORT_FILL = 512
+GPSIMD_END = 1664
+SHORT_FILL = 256
 EARLY_FILL = 1216
 LINE = 4
 WORD = 4
@@ -68,8 +68,11 @@ def tile_attend_pkv8q_silu_kb_kernel(
         page_bytes = WORD * PAGE
 
         tail = 2 * window_bytes
-        vw_at = tail + PAGE
+        half_plane = PAGES * DV // 2
+        vw_at = tail + half_plane + page_bytes
         keys_at = [tail, vw_at + WORD * PAGES * DV, vw_at + WORD * PAGES * DV + page_bytes]
+        vsc_at = keys_at[-1] + page_bytes
+        dealt_at = vsc_at + PAGES * DV
 
         vs_pool = placed(windows, "vs_pool", [P, POOL_TOKENS], F32, window_bytes)
         nc.scalar.dma_start(vs_pool[LIVE:, :], vs[0:1, :])
@@ -108,7 +111,7 @@ def tile_attend_pkv8q_silu_kb_kernel(
         qw = sbuf("qw", [P, NQ], I32)
         nc.sync.dma_start(qw[:], q_words[0, 0].rearrange("p n r -> p (n r)").bitcast(I32))
         nc.vector.memset(kb_pool[:LIVE, :], 0.0)
-        nc.vector.memset(vs_pool[:LIVE, ZEROED:VECTOR_END], 0.0)
+        nc.gpsimd.memset(vs_pool[:LIVE, ZEROED - FILL : GPSIMD_END], 0.0)
 
         fill(vs_pool[:LIVE, POOL_TOKENS - EARLY_FILL :], vs_head[:LIVE, :])
         turned = ps.tile([P, PAGE], F32, name="turned", tag="turned", bufs=1)
@@ -126,34 +129,25 @@ def tile_attend_pkv8q_silu_kb_kernel(
         nc.scalar.activation(last_row[:], kb_pool[:].indirect(entries(slots, SLOTS - PAGE, PAGE)), ACT.Copy)
         late_head = placed(windows, "late_head", [P, FILL], F32, 0)
         nc.scalar.activation(late_head[:LIVE, :], vs_head[:LIVE, :], ACT.Copy)
-        fill(vs_pool[:LIVE, VECTOR_END : VECTOR_END + SHORT_FILL], late_head[:LIVE, :])
+        fill(vs_pool[:LIVE, GPSIMD_END : GPSIMD_END + SHORT_FILL], late_head[:LIVE, :])
         vw_pool = placed(windows, "vw_pool", [P, POOL_PAGES * DV], I32, values_at)
         nc.scalar.dma_start(
             vw_pool[:].rearrange("p (u e) -> p u e", u=POOL_PAGES),
             v_words.rearrange("u p e r -> p u (e r)").bitcast(I32),
         )
-        fill(vs_pool[:LIVE, VECTOR_END + SHORT_FILL : POOL_TOKENS - EARLY_FILL], late_head[:LIVE, :])
+        fill(vs_pool[:LIVE, GPSIMD_END + SHORT_FILL : POOL_TOKENS - EARLY_FILL], late_head[:LIVE, :])
 
-        dealt_at = keys_at[-1] + page_bytes
         ks_first = placed(windows, "ks_first", [P, PAGE], U8, dealt_at)
-        ks_rest = placed(windows, "ks_rest", [P, keys_at[-1] - tail], U8, tail + page_bytes)
-        ks = [ks_first[:]] + [ks_rest[:, u * PAGE : (u + 1) * PAGE] for u in range(PAGES - 1)]
+        ks_rest = placed(windows, "ks_rest", [P, dealt_at - tail - page_bytes], U8, tail + page_bytes)
+        pieces = [(ks_first[:], 0, 1), (ks_rest[:, : SLOTS - PAGE], PAGE, PAGES - 1)]
         kq_bytes = kq_plane[:].bitcast(U8)
-
-        def gather_scales(u):
-            nc.vector.tensor_copy(ks[u], ks_pool[:].bitcast(U8).indirect(entries(slots, u * PAGE, PAGE)))
-
-        def deal_scales(u):
+        for ks, first, pages in pieces:
+            nc.vector.tensor_copy(ks, ks_pool[:].bitcast(U8).indirect(entries(slots, first, pages * PAGE)))
+        for ks, first, pages in pieces:
             nc.vector.tensor_copy(
-                kq_bytes[:, u * PAGE : (u + 1) * PAGE].rearrange("p (r n) -> p r n", r=PACK),
-                ks[u].rearrange("p (n r) -> p r n", r=PACK),
+                kq_bytes[:, first : first + pages * PAGE].rearrange("p (u r n) -> p u r n", u=pages, r=PACK),
+                ks.rearrange("p (u n r) -> p u r n", u=pages, r=PACK),
             )
-
-        gather_scales(0)
-        for u in range(PAGES):
-            if u + 1 < PAGES:
-                gather_scales(u + 1)
-            deal_scales(u)
         for quad in range(1, QUADS):
             nc.sync.dma_start(
                 kq_plane[QUAD * quad : QUAD * quad + PACK, :], kq_plane[PACK * quad : PACK * (quad + 1), :]
@@ -164,16 +158,17 @@ def tile_attend_pkv8q_silu_kb_kernel(
         )
         for r in range(PACK):
             turn(PAGES - 1, r, last_dealt[:, r, :])
-        vsc = sbuf("vsc", [P, PAGES * DV], U8)
+        vsc = placed(windows, "vsc", [P, PAGES * DV], U8, vsc_at)
         nc.vector.tensor_copy(vsc[:], vsc_pool[:].bitcast(U8).indirect(vcols[:]))
 
         vs_cols = []
         for u in range(PAGES):
             vs_row = sbuf("vs_row%d" % u, [P, PAGE], F32)
             nc.scalar.activation(vs_row[:], vs_pool[:].indirect(entries(slots, u * PAGE, PAGE)), ACT.Copy)
-            cols = sbuf("vs_cols%d" % u, [P, PACK], F32)
-            nc.sync.dma_start(cols[:], vs_row[LIVE:, :])
-            vs_cols.append(cols)
+            if u < PAGES - 1:
+                cols = sbuf("vs_cols%d" % u, [P, PACK], F32)
+                nc.sync.dma_start(cols[:], vs_row[LIVE:, :])
+                vs_cols.append(cols[:])
 
         kb_cols = placed(windows, "kb_cols", [P, PAGES * PACK], F32, window_bytes)
         nc.scalar.activation(kb_cols[:], turned[:, LIVE : LIVE + 2 * PAGES * PACK : 2], ACT.Copy)
@@ -203,7 +198,16 @@ def tile_attend_pkv8q_silu_kb_kernel(
                 nc.scalar.activation(p[:, r, :], scores[:, r, :], ACT.Silu, bias=kb_cols[:, col : col + 1])
             silu.append(p)
 
-        v_plane = placed(windows, "v_plane", [P, PAGES * DV // WORD], I32, tail - PAGES * DV // 2)
+        vs_dealt = placed(windows, "vs_row_dealt", [P, PACK, P], F32, tail + half_plane)
+        nc.vector.tensor_copy(
+            vs_dealt[:].rearrange("p r n -> p n r"), vs_row[:].rearrange("p (n r) -> p n r", r=PACK)
+        )
+        vs_turned = ps.tile([P, PACK, P], F32, name="turned", tag="turned", bufs=1)
+        for r in range(PACK):
+            nc.tensor.transpose(vs_turned[:, r, :], vs_dealt[:, r, :], ident[:])
+        vs_cols.append(vs_turned[:, :, LIVE])
+
+        v_plane = placed(windows, "v_plane", [P, PAGES * DV // WORD], I32, tail - half_plane)
         nc.vector.tensor_copy(v_plane[:], vsc[:].bitcast(I32))
         for quad in range(1, QUADS):
             nc.sync.dma_start(
@@ -221,7 +225,7 @@ def tile_attend_pkv8q_silu_kb_kernel(
             nc.vector.tensor_tensor(
                 w[:].rearrange("p (c i) r -> p c r i", i=LINE),
                 silu[u][:].rearrange("p r (c i) -> p c r i", i=LINE),
-                vs_cols[u][:].unsqueeze(1).unsqueeze(3).broadcast_to([P, NQ // LINE, PACK, LINE]),
+                vs_cols[u].unsqueeze(1).unsqueeze(3).broadcast_to([P, NQ // LINE, PACK, LINE]),
                 ALU.mult,
             )
             return w

@@ -22,7 +22,8 @@ ZEROED = 32
 GPSIMD_END = 1664
 SHORT_FILL = 256
 EARLY_FILL = 1216
-LINE = 4
+LINE = 2
+VECTOR_QUERIES = 48
 WORD = 4
 
 FLOPS = 2 * NQ * SLOTS * (512 + DV)
@@ -97,15 +98,15 @@ def tile_attend_pkv8q_silu_kb_kernel(
         ks_pool = sbuf("ks_pool", [P, POOL_TOKENS // WORD], I32)
         nc.vector.memset(ks_pool[:], 0)
         nc.sync.dma_start(ks_pool[:SCALE_ROWS, :], k_scales[0].bitcast(I32))
-        ident = sbuf("ident", [P, P], F32)
-        nc.vector.memset(ident[:], 0.0)
-        make_identity(nc, ident[:], nomemset=True)
         vsc_pool = sbuf("vsc_pool", [P, POOL_PAGES * DV // WORD], I32)
         nc.vector.memset(vsc_pool[:], 0)
         nc.sync.dma_start(
             vsc_pool[:SCALE_ROWS, :].rearrange("p (u e) -> p u e", u=POOL_PAGES),
             v_scales.rearrange("u f e -> f u e").bitcast(I32),
         )
+        ident = sbuf("ident", [P, P], F32)
+        nc.vector.memset(ident[:], 0.0)
+        make_identity(nc, ident[:], nomemset=True)
         kw_pool = sbuf("kw_pool", [P, POOL_TOKENS], I32)
         nc.sync.dma_start(kw_pool[:], k_words[0].rearrange("p n r -> p (n r)").bitcast(I32))
         qw = sbuf("qw", [P, NQ], I32)
@@ -165,10 +166,9 @@ def tile_attend_pkv8q_silu_kb_kernel(
         for u in range(PAGES):
             vs_row = sbuf("vs_row%d" % u, [P, PAGE], F32)
             nc.scalar.activation(vs_row[:], vs_pool[:].indirect(entries(slots, u * PAGE, PAGE)), ACT.Copy)
-            if u < PAGES - 1:
-                cols = sbuf("vs_cols%d" % u, [P, PACK], F32)
-                nc.sync.dma_start(cols[:], vs_row[LIVE:, :])
-                vs_cols.append(cols[:])
+            cols = sbuf("vs_cols%d" % u, [P, PACK], F32)
+            nc.sync.dma_start(cols[:], vs_row[LIVE:, :])
+            vs_cols.append(cols)
 
         kb_cols = placed(windows, "kb_cols", [P, PAGES * PACK], F32, window_bytes)
         nc.scalar.activation(kb_cols[:], turned[:, LIVE : LIVE + 2 * PAGES * PACK : 2], ACT.Copy)
@@ -181,31 +181,26 @@ def tile_attend_pkv8q_silu_kb_kernel(
                 kw_pool[:].bitcast(U32).indirect(entries(slots, u * PAGE, PAGE)),
             )
             p = placed(windows, "p%d" % u, [P, PACK, NQ], F32, window_bytes + (1 + u) * page_bytes)
-            scores = ps.tile([P, PACK, NQ], F32, name="scores", tag="scores", bufs=PAGES)
-            for r in range(PACK):
-                first = u * PAGE + r * P
-                nc.tensor.matmul_mx(
-                    scores[:, r, :],
-                    lhsT=kw[:, r * P : (r + 1) * P].bitcast(FP8X4),
-                    lhsT_scale=kq_bytes[:, first : first + P],
-                    rhs=qw[:].bitcast(FP8X4),
-                    rhs_scale=kq_bytes[:, SLOTS:],
-                    start=True,
-                    stop=True,
-                )
-            for r in range(PACK):
-                col = PAGES * PACK - 1 - (u * PACK + r)
-                nc.scalar.activation(p[:, r, :], scores[:, r, :], ACT.Silu, bias=kb_cols[:, col : col + 1])
+            step = PACK // 2 if u == 0 else PACK
+            for r0 in range(0, PACK, step):
+                scores = ps.tile([P, step, NQ], F32, name="scores", tag="scores", bufs=PAGES + 1)
+                for i in range(step):
+                    r = r0 + i
+                    first = u * PAGE + r * P
+                    nc.tensor.matmul_mx(
+                        scores[:, i, :],
+                        lhsT=kw[:, r * P : (r + 1) * P].bitcast(FP8X4),
+                        lhsT_scale=kq_bytes[:, first : first + P],
+                        rhs=qw[:].bitcast(FP8X4),
+                        rhs_scale=kq_bytes[:, SLOTS:],
+                        start=True,
+                        stop=True,
+                    )
+                for i in range(step):
+                    r = r0 + i
+                    col = PAGES * PACK - 1 - (u * PACK + r)
+                    nc.scalar.activation(p[:, r, :], scores[:, i, :], ACT.Silu, bias=kb_cols[:, col : col + 1])
             silu.append(p)
-
-        vs_dealt = placed(windows, "vs_row_dealt", [P, PACK, P], F32, tail + half_plane)
-        nc.vector.tensor_copy(
-            vs_dealt[:].rearrange("p r n -> p n r"), vs_row[:].rearrange("p (n r) -> p n r", r=PACK)
-        )
-        vs_turned = ps.tile([P, PACK, P], F32, name="turned", tag="turned", bufs=1)
-        for r in range(PACK):
-            nc.tensor.transpose(vs_turned[:, r, :], vs_dealt[:, r, :], ident[:])
-        vs_cols.append(vs_turned[:, :, LIVE])
 
         v_plane = placed(windows, "v_plane", [P, PAGES * DV // WORD], I32, tail - half_plane)
         nc.vector.tensor_copy(v_plane[:], vsc[:].bitcast(I32))
@@ -222,12 +217,18 @@ def tile_attend_pkv8q_silu_kb_kernel(
 
         def weigh(u):
             w = sbuf("w%d" % u, [P, NQ, PACK], BF16)
+            own = NQ if u + 1 < PAGES else VECTOR_QUERIES
             nc.vector.tensor_tensor(
-                w[:].rearrange("p (c i) r -> p c r i", i=LINE),
-                silu[u][:].rearrange("p r (c i) -> p c r i", i=LINE),
-                vs_cols[u].unsqueeze(1).unsqueeze(3).broadcast_to([P, NQ // LINE, PACK, LINE]),
+                w[:, :own, :].rearrange("p (c i) r -> p c r i", i=LINE),
+                silu[u][:, :, :own].rearrange("p r (c i) -> p c r i", i=LINE),
+                vs_cols[u][:].unsqueeze(1).unsqueeze(3).broadcast_to([P, own // LINE, PACK, LINE]),
                 ALU.mult,
             )
+            if own < NQ:
+                for r in range(PACK):
+                    nc.scalar.activation(
+                        w[:, own:, r], silu[u][:, r, own:], ACT.Copy, scale=vs_cols[u][:, r : r + 1]
+                    )
             return w
 
         def multiply(u, w):

@@ -19,11 +19,11 @@ QUAD = 32
 QUADS = P // QUAD
 FILL = 8
 ZEROED = 32
-GPSIMD_END = 1664
+GPSIMD_END = 2048
 SHORT_FILL = 256
 EARLY_FILL = 1216
 LINE = 2
-VECTOR_QUERIES = 48
+VECTOR_QUERIES = 72
 WORD = 4
 
 FLOPS = 2 * NQ * SLOTS * (512 + DV)
@@ -69,11 +69,10 @@ def tile_attend_pkv8q_silu_kb_kernel(
         page_bytes = WORD * PAGE
 
         tail = 2 * window_bytes
-        half_plane = PAGES * DV // 2
-        vw_at = tail + half_plane + page_bytes
+        vw_at = tail + page_bytes
         keys_at = [tail, vw_at + WORD * PAGES * DV, vw_at + WORD * PAGES * DV + page_bytes]
-        vsc_at = keys_at[-1] + page_bytes
-        dealt_at = vsc_at + PAGES * DV
+        dealt_at = keys_at[-1] + page_bytes
+        vsc_at = dealt_at + page_bytes
 
         vs_pool = placed(windows, "vs_pool", [P, POOL_TOKENS], F32, window_bytes)
         nc.scalar.dma_start(vs_pool[LIVE:, :], vs[0:1, :])
@@ -86,9 +85,9 @@ def tile_attend_pkv8q_silu_kb_kernel(
         nc.sync.dma_start(kb_pool[LIVE:, :], kb[0:1, :])
         vcols = sb.tile([P, PAGES * DV // LIST_ROWS], U16, name="vcols")
         nc.sync.dma_start(vcols[:], voffs)
-        kq_plane = sbuf("kq_plane", [P, (SLOTS + NQ) // WORD], I32)
+        planes = sbuf("planes", [P, (SLOTS + NQ + PAGES * DV) // WORD], I32)
         nc.gpsimd.dma_start(
-            kq_plane[:, SLOTS // WORD :],
+            planes[:, SLOTS // WORD : (SLOTS + NQ) // WORD],
             q_scales[0, 0].bitcast(I32).unsqueeze(0).broadcast_to([P // SCALE_ROWS, SCALE_ROWS, NQ // WORD]),
         )
 
@@ -138,20 +137,19 @@ def tile_attend_pkv8q_silu_kb_kernel(
         )
         fill(vs_pool[:LIVE, GPSIMD_END + SHORT_FILL : POOL_TOKENS - EARLY_FILL], late_head[:LIVE, :])
 
-        ks_first = placed(windows, "ks_first", [P, PAGE], U8, dealt_at)
-        ks_rest = placed(windows, "ks_rest", [P, dealt_at - tail - page_bytes], U8, tail + page_bytes)
-        pieces = [(ks_first[:], 0, 1), (ks_rest[:, : SLOTS - PAGE], PAGE, PAGES - 1)]
-        kq_bytes = kq_plane[:].bitcast(U8)
-        for ks, first, pages in pieces:
-            nc.vector.tensor_copy(ks, ks_pool[:].bitcast(U8).indirect(entries(slots, first, pages * PAGE)))
-        for ks, first, pages in pieces:
-            nc.vector.tensor_copy(
-                kq_bytes[:, first : first + pages * PAGE].rearrange("p (u r n) -> p u r n", u=pages, r=PACK),
-                ks.rearrange("p (u n r) -> p u r n", u=pages, r=PACK),
-            )
+        ks = placed(windows, "ks", [P, dealt_at + 64 - tail - page_bytes], U8, tail + page_bytes)
+        nc.vector.tensor_copy(ks[:, :SLOTS], ks_pool[:].bitcast(U8).indirect(slots[:]))
+        vsc = placed(windows, "vsc", [P, PAGES * DV], U8, vsc_at)
+        nc.vector.tensor_copy(vsc[:], vsc_pool[:].bitcast(U8).indirect(vcols[:]))
+        plane_bytes = planes[:].bitcast(U8)
+        nc.vector.tensor_copy(
+            plane_bytes[:, :SLOTS].rearrange("p (r n) -> p r n", r=PACK),
+            ks[:, :SLOTS].rearrange("p (n r) -> p r n", r=PACK),
+        )
+        nc.vector.tensor_copy(planes[:, (SLOTS + NQ) // WORD :], vsc[:].bitcast(I32))
         for quad in range(1, QUADS):
             nc.sync.dma_start(
-                kq_plane[QUAD * quad : QUAD * quad + PACK, :], kq_plane[PACK * quad : PACK * (quad + 1), :]
+                planes[QUAD * quad : QUAD * quad + PACK, :], planes[PACK * quad : PACK * (quad + 1), :]
             )
         last_dealt = placed(windows, "kb_row_dealt", [P, PACK, P], F32, dealt_at)
         nc.vector.tensor_copy(
@@ -159,14 +157,12 @@ def tile_attend_pkv8q_silu_kb_kernel(
         )
         for r in range(PACK):
             turn(PAGES - 1, r, last_dealt[:, r, :])
-        vsc = placed(windows, "vsc", [P, PAGES * DV], U8, vsc_at)
-        nc.vector.tensor_copy(vsc[:], vsc_pool[:].bitcast(U8).indirect(vcols[:]))
 
         vs_cols = []
         for u in range(PAGES):
             vs_row = sbuf("vs_row%d" % u, [P, PAGE], F32)
             nc.scalar.activation(vs_row[:], vs_pool[:].indirect(entries(slots, u * PAGE, PAGE)), ACT.Copy)
-            cols = sbuf("vs_cols%d" % u, [P, PACK], F32)
+            cols = placed(windows, "vs_cols%d" % u, [P, PACK], F32, vsc_at + 64 * u)
             nc.sync.dma_start(cols[:], vs_row[LIVE:, :])
             vs_cols.append(cols)
 
@@ -186,13 +182,13 @@ def tile_attend_pkv8q_silu_kb_kernel(
                 scores = ps.tile([P, step, NQ], F32, name="scores", tag="scores", bufs=PAGES + 1)
                 for i in range(step):
                     r = r0 + i
-                    first = u * PAGE + r * P
+                    first = (r * PAGES + u) * P
                     nc.tensor.matmul_mx(
                         scores[:, i, :],
                         lhsT=kw[:, r * P : (r + 1) * P].bitcast(FP8X4),
-                        lhsT_scale=kq_bytes[:, first : first + P],
+                        lhsT_scale=plane_bytes[:, first : first + P],
                         rhs=qw[:].bitcast(FP8X4),
-                        rhs_scale=kq_bytes[:, SLOTS:],
+                        rhs_scale=plane_bytes[:, SLOTS : SLOTS + NQ],
                         start=True,
                         stop=True,
                     )
@@ -202,18 +198,11 @@ def tile_attend_pkv8q_silu_kb_kernel(
                     nc.scalar.activation(p[:, r, :], scores[:, i, :], ACT.Silu, bias=kb_cols[:, col : col + 1])
             silu.append(p)
 
-        v_plane = placed(windows, "v_plane", [P, PAGES * DV // WORD], I32, tail - half_plane)
-        nc.vector.tensor_copy(v_plane[:], vsc[:].bitcast(I32))
-        for quad in range(1, QUADS):
-            nc.sync.dma_start(
-                v_plane[QUAD * quad : QUAD * quad + PACK, :], v_plane[PACK * quad : PACK * (quad + 1), :]
-            )
-
         vw = placed(windows, "vw", [P, PAGES * DV], U32, vw_at)
         nc.vector.tensor_copy(vw[:], vw_pool[:].bitcast(U32).indirect(vcols[:]))
 
         acc = [ps.tile([NQ, P], F32, name="acc", tag="acc", bufs=2) for side in range(2)]
-        v_bytes = v_plane[:].bitcast(U8)
+        v_bytes = plane_bytes[:, SLOTS + NQ :]
 
         def weigh(u):
             w = sbuf("w%d" % u, [P, NQ, PACK], BF16)

@@ -16,14 +16,16 @@ LIST_ROWS = 16
 SCALE_ROWS = 16
 LIVE = P - 1
 QUAD = 32
-QUADS = P // QUAD
+ROW_STEP = P // SCALE_ROWS
 FILL = 8
 ZEROED = 32
-GPSIMD_END = 2048
-SHORT_FILL = 256
-EARLY_FILL = 1216
+GPSIMD_END = 2112
+SHORT_FILL = 640
+EARLY_FILL = 320
+KB_FILL = 704
+FIRST_KEYS = 1280
 LINE = 2
-VECTOR_QUERIES = 72
+VECTOR_QUERIES = 88
 WORD = 4
 
 FLOPS = 2 * NQ * SLOTS * (512 + DV)
@@ -74,21 +76,23 @@ def tile_attend_pkv8q_silu_kb_kernel(
         dealt_at = keys_at[-1] + page_bytes
         vsc_at = dealt_at + page_bytes
 
+        kb_head = sbuf("kb_head", [P, FILL], F32)
+        nc.sync.dma_start(kb_head[:], kb[0].rearrange("(p f) -> p f", p=P)[:, :FILL])
         vs_pool = placed(windows, "vs_pool", [P, POOL_TOKENS], F32, window_bytes)
         nc.scalar.dma_start(vs_pool[LIVE:, :], vs[0:1, :])
-        slots = sb.tile([P, SLOTS // LIST_ROWS], U16, name="slots")
-        nc.sync.dma_start(slots[:], offs)
+        kb_pool = placed(windows, "kb_pool", [P, POOL_TOKENS], F32, 0)
+        nc.sync.dma_start(kb_pool[LIVE:, :], kb[0:1, :])
         values_at = 3 * window_bytes
         vs_head = placed(windows, "vs_head", [P, FILL], F32, values_at)
         nc.sync.dma_start(vs_head[:], vs[0].rearrange("(p f) -> p f", p=P)[:, :FILL])
-        kb_pool = placed(windows, "kb_pool", [P, POOL_TOKENS], F32, 0)
-        nc.sync.dma_start(kb_pool[LIVE:, :], kb[0:1, :])
+        slots = sb.tile([P, SLOTS // LIST_ROWS], U16, name="slots")
+        nc.sync.dma_start(slots[:], offs)
         vcols = sb.tile([P, PAGES * DV // LIST_ROWS], U16, name="vcols")
         nc.sync.dma_start(vcols[:], voffs)
         planes = sbuf("planes", [P, (SLOTS + NQ + PAGES * DV) // WORD], I32)
         nc.gpsimd.dma_start(
             planes[:, SLOTS // WORD : (SLOTS + NQ) // WORD],
-            q_scales[0, 0].bitcast(I32).unsqueeze(0).broadcast_to([P // SCALE_ROWS, SCALE_ROWS, NQ // WORD]),
+            q_scales[0, 0].bitcast(I32).unsqueeze(1).broadcast_to([SCALE_ROWS, ROW_STEP, NQ // WORD]),
         )
 
         nc.vector.memset(vs_pool[:LIVE, :ZEROED], 0.0)
@@ -96,23 +100,26 @@ def tile_attend_pkv8q_silu_kb_kernel(
         nc.scalar.activation(warm[:LIVE, :], vs_pool[:LIVE, :ZEROED], ACT.Silu)
         ks_pool = sbuf("ks_pool", [P, POOL_TOKENS // WORD], I32)
         nc.vector.memset(ks_pool[:], 0)
-        nc.sync.dma_start(ks_pool[:SCALE_ROWS, :], k_scales[0].bitcast(I32))
+        nc.sync.dma_start(ks_pool[0:P:ROW_STEP, :], k_scales[0].bitcast(I32))
+        kw_pool = sbuf("kw_pool", [P, POOL_TOKENS], I32)
+        key_words = k_words[0].rearrange("p n r -> p (n r)").bitcast(I32)
+        nc.sync.dma_start(kw_pool[:, :FIRST_KEYS], key_words[:, :FIRST_KEYS])
         vsc_pool = sbuf("vsc_pool", [P, POOL_PAGES * DV // WORD], I32)
         nc.vector.memset(vsc_pool[:], 0)
         nc.sync.dma_start(
-            vsc_pool[:SCALE_ROWS, :].rearrange("p (u e) -> p u e", u=POOL_PAGES),
+            vsc_pool[0:P:ROW_STEP, :].rearrange("p (u e) -> p u e", u=POOL_PAGES),
             v_scales.rearrange("u f e -> f u e").bitcast(I32),
         )
         ident = sbuf("ident", [P, P], F32)
         nc.vector.memset(ident[:], 0.0)
         make_identity(nc, ident[:], nomemset=True)
-        kw_pool = sbuf("kw_pool", [P, POOL_TOKENS], I32)
-        nc.sync.dma_start(kw_pool[:], k_words[0].rearrange("p n r -> p (n r)").bitcast(I32))
+        nc.sync.dma_start(kw_pool[:, FIRST_KEYS:], key_words[:, FIRST_KEYS:])
         qw = sbuf("qw", [P, NQ], I32)
         nc.sync.dma_start(qw[:], q_words[0, 0].rearrange("p n r -> p (n r)").bitcast(I32))
-        nc.vector.memset(kb_pool[:LIVE, :], 0.0)
+        nc.vector.memset(kb_pool[:LIVE, : POOL_TOKENS - KB_FILL], 0.0)
         nc.gpsimd.memset(vs_pool[:LIVE, ZEROED - FILL : GPSIMD_END], 0.0)
 
+        fill(kb_pool[:LIVE, POOL_TOKENS - KB_FILL :], kb_head[:LIVE, :])
         fill(vs_pool[:LIVE, POOL_TOKENS - EARLY_FILL :], vs_head[:LIVE, :])
         turned = ps.tile([P, PAGE], F32, name="turned", tag="turned", bufs=1)
 
@@ -147,10 +154,8 @@ def tile_attend_pkv8q_silu_kb_kernel(
             ks[:, :SLOTS].rearrange("p (n r) -> p r n", r=PACK),
         )
         nc.vector.tensor_copy(planes[:, (SLOTS + NQ) // WORD :], vsc[:].bitcast(I32))
-        for quad in range(1, QUADS):
-            nc.sync.dma_start(
-                planes[QUAD * quad : QUAD * quad + PACK, :], planes[PACK * quad : PACK * (quad + 1), :]
-            )
+        for row in range(1, PACK):
+            nc.sync.dma_start(planes[row:P:QUAD, :], planes[ROW_STEP * row : P : QUAD, :])
         last_dealt = placed(windows, "kb_row_dealt", [P, PACK, P], F32, dealt_at)
         nc.vector.tensor_copy(
             last_dealt[:].rearrange("p r n -> p n r"), last_row[:].rearrange("p (n r) -> p n r", r=PACK)

from contextlib import ExitStack

import concourse.mybir as mybir
from concourse.masks import make_identity

P = 128
PACK = 4
PAGE = P * PACK
PAGES = 3
SLOTS = PAGES * PAGE
POOL_TOKENS = 4096
POOL_PAGES = POOL_TOKENS // PAGE
DV = 256
NQ = 128
LIST_ROWS = 16
SCALE_ROWS = 16
LIVE = P - 1
QUAD = 32
ROW_STEP = P // SCALE_ROWS
FILL = 8
ZEROED = 32
GPSIMD_END = 2112
SHORT_FILL = 640
EARLY_FILL = 320
KB_FILL = 704
FIRST_KEYS = 1280
LINE = 2
VECTOR_QUERIES = 88
WORD = 4

FLOPS = 2 * NQ * SLOTS * (512 + DV)

F32 = mybir.dt.float32
BF16 = mybir.dt.bfloat16
I32 = mybir.dt.int32
U32 = mybir.dt.uint32
U16 = mybir.dt.uint16
U8 = mybir.dt.uint8
FP8X4 = mybir.dt.float8_e4m3fn_x4
ACT = mybir.ActivationFunctionType
ALU = mybir.AluOpType


def tile_attend_pkv8q_silu_kb_kernel(
    tc, q_words, q_scales, k_words, k_scales, v_words, v_scales, vs, kb, offs, voffs, out
):
    nc = tc.nc
    with ExitStack() as ctx:
        sb = ctx.enter_context(tc.tile_pool(name="sb", bufs=1))
        windows = ctx.enter_context(tc.tile_pool(name="windows", bufs=1))
        ps = ctx.enter_context(tc.psum_pool(name="ps", bufs=1))

        def sbuf(name, shape, dtype):
            return sb.tile(shape, dtype, name=name, tag=name, align_bytes=64)

        def placed(pool, name, shape, dtype, offset):
            return pool.tile(shape, dtype, name=name, offset=offset, align_bytes=64)

        def entries(list_tile, first, count):
            return list_tile[:, first // LIST_ROWS : (first + count) // LIST_ROWS]

        def fill(dst, src):
            cols = dst.shape[1]
            nc.scalar.activation(
                dst.rearrange("p (a b) -> p a b", b=FILL),
                src.unsqueeze(1).broadcast_to([LIVE, cols // FILL, FILL]),
                ACT.Copy,
            )

        window_bytes = WORD * POOL_TOKENS
        page_bytes = WORD * PAGE

        tail = 2 * window_bytes
        vw_at = tail + page_bytes
        keys_at = [tail, vw_at + WORD * PAGES * DV, vw_at + WORD * PAGES * DV + page_bytes]
        dealt_at = keys_at[-1] + page_bytes
        vsc_at = dealt_at + page_bytes

        kb_head = sbuf("kb_head", [P, FILL], F32)
        nc.sync.dma_start(kb_head[:], kb[0].rearrange("(p f) -> p f", p=P)[:, :FILL])
        vs_pool = placed(windows, "vs_pool", [P, POOL_TOKENS], F32, window_bytes)
        nc.scalar.dma_start(vs_pool[LIVE:, :], vs[0:1, :])
        kb_pool = placed(windows, "kb_pool", [P, POOL_TOKENS], F32, 0)
        nc.sync.dma_start(kb_pool[LIVE:, :], kb[0:1, :])
        values_at = 3 * window_bytes
        vs_head = placed(windows, "vs_head", [P, FILL], F32, values_at)
        nc.sync.dma_start(vs_head[:], vs[0].rearrange("(p f) -> p f", p=P)[:, :FILL])
        slots = sb.tile([P, SLOTS // LIST_ROWS], U16, name="slots")
        nc.sync.dma_start(slots[:], offs)
        vcols = sb.tile([P, PAGES * DV // LIST_ROWS], U16, name="vcols")
        nc.sync.dma_start(vcols[:], voffs)
        planes = sbuf("planes", [P, (SLOTS + NQ + PAGES * DV) // WORD], I32)
        nc.gpsimd.dma_start(
            planes[:, SLOTS // WORD : (SLOTS + NQ) // WORD],
            q_scales[0, 0].bitcast(I32).unsqueeze(1).broadcast_to([SCALE_ROWS, ROW_STEP, NQ // WORD]),
        )

        nc.vector.memset(vs_pool[:LIVE, :ZEROED], 0.0)
        warm = sbuf("warm", [P, ZEROED], F32)
        nc.scalar.activation(warm[:LIVE, :], vs_pool[:LIVE, :ZEROED], ACT.Silu)
        ks_pool = sbuf("ks_pool", [P, POOL_TOKENS // WORD], I32)
        nc.vector.memset(ks_pool[:], 0)
        nc.sync.dma_start(ks_pool[0:P:ROW_STEP, :], k_scales[0].bitcast(I32))
        kw_pool = sbuf("kw_pool", [P, POOL_TOKENS], I32)
        key_words = k_words[0].rearrange("p n r -> p (n r)").bitcast(I32)
        nc.sync.dma_start(kw_pool[:, :FIRST_KEYS], key_words[:, :FIRST_KEYS])
        vsc_pool = sbuf("vsc_pool", [P, POOL_PAGES * DV // WORD], I32)
        nc.vector.memset(vsc_pool[:], 0)
        nc.sync.dma_start(
            vsc_pool[0:P:ROW_STEP, :].rearrange("p (u e) -> p u e", u=POOL_PAGES),
            v_scales.rearrange("u f e -> f u e").bitcast(I32),
        )
        ident = sbuf("ident", [P, P], F32)
        nc.vector.memset(ident[:], 0.0)
        make_identity(nc, ident[:], nomemset=True)
        nc.sync.dma_start(kw_pool[:, FIRST_KEYS:], key_words[:, FIRST_KEYS:])
        qw = sbuf("qw", [P, NQ], I32)
        nc.sync.dma_start(qw[:], q_words[0, 0].rearrange("p n r -> p (n r)").bitcast(I32))
        nc.vector.memset(kb_pool[:LIVE, : POOL_TOKENS - KB_FILL], 0.0)
        nc.gpsimd.memset(vs_pool[:LIVE, ZEROED - FILL : GPSIMD_END], 0.0)

        fill(kb_pool[:LIVE, POOL_TOKENS - KB_FILL :], kb_head[:LIVE, :])
        fill(vs_pool[:LIVE, POOL_TOKENS - EARLY_FILL :], vs_head[:LIVE, :])
        turned = ps.tile([P, PAGE], F32, name="turned", tag="turned", bufs=1)

        def turn(u, r, cols):
            first = 2 * (PAGES * PACK - 1 - (u * PACK + r))
            nc.tensor.transpose(turned[:, first : first + P], cols, ident[:])

        for u in range(PAGES - 1):
            row = sbuf("kb_row%d" % u, [P, PAGE], F32)
            nc.scalar.activation(row[:], kb_pool[:].indirect(entries(slots, u * PAGE, PAGE)), ACT.Copy)
            for r in range(PACK):
                turn(u, r, row[:, r::PACK])
        last_row = placed(windows, "kb_row_last", [P, PAGE], F32, tail)
        nc.scalar.activation(last_row[:], kb_pool[:].indirect(entries(slots, SLOTS - PAGE, PAGE)), ACT.Copy)
        late_head = placed(windows, "late_head", [P, FILL], F32, 0)
        nc.scalar.activation(late_head[:LIVE, :], vs_head[:LIVE, :], ACT.Copy)
        fill(vs_pool[:LIVE, GPSIMD_END : GPSIMD_END + SHORT_FILL], late_head[:LIVE, :])
        vw_pool = placed(windows, "vw_pool", [P, POOL_PAGES * DV], I32, values_at)
        nc.scalar.dma_start(
            vw_pool[:].rearrange("p (u e) -> p u e", u=POOL_PAGES),
            v_words.rearrange("u p e r -> p u (e r)").bitcast(I32),
        )
        fill(vs_pool[:LIVE, GPSIMD_END + SHORT_FILL : POOL_TOKENS - EARLY_FILL], late_head[:LIVE, :])

        ks = placed(windows, "ks", [P, dealt_at + 64 - tail - page_bytes], U8, tail + page_bytes)
        nc.vector.tensor_copy(ks[:, :SLOTS], ks_pool[:].bitcast(U8).indirect(slots[:]))
        vsc = placed(windows, "vsc", [P, PAGES * DV], U8, vsc_at)
        nc.vector.tensor_copy(vsc[:], vsc_pool[:].bitcast(U8).indirect(vcols[:]))
        plane_bytes = planes[:].bitcast(U8)
        nc.vector.tensor_copy(
            plane_bytes[:, :SLOTS].rearrange("p (r n) -> p r n", r=PACK),
            ks[:, :SLOTS].rearrange("p (n r) -> p r n", r=PACK),
        )
        nc.vector.tensor_copy(planes[:, (SLOTS + NQ) // WORD :], vsc[:].bitcast(I32))
        for row in range(1, PACK):
            nc.sync.dma_start(planes[row:P:QUAD, :], planes[ROW_STEP * row : P : QUAD, :])
        last_dealt = placed(windows, "kb_row_dealt", [P, PACK, P], F32, dealt_at)
        nc.vector.tensor_copy(
            last_dealt[:].rearrange("p r n -> p n r"), last_row[:].rearrange("p (n r) -> p n r", r=PACK)
        )
        for r in range(PACK):
            turn(PAGES - 1, r, last_dealt[:, r, :])

        vs_cols = []
        for u in range(PAGES):
            vs_row = sbuf("vs_row%d" % u, [P, PAGE], F32)
            nc.scalar.activation(vs_row[:], vs_pool[:].indirect(entries(slots, u * PAGE, PAGE)), ACT.Copy)
            cols = placed(windows, "vs_cols%d" % u, [P, PACK], F32, vsc_at + 64 * u)
            nc.sync.dma_start(cols[:], vs_row[LIVE:, :])
            vs_cols.append(cols)

        kb_cols = placed(windows, "kb_cols", [P, PAGES * PACK], F32, window_bytes)
        nc.scalar.activation(kb_cols[:], turned[:, LIVE : LIVE + 2 * PAGES * PACK : 2], ACT.Copy)

        silu = []
        for u in range(PAGES):
            kw = placed(windows, "kw%d" % u, [P, PAGE + (P if u == 0 else 0)], U32, keys_at[u])
            nc.vector.tensor_copy(
                kw[:, :PAGE].rearrange("p (r s) -> p s r", r=PACK),
                kw_pool[:].bitcast(U32).indirect(entries(slots, u * PAGE, PAGE)),
            )
            p = placed(windows, "p%d" % u, [P, PACK, NQ], F32, window_bytes + (1 + u) * page_bytes)
            step = PACK // 2 if u == 0 else PACK
            for r0 in range(0, PACK, step):
                scores = ps.tile([P, step, NQ], F32, name="scores", tag="scores", bufs=PAGES + 1)
                for i in range(step):
                    r = r0 + i
                    first = (r * PAGES + u) * P
                    nc.tensor.matmul_mx(
                        scores[:, i, :],
                        lhsT=kw[:, r * P : (r + 1) * P].bitcast(FP8X4),
                        lhsT_scale=plane_bytes[:, first : first + P],
                        rhs=qw[:].bitcast(FP8X4),
                        rhs_scale=plane_bytes[:, SLOTS : SLOTS + NQ],
                        start=True,
                        stop=True,
                    )
                for i in range(step):
                    r = r0 + i
                    col = PAGES * PACK - 1 - (u * PACK + r)
                    nc.scalar.activation(p[:, r, :], scores[:, i, :], ACT.Silu, bias=kb_cols[:, col : col + 1])
            silu.append(p)

        vw = placed(windows, "vw", [P, PAGES * DV], U32, vw_at)
        nc.vector.tensor_copy(vw[:], vw_pool[:].bitcast(U32).indirect(vcols[:]))

        acc = [ps.tile([NQ, P], F32, name="acc", tag="acc", bufs=2) for side in range(2)]
        v_bytes = plane_bytes[:, SLOTS + NQ :]

        def weigh(u):
            w = sbuf("w%d" % u, [P, NQ, PACK], BF16)
            own = NQ if u + 1 < PAGES else VECTOR_QUERIES
            nc.vector.tensor_tensor(
                w[:, :own, :].rearrange("p (c i) r -> p c r i", i=LINE),
                silu[u][:, :, :own].rearrange("p r (c i) -> p c r i", i=LINE),
                vs_cols[u][:].unsqueeze(1).unsqueeze(3).broadcast_to([P, own // LINE, PACK, LINE]),
                ALU.mult,
            )
            if own < NQ:
                for r in range(PACK):
                    nc.scalar.activation(
                        w[:, own:, r], silu[u][:, r, own:], ACT.Copy, scale=vs_cols[u][:, r : r + 1]
                    )
            return w

        def multiply(u, w):
            w_codes = sbuf("w_codes%d" % u, [P, NQ], U32)
            w_scales = sbuf("w_scales%d" % u, [P, NQ], U8)
            nc.vector.quantize_mx(
                out=w_codes[:].bitcast(FP8X4), scales=w_scales[:], in_=w[:].rearrange("p q r -> p (q r)")
            )
            for side in range(2):
                cols = slice(u * DV + side * P, u * DV + (side + 1) * P)
                nc.tensor.matmul_mx(
                    acc[side][:],
                    lhsT=w_codes[:].bitcast(FP8X4),
                    lhsT_scale=w_scales[:],
                    rhs=vw[:, cols].bitcast(FP8X4),
                    rhs_scale=v_bytes[:, cols],
                    start=(u == 0),
                    stop=(u == PAGES - 1),
                )

        weights = [weigh(0)]
        for u in range(PAGES):
            if u + 1 < PAGES:
                weights.append(weigh(u + 1))
            multiply(u, weights[u])

        left = sbuf("left", [NQ, P], F32)
        nc.vector.tensor_scalar_mul(left[:], acc[0][:], 1.0 / 16.0)
        nc.sync.dma_start(out[0, :, :P], left[:])
        right = sbuf("right", [NQ, P], F32)
        nc.scalar.activation(right[:], acc[1][:], ACT.Copy, scale=1.0 / 16.0)
        nc.scalar.dma_start(out[0, :, P:], right[:])
